import numpy as np
import ml_dtypes


def mxq(x, axis, fmt="e4m3"):
    dtype, down = {"e4m3": (ml_dtypes.float8_e4m3fn, 7), "e5m2": (ml_dtypes.float8_e5m2, 14)}[fmt]
    v = np.moveaxis(np.asarray(x, np.float32).astype(ml_dtypes.bfloat16).astype(np.float64), axis, -1)
    blocks = v.reshape(v.shape[:-1] + (-1, 32))
    amax = np.abs(blocks).max(-1, keepdims=True)
    byte = np.maximum(np.where(amax > 0, np.frexp(amax)[1] - 1 + 127, 0) - down, 1)
    scale = np.exp2(byte - 127.0)
    codes = (blocks / scale).astype(np.float32).astype(dtype).astype(np.float64)
    return np.moveaxis((codes * scale).reshape(v.shape), -1, axis)


WIDE = False


def mx_kscale(k):
    if not WIDE:
        return np.ones(k)
    levels = np.array([10, -10, 5, -5, 0])
    if k % 512:
        return np.exp2(np.random.permutation(np.resize(levels, k // 32))).repeat(32)
    a = np.empty((k // 512, 16))
    for p in range(k // 512):
        a[p, :8] = np.random.permutation(np.resize(levels, 8))
        for g in range(8):
            far = levels[np.abs(levels - a[p, g]) >= 10]
            a[p, g + 8] = far[np.random.randint(len(far))]
    return np.exp2(a.ravel()).repeat(32)


def f64(x):
    return np.asarray(x).astype(np.float64)


def striped(idx):
    return np.tile(idx.reshape(-1, 16).T, (8, 1)).astype(np.uint16)


def unstriped(offs):
    return offs[:16].T.reshape(-1).astype(np.int64)


E2M1 = np.array([0.0, 0.5, 1.0, 1.5, 2.0, 3.0, 4.0, 6.0, -0.0, -0.5, -1.0, -1.5, -2.0, -3.0, -4.0, -6.0])


def pack_weight(w, fmt):
    k, n = w.shape
    w = f64(np.asarray(w, np.float32).astype(ml_dtypes.bfloat16)).reshape(k // 32, 32, n)
    amax = np.abs(w).max(1)
    if fmt == "e4m3":
        byte = np.frexp(amax)[1] - 1 + 127 - 7
    else:
        mant, ex = np.frexp(amax / 6.0)
        byte = np.where(mant > 0.5, ex, ex - 1) + 127
    byte = np.clip(np.where(amax > 0, byte, 1), 1, 254)
    scaled = (w * np.exp2(127.0 - byte)[:, None, :]).reshape(k, n).astype(np.float32)
    by_word = np.ascontiguousarray(scaled.reshape(k // 512, 128, 4, n).transpose(0, 1, 3, 2))
    if fmt == "e4m3":
        words = by_word.astype(ml_dtypes.float8_e4m3fn).view(np.uint8)
    else:
        c = by_word.astype(ml_dtypes.float4_e2m1fn).view(np.uint8) & 0xF
        words = (c[..., 0::2] | (c[..., 1::2] << 4)).reshape(k // 512, 128, 2 * n)
    return np.ascontiguousarray(words), np.ascontiguousarray(byte.astype(np.uint8).reshape(k // 512, 16, n))


def unpack_weight(words, scales, fmt):
    g, _, n = scales.shape
    words = np.ascontiguousarray(words).reshape(g, 128, n, -1)
    if fmt == "e4m3":
        vals = words.view(ml_dtypes.float8_e4m3fn).astype(np.float64)
    else:
        nib = np.empty((g, 128, n, 4), np.uint8)
        nib[..., 0::2] = words & 0xF
        nib[..., 1::2] = words >> 4
        vals = E2M1[nib]
    vals = vals * np.repeat(np.exp2(scales.astype(np.float64) - 127.0), 8, axis=1)[..., None]
    return vals.transpose(0, 1, 3, 2).reshape(g * 512, n)


def gelu(v):
    return 0.5 * v * (1.0 + np.tanh(np.sqrt(2.0 / np.pi) * (v + 0.044715 * v**3)))


K, T, S, H, T2, P, N = 1024, 2048, 1024, 1024, 2048, 1024, 512

def setup_inputs():
    n = np.random.standard_normal
    s = mx_kscale(K)[:, None]
    u = mx_kscale(H)[:, None]
    tab_words, tab_scales = pack_weight(n((K, T)) * s, "e4m3")
    w4_words, w4_scales = pack_weight(n((K, H)) / np.sqrt(K) / s, "e2m1")
    return {
        "tab_words": tab_words, "tab_scales": tab_scales,
        "offs": striped(np.random.permutation(T)[:S]),
        "w4_words": w4_words, "w4_scales": w4_scales,
        "wgs": np.exp(0.3 * n((128, S))).astype(np.float32),
        "page0": n((H, T2)).astype(np.float32),
        "offs2": striped(np.random.permutation(T2)[:S]),
        "offs3": striped(np.random.permutation(T2)[:P]),
        "pref": n(H).astype(np.float32),
        "gain": (np.exp(0.3 * n(H)) * u[:, 0]).astype(np.float32),
        "wd": (1.5 * n((H, N)) / np.sqrt(H) / u).astype(np.float32),
    }

def reference(tab_words, tab_scales, offs, w4_words, w4_scales, wgs, page0,
              offs2, offs3, pref, gain, wd):
    v = unpack_weight(tab_words, tab_scales, "e4m3")[:, unstriped(offs)]
    w4 = unpack_weight(w4_words, w4_scales, "e2m1")
    h = w4.T @ v
    page = f64(page0).copy()
    page[:, unstriped(offs2)] = np.tile(f64(wgs), (H // 128, 1)) * h
    x = page[:, unstriped(offs3)]
    d = x - f64(pref)[:, None]
    z = f64(gain)[:, None] * np.exp(-0.25 * np.square(d))
    return mxq(f64(wd), 0, "e4m3").T @ mxq(z, 0, "e4m3")

@@ -1,0 +1,250 @@
+from contextlib import ExitStack
+
+import concourse.mybir as mybir
+from concourse.masks import make_identity
+
+K, T, S, H, T2, PC, N = 1024, 2048, 1024, 1024, 2048, 1024, 512
+FLOPS = 2 * K * H * S + 2 * H * N * PC
+
+F32 = mybir.dt.float32
+BF16 = mybir.dt.bfloat16
+I32 = mybir.dt.int32
+U32 = mybir.dt.uint32
+U16 = mybir.dt.uint16
+U8 = mybir.dt.uint8
+FP8X4 = mybir.dt.float8_e4m3fn_x4
+FP4X4 = mybir.dt.float4_e2m1fn_x4
+ACT = mybir.ActivationFunctionType
+MULT = mybir.AluOpType.mult
+
+P = 128
+PACK = 4
+BANK = 512
+PASSES = 2
+LIST_COLS = 64
+HALF_COLS = 32
+
+
+def tile_list_place_field_atlas_kernel(
+    tc, tab_words, tab_scales, offs, w4_words, w4_scales, wgs, page0, offs2, offs3, pref, gain, wd, out
+):
+    nc = tc.nc
+    with ExitStack() as ctx:
+        lists = ctx.enter_context(tc.tile_pool(name="lists", bufs=1))
+        keep = ctx.enter_context(tc.tile_pool(name="keep", bufs=1))
+        psum = ctx.enter_context(tc.psum_pool(name="psum", bufs=8))
+
+        idx = lists.tile([P, LIST_COLS], U16, name="idx")
+        idx2 = lists.tile([P, LIST_COLS], U16, name="idx2")
+        idx3 = lists.tile([P, LIST_COLS], U16, name="idx3")
+
+        nc.sync.dma_start(idx[:], offs)
+        tab_sc = keep.tile([P, T], U8, name="tab_sc", align_bytes=64)
+        nc.vector.memset(tab_sc[32:64, :].bitcast(I32), 0)
+        nc.vector.memset(tab_sc[64:128, :].bitcast(I32), 0)
+        nc.sync.dma_start(tab_sc[0:32, :].bitcast(I32), tab_scales.rearrange("a q t -> q a t").bitcast(I32))
+        tab_w = []
+        for a in range(PASSES):
+            w = keep.tile([P, T], I32, name="big%d" % a, tag="big%d" % a, align_bytes=64)
+            nc.sync.dma_start(w[:], tab_words[a].rearrange("p t i -> p (t i)").bitcast(I32))
+            tab_w.append(w)
+
+        w4s_raw = keep.tile([P, PASSES, H], U8, name="w4s_raw", align_bytes=64)
+        nc.vector.memset(w4s_raw[:].bitcast(I32), 0)
+        for q in range(4):
+            nc.gpsimd.dma_start(
+                w4s_raw[32 * q : 32 * q + 4, :, :].bitcast(I32),
+                w4_scales[:, 4 * q : 4 * q + 4, :].rearrange("a r c -> r a c").bitcast(I32),
+            )
+        v_plane = keep.tile([P, PASSES, S], U8, name="v_plane", align_bytes=64)
+        nc.vector.memset(v_plane[:].bitcast(I32), 0)
+
+        w4_raw = [keep.tile([P, PASSES, 256], I32, name="w4_raw%d" % b, align_bytes=64) for b in range(2)]
+        w4_src = w4_words.rearrange("a p c -> p a c").bitcast(I32)
+
+        def load_w4(b):
+            nc.sync.dma_start(w4_raw[b][:], w4_src[:, :, 256 * b : 256 * (b + 1)])
+
+        page_src = page0.rearrange("(b x t y) c -> b t x y c", b=2, t=PACK, y=4)
+        pages = {}
+
+        def load_page(s):
+            b, t = divmod(s, PACK)
+            pages[s] = keep.tile([P, T2], F32, name="page%d" % s, tag="page%d" % (s % 2))
+            nc.sync.dma_start(pages[s][:], page_src[b, t])
+
+        wgs_src = wgs.rearrange("(x t y) s -> t x y s", t=PACK, y=4)
+        wg = [keep.tile([P, S], F32, name="wg%d" % t) for t in range(PACK)]
+
+        def load_wgs(t):
+            for q in range(4):
+                nc.sync.dma_start(wg[t][32 * q : 32 * (q + 1), :], wgs_src[t])
+
+        load_w4(0)
+        load_page(0)
+        load_wgs(0)
+        nc.sync.dma_start(idx2[:], offs2)
+
+        v_sc = keep.tile([P, S], U8, name="v_sc", align_bytes=64)
+        nc.vector.tensor_copy(v_sc[:], tab_sc[:].indirect(idx[:]))
+        for q in range(4):
+            (nc.gpsimd if q % 2 else nc.scalar).dma_start(
+                v_plane[32 * q : 32 * q + 4, :, :].bitcast(I32), v_sc[8 * q : 8 * q + 8, :].bitcast(I32)
+            )
+        v_w = [[keep.tile([P, BANK], U32, name="v_w%d%d" % (a, c), align_bytes=64) for c in range(2)] for a in range(PASSES)]
+
+        def gather_words(a, c):
+            nc.vector.tensor_copy(
+                v_w[a][c][:], tab_w[a][:].bitcast(U32).indirect(idx[:, HALF_COLS * c : HALF_COLS * (c + 1)])
+            )
+
+        w4_w = [keep.tile([P, PASSES, PACK, 256], U8, name="w4_w%d" % b, align_bytes=64) for b in range(2)]
+        w4_s = keep.tile([P, PASSES, 2, PACK, P], U8, name="w4_s", align_bytes=64)
+
+        def order_w4_words(b):
+            nc.vector.tensor_copy(
+                w4_w[b][:].bitcast(I32).rearrange("p a t (x e) -> p a x t e", e=2),
+                w4_raw[b][:].rearrange("p a (x t e) -> p a x t e", t=PACK, e=2),
+            )
+
+        def order_w4_scales():
+            nc.vector.tensor_copy(
+                w4_s[:].bitcast(I32).rearrange("p a b t x -> p (a b) x t"),
+                w4s_raw[:].bitcast(I32).rearrange("p a (b x t) -> p (a b) x t", b=2, t=PACK),
+            )
+
+        gather_words(0, 0)
+        gather_words(0, 1)
+        order_w4_scales()
+        gather_words(1, 0)
+        order_w4_words(0)
+        gather_words(1, 1)
+
+        nc.sync.dma_start(idx3[:], offs3)
+        load_w4(1)
+        load_wgs(1)
+        order_w4_words(1)
+
+
+        h = {}
+        for s in range(8):
+            b, t = divmod(s, PACK)
+            for c in range(2):
+                acc = psum.tile([P, BANK], F32, name="acc", tag="bank")
+                for a in range(PASSES):
+                    nc.tensor.matmul_mx(
+                        out=acc[:],
+                        lhsT=w4_w[b][:, a, t, :].bitcast(FP4X4),
+                        lhsT_scale=w4_s[:, a, b, t, :],
+                        rhs=v_w[a][c][:].bitcast(FP8X4),
+                        rhs_scale=v_plane[:, a, BANK * c : BANK * (c + 1)],
+                        start=(a == 0),
+                        stop=(a == PASSES - 1),
+                    )
+                if s == 0:
+                    h[s, c] = keep.tile([P, BANK], F32, name="h0%d" % c, tag="page1" if c == 0 else "h0")
+                    nc.scalar.copy(h[s, c][:], acc[:])
+                else:
+                    if c == 0:
+                        h[s] = keep.tile([P, S], F32, name="h%d" % s, tag="h%d" % s)
+                    nc.scalar.copy(h[s][:, BANK * c : BANK * (c + 1)], acc[:])
+
+        rows = keep.tile([P, 2, P], F32, name="rows")
+        ident = keep.tile([P, P], F32, name="ident")
+        nc.vector.memset(rows[:], 0.0)
+        nc.vector.memset(ident[:], 0.0)
+        make_identity(nc, ident[:], nomemset=True)
+        for i, vec in enumerate((pref, gain)):
+            nc.sync.dma_start(
+                rows[PACK * i : PACK * (i + 1), :, :].rearrange("t b (x y) -> t (b x) y", y=4),
+                vec.rearrange("(bx t y) -> t bx y", t=PACK, y=4),
+            )
+        turned = psum.tile([P, 2, P], F32, name="turned", tag="bank")
+        for b in range(2):
+            nc.tensor.transpose(turned[:, b, :], rows[:, b, :], ident[:])
+        consts = keep.tile([P, 2, 2 * PACK], F32, name="consts")
+        nc.scalar.copy(consts[:], turned[:, :, 0 : 2 * PACK])
+        load_wgs(2)
+        load_wgs(3)
+
+        wd_src = wd.rearrange("(b x t y) n -> b t x y n", b=2, t=PACK, y=4)
+        wd_q = [keep.tile([P, N], U32, name="wd_q%d" % b, align_bytes=64) for b in range(2)]
+        wd_s = [keep.tile([P, N], U8, name="wd_s%d" % b, align_bytes=64) for b in range(2)]
+
+        def quantise_wd(b):
+            raw = keep.tile([P, PACK, N], F32, name="wd_raw%d" % b, tag="h%d" % (b + 1))
+            for t in range(PACK):
+                nc.sync.dma_start(raw[:, t, :], wd_src[b, t])
+            woven = keep.tile([P, N, PACK], BF16, name="wd_woven%d" % b, align_bytes=64)
+            nc.scalar.copy(woven[:], raw[:].rearrange("p t n -> p n t"))
+            nc.vector.quantize_mx(
+                out=wd_q[b][:].bitcast(FP8X4), scales=wd_s[b][:], in_=woven[:].rearrange("p n t -> p (n t)")
+            )
+
+
+        z = [[keep.tile([P, BANK, PACK], BF16, name="z%d%d" % (b, c), align_bytes=64) for c in range(2)] for b in range(2)]
+        z_q = [[keep.tile([P, BANK], U32, name="z_q%d%d" % (b, c), align_bytes=64) for c in range(2)] for b in range(2)]
+        z_s = [[keep.tile([P, BANK], U8, name="z_s%d%d" % (b, c), align_bytes=64) for c in range(2)] for b in range(2)]
+        res = {}
+
+        def scatter(s, src, lo, hi):
+            t = s % PACK
+            nc.vector.tensor_tensor(
+                pages[s][:].indirect(idx2[:, lo // 16 : hi // 16]), src, wg[t][:, lo:hi], MULT
+            )
+
+        def tune(s, x, lo, hi):
+            b, t = divmod(s, PACK)
+            nc.vector.tensor_copy(x[:, lo:hi], pages[s][:].indirect(idx3[:, lo // 16 : hi // 16]))
+            nc.scalar.activation(x[:, lo:hi], x[:, lo:hi], ACT.Square, bias=consts[:, b, t : t + 1], scale=-1.0)
+            nc.scalar.activation(x[:, lo:hi], x[:, lo:hi], ACT.Exp, scale=-0.25)
+            for c in range(lo // BANK, hi // BANK):
+                nc.scalar.activation(
+                    z[b][c][:, :, t], x[:, BANK * c : BANK * (c + 1)], ACT.Copy, scale=consts[:, b, PACK + t : PACK + t + 1]
+                )
+
+        def second_product(b, c):
+            nc.vector.quantize_mx(
+                out=z_q[b][c][:].bitcast(FP8X4), scales=z_s[b][c][:], in_=z[b][c][:].rearrange("p m t -> p (m t)")
+            )
+            for nt in range(4):
+                if b == 0:
+                    res[c, nt] = psum.tile([P, BANK], F32, name="res", tag="bank")
+                nc.tensor.matmul_mx(
+                    out=res[c, nt][:],
+                    lhsT=wd_q[b][:, P * nt : P * (nt + 1)].bitcast(FP8X4),
+                    lhsT_scale=wd_s[b][:, P * nt : P * (nt + 1)],
+                    rhs=z_q[b][c][:].bitcast(FP8X4),
+                    rhs_scale=z_s[b][c][:],
+                    start=(b == 0),
+                    stop=(b == 1),
+                )
+                if b == 1:
+                    staged = keep.tile([P, BANK], F32, name="staged", tag="h%d" % (4 * c + nt))
+                    if nt % 2 == 0:
+                        nc.vector.tensor_copy(staged[:], res[c, nt][:])
+                    else:
+                        nc.scalar.copy(staged[:], res[c, nt][:])
+                    nc.sync.dma_start(out[P * nt : P * (nt + 1), BANK * c : BANK * (c + 1)], staged[:])
+
+        for s in range(8):
+            b, t = divmod(s, PACK)
+            if s == 0:
+                scatter(s, h[0, 0][:], 0, BANK)
+                load_page(1)
+                scatter(s, h[0, 1][:], BANK, S)
+            else:
+                scatter(s, h[s][:], 0, S)
+            if s in (1, 2):
+                quantise_wd(s - 1)
+            x = keep.tile([P, PC], F32, name="x%d" % s)
+            if s == 7:
+                tune(s, x, 0, BANK)
+                tune(s, x, BANK, PC)
+            else:
+                tune(s, x, 0, PC)
+            if s + 2 < 8:
+                load_page(s + 2)
+            if t == PACK - 1:
+                second_product(b, 0)
+                second_product(b, 1)

@@ -32,37 +32,32 @@ def tile_list_place_field_atlas_kernel(
     with ExitStack() as ctx:
         lists = ctx.enter_context(tc.tile_pool(name="lists", bufs=1))
         keep = ctx.enter_context(tc.tile_pool(name="keep", bufs=1))
-        psum = ctx.enter_context(tc.psum_pool(name="psum", bufs=8))
+        psum = ctx.enter_context(tc.psum_pool(name="psum", bufs=1))
 
         idx = lists.tile([P, LIST_COLS], U16, name="idx")
         idx2 = lists.tile([P, LIST_COLS], U16, name="idx2")
         idx3 = lists.tile([P, LIST_COLS], U16, name="idx3")
 
         nc.sync.dma_start(idx[:], offs)
-        tab_sc = keep.tile([P, T], U8, name="tab_sc", align_bytes=64)
+        tab_sc = keep.tile([P, T], U8, name="tab_sc", tag="page0", align_bytes=64)
         nc.vector.memset(tab_sc[32:64, :].bitcast(I32), 0)
         nc.vector.memset(tab_sc[64:128, :].bitcast(I32), 0)
         nc.sync.dma_start(tab_sc[0:32, :].bitcast(I32), tab_scales.rearrange("a q t -> q a t").bitcast(I32))
-        tab_w = []
-        for a in range(PASSES):
-            w = keep.tile([P, T], I32, name="big%d" % a, tag="big%d" % a, align_bytes=64)
-            nc.sync.dma_start(w[:], tab_words[a].rearrange("p t i -> p (t i)").bitcast(I32))
-            tab_w.append(w)
-
-        w4s_raw = keep.tile([P, PASSES, H], U8, name="w4s_raw", align_bytes=64)
-        nc.vector.memset(w4s_raw[:].bitcast(I32), 0)
+        w4s_raw = keep.tile([P, PASSES, H], U8, name="w4s_raw", tag="w4s_raw", align_bytes=64)
+        nc.gpsimd.memset(w4s_raw[:].bitcast(I32), 0)
         for q in range(4):
-            nc.gpsimd.dma_start(
+            nc.scalar.dma_start(
                 w4s_raw[32 * q : 32 * q + 4, :, :].bitcast(I32),
                 w4_scales[:, 4 * q : 4 * q + 4, :].rearrange("a r c -> r a c").bitcast(I32),
             )
         v_plane = keep.tile([P, PASSES, S], U8, name="v_plane", align_bytes=64)
         nc.vector.memset(v_plane[:].bitcast(I32), 0)
 
-        w4_raw = [keep.tile([P, PASSES, 256], I32, name="w4_raw%d" % b, align_bytes=64) for b in range(2)]
+        w4_raw = {}
         w4_src = w4_words.rearrange("a p c -> p a c").bitcast(I32)
 
         def load_w4(b):
+            w4_raw[b] = keep.tile([P, PASSES, 256], I32, name="w4_raw%d" % b, tag=("w4_raw", "v_sc")[b], align_bytes=64)
             nc.sync.dma_start(w4_raw[b][:], w4_src[:, :, 256 * b : 256 * (b + 1)])
 
         page_src = page0.rearrange("(b x t y) c -> b t x y c", b=2, t=PACK, y=4)
@@ -70,32 +65,37 @@ def tile_list_place_field_atlas_kernel(
 
         def load_page(s):
             b, t = divmod(s, PACK)
-            pages[s] = keep.tile([P, T2], F32, name="page%d" % s, tag="page%d" % (s % 2))
+            pages[s] = keep.tile([P, T2], F32, name="page%d" % s, tag="page%d" % (s % 2), align_bytes=64)
             nc.sync.dma_start(pages[s][:], page_src[b, t])
 
         wgs_src = wgs.rearrange("(x t y) s -> t x y s", t=PACK, y=4)
-        wg = [keep.tile([P, S], F32, name="wg%d" % t) for t in range(PACK)]
+        wg = {}
 
         def load_wgs(t):
+            wg[t] = keep.tile([P, S], F32, name="wg%d" % t, tag=("w4_raw", "big", "h0", "h1")[t], align_bytes=64)
             for q in range(4):
                 nc.sync.dma_start(wg[t][32 * q : 32 * (q + 1), :], wgs_src[t])
 
         load_w4(0)
-        load_page(0)
-        load_wgs(0)
+        tab_w = keep.tile([P, PASSES, T], I32, name="tab_w", tag="big", align_bytes=64)
+        nc.sync.dma_start(tab_w[:], tab_words.rearrange("a p t i -> p a (t i)").bitcast(I32))
         nc.sync.dma_start(idx2[:], offs2)
+        nc.sync.dma_start(idx3[:], offs3)
 
-        v_sc = keep.tile([P, S], U8, name="v_sc", align_bytes=64)
+        v_sc = keep.tile([P, S], U8, name="v_sc", tag="v_sc", align_bytes=64)
         nc.vector.tensor_copy(v_sc[:], tab_sc[:].indirect(idx[:]))
         for q in range(4):
-            (nc.gpsimd if q % 2 else nc.scalar).dma_start(
+            nc.scalar.dma_start(
                 v_plane[32 * q : 32 * q + 4, :, :].bitcast(I32), v_sc[8 * q : 8 * q + 8, :].bitcast(I32)
             )
-        v_w = [[keep.tile([P, BANK], U32, name="v_w%d%d" % (a, c), align_bytes=64) for c in range(2)] for a in range(PASSES)]
+        load_page(0)
+        v_w = [{}, {}]
 
         def gather_words(a, c):
+            tag = "w4s_raw" if (a, c) == (0, 1) else "v_w%d%d" % (a, c)
+            v_w[a][c] = keep.tile([P, BANK], U32, name="v_w%d%d" % (a, c), tag=tag, align_bytes=64)
             nc.vector.tensor_copy(
-                v_w[a][c][:], tab_w[a][:].bitcast(U32).indirect(idx[:, HALF_COLS * c : HALF_COLS * (c + 1)])
+                v_w[a][c][:], tab_w[:, a, :].bitcast(U32).indirect(idx[:, HALF_COLS * c : HALF_COLS * (c + 1)])
             )
 
         w4_w = [keep.tile([P, PASSES, PACK, 256], U8, name="w4_w%d" % b, align_bytes=64) for b in range(2)]
@@ -113,24 +113,41 @@ def tile_list_place_field_atlas_kernel(
                 w4s_raw[:].bitcast(I32).rearrange("p a (b x t) -> p (a b) x t", b=2, t=PACK),
             )
 
-        gather_words(0, 0)
-        gather_words(0, 1)
-        order_w4_scales()
-        gather_words(1, 0)
         order_w4_words(0)
+        load_wgs(0)
+        gather_words(0, 0)
+        gather_words(1, 0)
+        order_w4_scales()
+        gather_words(0, 1)
         gather_words(1, 1)
 
-        nc.sync.dma_start(idx3[:], offs3)
-        load_w4(1)
         load_wgs(1)
+        load_w4(1)
         order_w4_words(1)
 
+
+        consts = keep.tile([P, 2, 2 * PACK], F32, name="consts")
+
+        def make_consts():
+            rows = keep.tile([P, 2, P], F32, name="rows")
+            ident = keep.tile([P, P], F32, name="ident")
+            nc.gpsimd.memset(rows[:], 0.0)
+            make_identity(nc, ident[:])
+            for i, vec in enumerate((pref, gain)):
+                nc.gpsimd.dma_start(
+                    rows[PACK * i : PACK * (i + 1), :, :].rearrange("t b (x y) -> t (b x) y", y=4),
+                    vec.rearrange("(bx t y) -> t bx y", t=PACK, y=4),
+                )
+            turned = psum.tile([P, 2, P], F32, name="turned", tag="bank3")
+            for b in range(2):
+                nc.tensor.transpose(turned[:, b, :], rows[:, b, :], ident[:])
+            nc.scalar.copy(consts[:], turned[:, :, 0 : 2 * PACK])
 
         h = {}
         for s in range(8):
             b, t = divmod(s, PACK)
             for c in range(2):
-                acc = psum.tile([P, BANK], F32, name="acc", tag="bank")
+                acc = psum.tile([P, BANK], F32, name="acc", tag="bank%d" % ((2 * s + c) % 8))
                 for a in range(PASSES):
                     nc.tensor.matmul_mx(
                         out=acc[:],
@@ -142,43 +159,31 @@ def tile_list_place_field_atlas_kernel(
                         stop=(a == PASSES - 1),
                     )
                 if s == 0:
-                    h[s, c] = keep.tile([P, BANK], F32, name="h0%d" % c, tag="page1" if c == 0 else "h0")
+                    h[s, c] = keep.tile([P, BANK], F32, name="h0%d" % c, tag="page1" if c == 0 else "h0", align_bytes=64)
                     nc.scalar.copy(h[s, c][:], acc[:])
                 else:
                     if c == 0:
-                        h[s] = keep.tile([P, S], F32, name="h%d" % s, tag="h%d" % s)
+                        h[s] = keep.tile([P, S], F32, name="h%d" % s, tag="h%d" % s, align_bytes=64)
                     nc.scalar.copy(h[s][:, BANK * c : BANK * (c + 1)], acc[:])
+            if s == 1:
+                make_consts()
 
-        rows = keep.tile([P, 2, P], F32, name="rows")
-        ident = keep.tile([P, P], F32, name="ident")
-        nc.vector.memset(rows[:], 0.0)
-        nc.vector.memset(ident[:], 0.0)
-        make_identity(nc, ident[:], nomemset=True)
-        for i, vec in enumerate((pref, gain)):
-            nc.sync.dma_start(
-                rows[PACK * i : PACK * (i + 1), :, :].rearrange("t b (x y) -> t (b x) y", y=4),
-                vec.rearrange("(bx t y) -> t bx y", t=PACK, y=4),
-            )
-        turned = psum.tile([P, 2, P], F32, name="turned", tag="bank")
-        for b in range(2):
-            nc.tensor.transpose(turned[:, b, :], rows[:, b, :], ident[:])
-        consts = keep.tile([P, 2, 2 * PACK], F32, name="consts")
-        nc.scalar.copy(consts[:], turned[:, :, 0 : 2 * PACK])
-        load_wgs(2)
-        load_wgs(3)
 
         wd_src = wd.rearrange("(b x t y) n -> b t x y n", b=2, t=PACK, y=4)
-        wd_q = [keep.tile([P, N], U32, name="wd_q%d" % b, align_bytes=64) for b in range(2)]
+        wd_q, woven = {}, {}
         wd_s = [keep.tile([P, N], U8, name="wd_s%d" % b, align_bytes=64) for b in range(2)]
 
-        def quantise_wd(b):
-            raw = keep.tile([P, PACK, N], F32, name="wd_raw%d" % b, tag="h%d" % (b + 1))
+        def weave_wd(b):
+            raw = keep.tile([P, PACK, N], F32, name="wd_raw%d" % b, tag="h%d" % (b + 2), align_bytes=64)
             for t in range(PACK):
                 nc.sync.dma_start(raw[:, t, :], wd_src[b, t])
-            woven = keep.tile([P, N, PACK], BF16, name="wd_woven%d" % b, align_bytes=64)
-            nc.scalar.copy(woven[:], raw[:].rearrange("p t n -> p n t"))
+            woven[b] = keep.tile([P, N, PACK], BF16, name="wd_woven%d" % b, align_bytes=64)
+            nc.scalar.copy(woven[b][:], raw[:].rearrange("p t n -> p n t"))
+
+        def quantise_wd(b):
+            wd_q[b] = keep.tile([P, N], U32, name="wd_q%d" % b, tag=("h7", "wd_q")[b], align_bytes=64)
             nc.vector.quantize_mx(
-                out=wd_q[b][:].bitcast(FP8X4), scales=wd_s[b][:], in_=woven[:].rearrange("p n t -> p (n t)")
+                out=wd_q[b][:].bitcast(FP8X4), scales=wd_s[b][:], in_=woven[b][:].rearrange("p n t -> p (n t)")
             )
 
 
@@ -199,17 +204,21 @@ def tile_list_place_field_atlas_kernel(
             nc.scalar.activation(x[:, lo:hi], x[:, lo:hi], ACT.Square, bias=consts[:, b, t : t + 1], scale=-1.0)
             nc.scalar.activation(x[:, lo:hi], x[:, lo:hi], ACT.Exp, scale=-0.25)
             for c in range(lo // BANK, hi // BANK):
-                nc.scalar.activation(
-                    z[b][c][:, :, t], x[:, BANK * c : BANK * (c + 1)], ACT.Copy, scale=consts[:, b, PACK + t : PACK + t + 1]
-                )
+                g = consts[:, b, PACK + t : PACK + t + 1]
+                if s == 7:
+                    nc.vector.tensor_scalar(z[b][c][:, :, t], x[:, BANK * c : BANK * (c + 1)], g, None, MULT)
+                else:
+                    nc.scalar.activation(z[b][c][:, :, t], x[:, BANK * c : BANK * (c + 1)], ACT.Copy, scale=g)
 
-        def second_product(b, c):
+        def quantise_z(b, c):
             nc.vector.quantize_mx(
                 out=z_q[b][c][:].bitcast(FP8X4), scales=z_s[b][c][:], in_=z[b][c][:].rearrange("p m t -> p (m t)")
             )
+
+        def second_product(b, c):
             for nt in range(4):
                 if b == 0:
-                    res[c, nt] = psum.tile([P, BANK], F32, name="res", tag="bank")
+                    res[c, nt] = psum.tile([P, BANK], F32, name="res", tag="bank%d" % (4 * c + nt))
                 nc.tensor.matmul_mx(
                     out=res[c, nt][:],
                     lhsT=wd_q[b][:, P * nt : P * (nt + 1)].bitcast(FP8X4),
@@ -220,8 +229,8 @@ def tile_list_place_field_atlas_kernel(
                     stop=(b == 1),
                 )
                 if b == 1:
-                    staged = keep.tile([P, BANK], F32, name="staged", tag="h%d" % (4 * c + nt))
-                    if nt % 2 == 0:
+                    staged = keep.tile([P, BANK], F32, name="staged", tag="out%d" % (4 * c + nt))
+                    if (c, nt) in ((0, 3), (1, 0), (1, 2)):
                         nc.vector.tensor_copy(staged[:], res[c, nt][:])
                     else:
                         nc.scalar.copy(staged[:], res[c, nt][:])
@@ -233,11 +242,20 @@ def tile_list_place_field_atlas_kernel(
                 scatter(s, h[0, 0][:], 0, BANK)
                 load_page(1)
                 scatter(s, h[0, 1][:], BANK, S)
+                load_wgs(2)
             else:
                 scatter(s, h[s][:], 0, S)
-            if s in (1, 2):
-                quantise_wd(s - 1)
-            x = keep.tile([P, PC], F32, name="x%d" % s)
+            if s == 1:
+                load_wgs(3)
+            if s in (2, 3):
+                weave_wd(s - 2)
+            if s == 3:
+                quantise_wd(1)
+            if s == 7:
+                quantise_wd(0)
+                second_product(0, 0)
+                second_product(0, 1)
+            x = keep.tile([P, PC], F32, name="x%d" % s, tag="x%d" % s, align_bytes=64)
             if s == 7:
                 tune(s, x, 0, BANK)
                 tune(s, x, BANK, PC)
@@ -246,5 +264,7 @@ def tile_list_place_field_atlas_kernel(
             if s + 2 < 8:
                 load_page(s + 2)
             if t == PACK - 1:
-                second_product(b, 0)
-                second_product(b, 1)
+                quantise_z(b, 0)
+                quantise_z(b, 1)
+        second_product(1, 0)
+        second_product(1, 1)

@@ -20,6 +20,7 @@ MULT = mybir.AluOpType.mult
 P = 128
 PACK = 4
 BANK = 512
+CHUNK = 256
 PASSES = 2
 LIST_COLS = 64
 HALF_COLS = 32
@@ -39,14 +40,14 @@ def tile_list_place_field_atlas_kernel(
         idx3 = lists.tile([P, LIST_COLS], U16, name="idx3")
 
         nc.sync.dma_start(idx[:], offs)
-        tab_sc = keep.tile([P, T], U8, name="tab_sc", tag="page0", align_bytes=64)
+        tab_sc = keep.tile([P, T], U8, name="tab_sc", align_bytes=64)
         nc.vector.memset(tab_sc[32:64, :].bitcast(I32), 0)
         nc.vector.memset(tab_sc[64:128, :].bitcast(I32), 0)
         nc.sync.dma_start(tab_sc[0:32, :].bitcast(I32), tab_scales.rearrange("a q t -> q a t").bitcast(I32))
         w4s_raw = keep.tile([P, PASSES, H], U8, name="w4s_raw", tag="w4s_raw", align_bytes=64)
         nc.gpsimd.memset(w4s_raw[:].bitcast(I32), 0)
         for q in range(4):
-            nc.scalar.dma_start(
+            (nc.gpsimd if q % 2 else nc.scalar).dma_start(
                 w4s_raw[32 * q : 32 * q + 4, :, :].bitcast(I32),
                 w4_scales[:, 4 * q : 4 * q + 4, :].rearrange("a r c -> r a c").bitcast(I32),
             )
@@ -57,7 +58,7 @@ def tile_list_place_field_atlas_kernel(
         w4_src = w4_words.rearrange("a p c -> p a c").bitcast(I32)
 
         def load_w4(b):
-            w4_raw[b] = keep.tile([P, PASSES, 256], I32, name="w4_raw%d" % b, tag=("w4_raw", "v_sc")[b], align_bytes=64)
+            w4_raw[b] = keep.tile([P, PASSES, 256], I32, name="w4_raw%d" % b, tag=("w4_raw", "h0")[b], align_bytes=64)
             nc.sync.dma_start(w4_raw[b][:], w4_src[:, :, 256 * b : 256 * (b + 1)])
 
         page_src = page0.rearrange("(b x t y) c -> b t x y c", b=2, t=PACK, y=4)
@@ -72,7 +73,7 @@ def tile_list_place_field_atlas_kernel(
         wg = {}
 
         def load_wgs(t):
-            wg[t] = keep.tile([P, S], F32, name="wg%d" % t, tag=("w4_raw", "big", "h0", "h1")[t], align_bytes=64)
+            wg[t] = keep.tile([P, S], F32, name="wg%d" % t, tag=("w4_raw", "big", "v_sc", "h1")[t], align_bytes=64)
             for q in range(4):
                 nc.sync.dma_start(wg[t][32 * q : 32 * (q + 1), :], wgs_src[t])
 
@@ -81,6 +82,7 @@ def tile_list_place_field_atlas_kernel(
         nc.sync.dma_start(tab_w[:], tab_words.rearrange("a p t i -> p a (t i)").bitcast(I32))
         nc.sync.dma_start(idx2[:], offs2)
         nc.sync.dma_start(idx3[:], offs3)
+        load_page(0)
 
         v_sc = keep.tile([P, S], U8, name="v_sc", tag="v_sc", align_bytes=64)
         nc.vector.tensor_copy(v_sc[:], tab_sc[:].indirect(idx[:]))
@@ -88,7 +90,6 @@ def tile_list_place_field_atlas_kernel(
             nc.scalar.dma_start(
                 v_plane[32 * q : 32 * q + 4, :, :].bitcast(I32), v_sc[8 * q : 8 * q + 8, :].bitcast(I32)
             )
-        load_page(0)
         v_w = [{}, {}]
 
         def gather_words(a, c):
@@ -122,8 +123,7 @@ def tile_list_place_field_atlas_kernel(
         gather_words(1, 1)
 
         load_wgs(1)
-        load_w4(1)
-        order_w4_words(1)
+        load_wgs(2)
 
 
         consts = keep.tile([P, 2, 2 * PACK], F32, name="consts")
@@ -144,7 +144,8 @@ def tile_list_place_field_atlas_kernel(
             nc.scalar.copy(consts[:], turned[:, :, 0 : 2 * PACK])
 
         h = {}
-        for s in range(8):
+
+        def project(s):
             b, t = divmod(s, PACK)
             for c in range(2):
                 acc = psum.tile([P, BANK], F32, name="acc", tag="bank%d" % ((2 * s + c) % 8))
@@ -165,6 +166,9 @@ def tile_list_place_field_atlas_kernel(
                     if c == 0:
                         h[s] = keep.tile([P, S], F32, name="h%d" % s, tag="h%d" % s, align_bytes=64)
                     nc.scalar.copy(h[s][:, BANK * c : BANK * (c + 1)], acc[:])
+
+        for s in range(PACK):
+            project(s)
             if s == 1:
                 make_consts()
 
@@ -187,9 +191,9 @@ def tile_list_place_field_atlas_kernel(
             )
 
 
-        z = [[keep.tile([P, BANK, PACK], BF16, name="z%d%d" % (b, c), align_bytes=64) for c in range(2)] for b in range(2)]
-        z_q = [[keep.tile([P, BANK], U32, name="z_q%d%d" % (b, c), align_bytes=64) for c in range(2)] for b in range(2)]
-        z_s = [[keep.tile([P, BANK], U8, name="z_s%d%d" % (b, c), align_bytes=64) for c in range(2)] for b in range(2)]
+        z = [keep.tile([P, PC, PACK], BF16, name="z%d" % b, align_bytes=64) for b in range(2)]
+        z_q = [keep.tile([P, PC], U32, name="z_q%d" % b, align_bytes=64) for b in range(2)]
+        z_s = [keep.tile([P, PC], U8, name="z_s%d" % b, align_bytes=64) for b in range(2)]
         res = {}
 
         def scatter(s, src, lo, hi):
@@ -198,43 +202,36 @@ def tile_list_place_field_atlas_kernel(
                 pages[s][:].indirect(idx2[:, lo // 16 : hi // 16]), src, wg[t][:, lo:hi], MULT
             )
 
-        def tune(s, x, lo, hi):
+        def tune(s, x, e, spans):
             b, t = divmod(s, PACK)
-            nc.vector.tensor_copy(x[:, lo:hi], pages[s][:].indirect(idx3[:, lo // 16 : hi // 16]))
-            nc.scalar.activation(x[:, lo:hi], x[:, lo:hi], ACT.Square, bias=consts[:, b, t : t + 1], scale=-1.0)
-            nc.scalar.activation(x[:, lo:hi], x[:, lo:hi], ACT.Exp, scale=-0.25)
-            for c in range(lo // BANK, hi // BANK):
-                g = consts[:, b, PACK + t : PACK + t + 1]
-                if s == 7:
-                    nc.vector.tensor_scalar(z[b][c][:, :, t], x[:, BANK * c : BANK * (c + 1)], g, None, MULT)
-                else:
-                    nc.scalar.activation(z[b][c][:, :, t], x[:, BANK * c : BANK * (c + 1)], ACT.Copy, scale=g)
+            for lo, hi in spans:
+                nc.vector.tensor_copy(x[:, lo:hi], pages[s][:].indirect(idx3[:, lo // 16 : hi // 16]))
+                nc.scalar.activation(e[:, lo:hi], x[:, lo:hi], ACT.Square, bias=consts[:, b, t : t + 1], scale=-1.0)
+            for lo, hi in spans:
+                nc.scalar.activation(e[:, lo:hi], e[:, lo:hi], ACT.Exp, scale=-0.25)
 
-        def quantise_z(b, c):
+        def gain_of(s):
+            b, t = divmod(s, PACK)
+            return consts[:, b, PACK + t : PACK + t + 1]
+
+        def quantise_z(b, lo, hi):
             nc.vector.quantize_mx(
-                out=z_q[b][c][:].bitcast(FP8X4), scales=z_s[b][c][:], in_=z[b][c][:].rearrange("p m t -> p (m t)")
+                out=z_q[b][:, lo:hi].bitcast(FP8X4),
+                scales=z_s[b][:, lo:hi],
+                in_=z[b][:, lo:hi, :].rearrange("p m t -> p (m t)"),
             )
 
-        def second_product(b, c):
-            for nt in range(4):
-                if b == 0:
-                    res[c, nt] = psum.tile([P, BANK], F32, name="res", tag="bank%d" % (4 * c + nt))
-                nc.tensor.matmul_mx(
-                    out=res[c, nt][:],
-                    lhsT=wd_q[b][:, P * nt : P * (nt + 1)].bitcast(FP8X4),
-                    lhsT_scale=wd_s[b][:, P * nt : P * (nt + 1)],
-                    rhs=z_q[b][c][:].bitcast(FP8X4),
-                    rhs_scale=z_s[b][c][:],
-                    start=(b == 0),
-                    stop=(b == 1),
-                )
-                if b == 1:
-                    staged = keep.tile([P, BANK], F32, name="staged", tag="out%d" % (4 * c + nt))
-                    if (c, nt) in ((0, 3), (1, 0), (1, 2)):
-                        nc.vector.tensor_copy(staged[:], res[c, nt][:])
-                    else:
-                        nc.scalar.copy(staged[:], res[c, nt][:])
-                    nc.sync.dma_start(out[P * nt : P * (nt + 1), BANK * c : BANK * (c + 1)], staged[:])
+        def out_pass(k, nt, b):
+            cols = slice(CHUNK * k, CHUNK * (k + 1))
+            nc.tensor.matmul_mx(
+                out=res[k, nt // 2][:, nt % 2, :],
+                lhsT=wd_q[b][:, P * nt : P * (nt + 1)].bitcast(FP8X4),
+                lhsT_scale=wd_s[b][:, P * nt : P * (nt + 1)],
+                rhs=z_q[b][:, cols].bitcast(FP8X4),
+                rhs_scale=z_s[b][:, cols],
+                start=(b == 0),
+                stop=(b == 1),
+            )
 
         for s in range(8):
             b, t = divmod(s, PACK)
@@ -242,7 +239,10 @@ def tile_list_place_field_atlas_kernel(
                 scatter(s, h[0, 0][:], 0, BANK)
                 load_page(1)
                 scatter(s, h[0, 1][:], BANK, S)
-                load_wgs(2)
+                load_w4(1)
+                order_w4_words(1)
+                for later in range(PACK, 2 * PACK):
+                    project(later)
             else:
                 scatter(s, h[s][:], 0, S)
             if s == 1:
@@ -252,19 +252,42 @@ def tile_list_place_field_atlas_kernel(
             if s == 3:
                 quantise_wd(1)
             if s == 7:
-                quantise_wd(0)
-                second_product(0, 0)
-                second_product(0, 1)
+                break
             x = keep.tile([P, PC], F32, name="x%d" % s, tag="x%d" % s, align_bytes=64)
-            if s == 7:
-                tune(s, x, 0, BANK)
-                tune(s, x, BANK, PC)
-            else:
-                tune(s, x, 0, PC)
+            tune(s, x, x, [(0, PC)])
+            nc.scalar.activation(z[b][:, :, t], x[:], ACT.Copy, scale=gain_of(s))
             if s + 2 < 8:
                 load_page(s + 2)
-            if t == PACK - 1:
-                quantise_z(b, 0)
-                quantise_z(b, 1)
-        second_product(1, 0)
-        second_product(1, 1)
+            if s == 3:
+                quantise_z(0, 0, PC)
+
+        quantise_wd(0)
+        for k in range(4):
+            for j in range(2):
+                res[k, j] = psum.tile([P, 2, CHUNK], F32, name="res", tag="bank%d" % (2 * k + j))
+                out_pass(k, 2 * j, 0)
+        x = keep.tile([P, PC], F32, name="x7", tag="x7", align_bytes=64)
+        e = keep.tile([P, PC], F32, name="e7", tag="x6", align_bytes=64)
+        for lo in range(0, PC, 2 * CHUNK):
+            tune(7, x, e, [(lo, lo + CHUNK), (lo + CHUNK, lo + 2 * CHUNK)])
+        for k in range(4):
+            lo, hi = CHUNK * k, CHUNK * (k + 1)
+            if k < 3:
+                nc.vector.tensor_scalar(z[1][:, lo:hi, PACK - 1], e[:, lo:hi], gain_of(7), None, MULT)
+            else:
+                nc.scalar.activation(z[1][:, lo:hi, PACK - 1], e[:, lo:hi], ACT.Copy, scale=gain_of(7))
+            if k > 0:
+                quantise_z(1, lo - CHUNK, lo)
+        quantise_z(1, PC - CHUNK, PC)
+        out_v = out.rearrange("(j i p) m -> j p i m", j=2, i=2)
+        for k in range(4):
+            for j in range(2):
+                out_pass(k, 2 * j, 1)
+                out_pass(k, 2 * j + 1, 0)
+                out_pass(k, 2 * j + 1, 1)
+                staged = keep.tile([P, 2, CHUNK], F32, name="staged", tag="out%d" % (2 * k + j))
+                if k >= 2 and j == 1:
+                    nc.vector.tensor_copy(staged[:], res[k, j][:])
+                else:
+                    nc.scalar.copy(staged[:], res[k, j][:])
+                nc.sync.dma_start(out_v[j][:, :, CHUNK * k : CHUNK * (k + 1)], staged[:])

@@ -3,8 +3,8 @@ from contextlib import ExitStack
 import concourse.mybir as mybir
 from concourse.masks import make_identity
 
-K, T, S, H, T2, PC, N = 1024, 2048, 1024, 1024, 2048, 1024, 512
-FLOPS = 2 * K * H * S + 2 * H * N * PC
+K, T, S, H, T2, M, N = 1024, 2048, 1024, 1024, 2048, 1024, 512
+FLOPS = 2 * K * H * S + 2 * H * N * M
 
 F32 = mybir.dt.float32
 BF16 = mybir.dt.bfloat16
@@ -19,11 +19,17 @@ MULT = mybir.AluOpType.mult
 
 P = 128
 PACK = 4
-BANK = 512
-CHUNK = 256
 PASSES = 2
-LIST_COLS = 64
-HALF_COLS = 32
+SLICES = PASSES * PACK
+LAST = SLICES - 1
+QUADRANTS = 4
+RUN = 4
+BANK = 512
+BANKS = 8
+PER_COLUMN = 16
+CHUNK = 256
+CHUNKS = M // CHUNK
+W4_WORDS = BANK // 2
 
 
 def tile_list_place_field_atlas_kernel(
@@ -35,19 +41,22 @@ def tile_list_place_field_atlas_kernel(
         keep = ctx.enter_context(tc.tile_pool(name="keep", bufs=1))
         psum = ctx.enter_context(tc.psum_pool(name="psum", bufs=1))
 
-        idx = lists.tile([P, LIST_COLS], U16, name="idx")
-        idx2 = lists.tile([P, LIST_COLS], U16, name="idx2")
-        idx3 = lists.tile([P, LIST_COLS], U16, name="idx3")
+        idx = lists.tile([P, S // PER_COLUMN], U16, name="idx")
+        idx2 = lists.tile([P, S // PER_COLUMN], U16, name="idx2")
+        idx3 = lists.tile([P, M // PER_COLUMN], U16, name="idx3")
+
+        def entries(offsets, lo, hi):
+            return offsets[:, lo // PER_COLUMN : hi // PER_COLUMN]
 
         nc.sync.dma_start(idx[:], offs)
-        tab_sc = keep.tile([P, T], U8, name="tab_sc", align_bytes=64)
+        tab_sc = keep.tile([P, T], U8, name="tab_sc", tag="page0", align_bytes=64)
         nc.vector.memset(tab_sc[32:64, :].bitcast(I32), 0)
         nc.vector.memset(tab_sc[64:128, :].bitcast(I32), 0)
         nc.sync.dma_start(tab_sc[0:32, :].bitcast(I32), tab_scales.rearrange("a q t -> q a t").bitcast(I32))
         w4s_raw = keep.tile([P, PASSES, H], U8, name="w4s_raw", tag="w4s_raw", align_bytes=64)
         nc.gpsimd.memset(w4s_raw[:].bitcast(I32), 0)
-        for q in range(4):
-            (nc.gpsimd if q % 2 else nc.scalar).dma_start(
+        for q in range(QUADRANTS):
+            nc.gpsimd.dma_start(
                 w4s_raw[32 * q : 32 * q + 4, :, :].bitcast(I32),
                 w4_scales[:, 4 * q : 4 * q + 4, :].rearrange("a r c -> r a c").bitcast(I32),
             )
@@ -58,10 +67,12 @@ def tile_list_place_field_atlas_kernel(
         w4_src = w4_words.rearrange("a p c -> p a c").bitcast(I32)
 
         def load_w4(b):
-            w4_raw[b] = keep.tile([P, PASSES, 256], I32, name="w4_raw%d" % b, tag=("w4_raw", "h0")[b], align_bytes=64)
-            nc.sync.dma_start(w4_raw[b][:], w4_src[:, :, 256 * b : 256 * (b + 1)])
+            w4_raw[b] = keep.tile(
+                [P, PASSES, W4_WORDS], I32, name="w4_raw%d" % b, tag=("w4_raw", "h0")[b], align_bytes=64
+            )
+            nc.sync.dma_start(w4_raw[b][:], w4_src[:, :, W4_WORDS * b : W4_WORDS * (b + 1)])
 
-        page_src = page0.rearrange("(b x t y) c -> b t x y c", b=2, t=PACK, y=4)
+        page_src = page0.rearrange("(b x t y) c -> b t x y c", b=PASSES, t=PACK, y=RUN)
         pages = {}
 
         def load_page(s):
@@ -69,38 +80,38 @@ def tile_list_place_field_atlas_kernel(
             pages[s] = keep.tile([P, T2], F32, name="page%d" % s, tag="page%d" % (s % 2), align_bytes=64)
             nc.sync.dma_start(pages[s][:], page_src[b, t])
 
-        wgs_src = wgs.rearrange("(x t y) s -> t x y s", t=PACK, y=4)
+        wgs_src = wgs.rearrange("(x t y) s -> t x y s", t=PACK, y=RUN)
         wg = {}
 
         def load_wgs(t):
-            wg[t] = keep.tile([P, S], F32, name="wg%d" % t, tag=("w4_raw", "big", "v_sc", "h1")[t], align_bytes=64)
-            for q in range(4):
+            wg[t] = keep.tile([P, S], F32, name="wg%d" % t, tag=("wg0", "tab_w", "w4_raw", "h1")[t], align_bytes=64)
+            for q in range(QUADRANTS):
                 nc.sync.dma_start(wg[t][32 * q : 32 * (q + 1), :], wgs_src[t])
 
         load_w4(0)
-        tab_w = keep.tile([P, PASSES, T], I32, name="tab_w", tag="big", align_bytes=64)
+        tab_w = keep.tile([P, PASSES, T], I32, name="tab_w", tag="tab_w", align_bytes=64)
         nc.sync.dma_start(tab_w[:], tab_words.rearrange("a p t i -> p a (t i)").bitcast(I32))
         nc.sync.dma_start(idx2[:], offs2)
         nc.sync.dma_start(idx3[:], offs3)
-        load_page(0)
+        load_wgs(0)
 
         v_sc = keep.tile([P, S], U8, name="v_sc", tag="v_sc", align_bytes=64)
         nc.vector.tensor_copy(v_sc[:], tab_sc[:].indirect(idx[:]))
-        for q in range(4):
+        for q in range(QUADRANTS):
             nc.scalar.dma_start(
                 v_plane[32 * q : 32 * q + 4, :, :].bitcast(I32), v_sc[8 * q : 8 * q + 8, :].bitcast(I32)
             )
-        v_w = [{}, {}]
+        load_page(0)
+        v_w = {}
 
-        def gather_words(a, c):
-            tag = "w4s_raw" if (a, c) == (0, 1) else "v_w%d%d" % (a, c)
-            v_w[a][c] = keep.tile([P, BANK], U32, name="v_w%d%d" % (a, c), tag=tag, align_bytes=64)
+        def gather_words(a, c, tag):
+            v_w[a, c] = keep.tile([P, BANK], U32, name="v_w%d%d" % (a, c), tag=tag, align_bytes=64)
             nc.vector.tensor_copy(
-                v_w[a][c][:], tab_w[:, a, :].bitcast(U32).indirect(idx[:, HALF_COLS * c : HALF_COLS * (c + 1)])
+                v_w[a, c][:], tab_w[:, a, :].bitcast(U32).indirect(entries(idx, BANK * c, BANK * (c + 1)))
             )
 
-        w4_w = [keep.tile([P, PASSES, PACK, 256], U8, name="w4_w%d" % b, align_bytes=64) for b in range(2)]
-        w4_s = keep.tile([P, PASSES, 2, PACK, P], U8, name="w4_s", align_bytes=64)
+        w4_w = [keep.tile([P, PASSES, PACK, 2 * P], U8, name="w4_w%d" % b, align_bytes=64) for b in range(PASSES)]
+        w4_s = keep.tile([P, PASSES, PASSES, PACK, P], U8, name="w4_s", align_bytes=64)
 
         def order_w4_words(b):
             nc.vector.tensor_copy(
@@ -108,38 +119,32 @@ def tile_list_place_field_atlas_kernel(
                 w4_raw[b][:].rearrange("p a (x t e) -> p a x t e", t=PACK, e=2),
             )
 
-        def order_w4_scales():
-            nc.vector.tensor_copy(
-                w4_s[:].bitcast(I32).rearrange("p a b t x -> p (a b) x t"),
-                w4s_raw[:].bitcast(I32).rearrange("p a (b x t) -> p (a b) x t", b=2, t=PACK),
-            )
-
         order_w4_words(0)
-        load_wgs(0)
-        gather_words(0, 0)
-        gather_words(1, 0)
-        order_w4_scales()
-        gather_words(0, 1)
-        gather_words(1, 1)
-
-        load_wgs(1)
         load_wgs(2)
+        gather_words(0, 0, "v_w00")
+        gather_words(1, 0, "v_w10")
+        nc.vector.tensor_copy(
+            w4_s[:].bitcast(I32).rearrange("p a b t x -> p (a b) x t"),
+            w4s_raw[:].bitcast(I32).rearrange("p a (b x t) -> p (a b) x t", b=PASSES, t=PACK),
+        )
+        gather_words(0, 1, "w4s_raw")
+        gather_words(1, 1, "v_w11")
+        load_wgs(1)
 
-
-        consts = keep.tile([P, 2, 2 * PACK], F32, name="consts")
+        consts = keep.tile([P, PASSES, 2 * PACK], F32, name="consts")
 
         def make_consts():
-            rows = keep.tile([P, 2, P], F32, name="rows")
+            rows = keep.tile([P, PASSES, P], F32, name="rows", tag="v_sc", align_bytes=64)
             ident = keep.tile([P, P], F32, name="ident")
             nc.gpsimd.memset(rows[:], 0.0)
             make_identity(nc, ident[:])
             for i, vec in enumerate((pref, gain)):
-                nc.gpsimd.dma_start(
-                    rows[PACK * i : PACK * (i + 1), :, :].rearrange("t b (x y) -> t (b x) y", y=4),
-                    vec.rearrange("(bx t y) -> t bx y", t=PACK, y=4),
+                nc.sync.dma_start(
+                    rows[PACK * i : PACK * (i + 1), :, :].rearrange("t b (x y) -> t (b x) y", y=RUN),
+                    vec.rearrange("(bx t y) -> t bx y", t=PACK, y=RUN),
                 )
-            turned = psum.tile([P, 2, P], F32, name="turned", tag="bank3")
-            for b in range(2):
+            turned = psum.tile([P, PASSES, P], F32, name="turned", tag="bank3")
+            for b in range(PASSES):
                 nc.tensor.transpose(turned[:, b, :], rows[:, b, :], ident[:])
             nc.scalar.copy(consts[:], turned[:, :, 0 : 2 * PACK])
 
@@ -148,77 +153,77 @@ def tile_list_place_field_atlas_kernel(
         def project(s):
             b, t = divmod(s, PACK)
             for c in range(2):
-                acc = psum.tile([P, BANK], F32, name="acc", tag="bank%d" % ((2 * s + c) % 8))
+                acc = psum.tile([P, BANK], F32, name="acc", tag="bank%d" % ((2 * s + c) % BANKS))
                 for a in range(PASSES):
                     nc.tensor.matmul_mx(
                         out=acc[:],
                         lhsT=w4_w[b][:, a, t, :].bitcast(FP4X4),
                         lhsT_scale=w4_s[:, a, b, t, :],
-                        rhs=v_w[a][c][:].bitcast(FP8X4),
+                        rhs=v_w[a, c][:].bitcast(FP8X4),
                         rhs_scale=v_plane[:, a, BANK * c : BANK * (c + 1)],
                         start=(a == 0),
                         stop=(a == PASSES - 1),
                     )
                 if s == 0:
-                    h[s, c] = keep.tile([P, BANK], F32, name="h0%d" % c, tag="page1" if c == 0 else "h0", align_bytes=64)
+                    h[s, c] = keep.tile([P, BANK], F32, name="h0%d" % c, tag=("page1", "h0")[c], align_bytes=64)
                     nc.scalar.copy(h[s, c][:], acc[:])
                 else:
                     if c == 0:
                         h[s] = keep.tile([P, S], F32, name="h%d" % s, tag="h%d" % s, align_bytes=64)
                     nc.scalar.copy(h[s][:, BANK * c : BANK * (c + 1)], acc[:])
 
-        for s in range(PACK):
-            project(s)
-            if s == 1:
-                make_consts()
+        project(0)
+        project(1)
+        make_consts()
+        project(2)
+        project(3)
 
-
-        wd_src = wd.rearrange("(b x t y) n -> b t x y n", b=2, t=PACK, y=4)
-        wd_q, woven = {}, {}
-        wd_s = [keep.tile([P, N], U8, name="wd_s%d" % b, align_bytes=64) for b in range(2)]
+        wd_src = wd.rearrange("(b x t y) n -> b t x y n", b=PASSES, t=PACK, y=RUN)
+        wd_q, wd_woven = {}, {}
+        wd_s = [keep.tile([P, N], U8, name="wd_s%d" % b, align_bytes=64) for b in range(PASSES)]
 
         def weave_wd(b):
             raw = keep.tile([P, PACK, N], F32, name="wd_raw%d" % b, tag="h%d" % (b + 2), align_bytes=64)
             for t in range(PACK):
                 nc.sync.dma_start(raw[:, t, :], wd_src[b, t])
-            woven[b] = keep.tile([P, N, PACK], BF16, name="wd_woven%d" % b, align_bytes=64)
-            nc.scalar.copy(woven[b][:], raw[:].rearrange("p t n -> p n t"))
+            wd_woven[b] = keep.tile([P, N, PACK], BF16, name="wd_woven%d" % b, align_bytes=64)
+            nc.scalar.copy(wd_woven[b][:], raw[:].rearrange("p t n -> p n t"))
 
-        def quantise_wd(b):
-            wd_q[b] = keep.tile([P, N], U32, name="wd_q%d" % b, tag=("h7", "wd_q")[b], align_bytes=64)
+        def quantise_wd(b, tag):
+            wd_q[b] = keep.tile([P, N], U32, name="wd_q%d" % b, tag=tag, align_bytes=64)
             nc.vector.quantize_mx(
-                out=wd_q[b][:].bitcast(FP8X4), scales=wd_s[b][:], in_=woven[b][:].rearrange("p n t -> p (n t)")
+                out=wd_q[b][:].bitcast(FP8X4), scales=wd_s[b][:], in_=wd_woven[b][:].rearrange("p n t -> p (n t)")
             )
 
-
-        z = [keep.tile([P, PC, PACK], BF16, name="z%d" % b, align_bytes=64) for b in range(2)]
-        z_q = [keep.tile([P, PC], U32, name="z_q%d" % b, align_bytes=64) for b in range(2)]
-        z_s = [keep.tile([P, PC], U8, name="z_s%d" % b, align_bytes=64) for b in range(2)]
+        z_rows = [keep.tile([P, PACK, M], BF16, name="z_rows%d" % b) for b in range(PASSES)]
+        z_woven = [keep.tile([P, M, PACK], BF16, name="z_woven%d" % b, align_bytes=64) for b in range(PASSES)]
+        z_q = [keep.tile([P, M], U32, name="z_q%d" % b, align_bytes=64) for b in range(PASSES)]
+        z_s = [keep.tile([P, M], U8, name="z_s%d" % b, align_bytes=64) for b in range(PASSES)]
         res = {}
 
-        def scatter(s, src, lo, hi):
-            t = s % PACK
-            nc.vector.tensor_tensor(
-                pages[s][:].indirect(idx2[:, lo // 16 : hi // 16]), src, wg[t][:, lo:hi], MULT
-            )
+        def scatter(s, values, lo, hi):
+            nc.vector.tensor_tensor(pages[s][:].indirect(entries(idx2, lo, hi)), values, wg[s % PACK][:, lo:hi], MULT)
 
-        def tune(s, x, e, spans):
+        def tune(s, x, spans):
             b, t = divmod(s, PACK)
             for lo, hi in spans:
-                nc.vector.tensor_copy(x[:, lo:hi], pages[s][:].indirect(idx3[:, lo // 16 : hi // 16]))
-                nc.scalar.activation(e[:, lo:hi], x[:, lo:hi], ACT.Square, bias=consts[:, b, t : t + 1], scale=-1.0)
+                nc.vector.tensor_copy(x[:, lo:hi], pages[s][:].indirect(entries(idx3, lo, hi)))
+                nc.scalar.activation(x[:, lo:hi], x[:, lo:hi], ACT.Square, bias=consts[:, b, t : t + 1], scale=-1.0)
             for lo, hi in spans:
-                nc.scalar.activation(e[:, lo:hi], e[:, lo:hi], ACT.Exp, scale=-0.25)
+                nc.scalar.activation(x[:, lo:hi], x[:, lo:hi], ACT.Exp, scale=-0.25)
+            for lo, hi in spans:
+                nc.scalar.activation(
+                    z_rows[b][:, t, lo:hi], x[:, lo:hi], ACT.Copy, scale=consts[:, b, PACK + t : PACK + t + 1]
+                )
 
-        def gain_of(s):
-            b, t = divmod(s, PACK)
-            return consts[:, b, PACK + t : PACK + t + 1]
+        def weave_z(copy, b, slots, lo, hi):
+            copy(z_woven[b][:, lo:hi, slots], z_rows[b][:, slots, lo:hi].rearrange("p t m -> p m t"))
 
         def quantise_z(b, lo, hi):
             nc.vector.quantize_mx(
                 out=z_q[b][:, lo:hi].bitcast(FP8X4),
                 scales=z_s[b][:, lo:hi],
-                in_=z[b][:, lo:hi, :].rearrange("p m t -> p (m t)"),
+                in_=z_woven[b][:, lo:hi, :].rearrange("p m t -> p (m t)"),
             )
 
         def out_pass(k, nt, b):
@@ -230,63 +235,66 @@ def tile_list_place_field_atlas_kernel(
                 rhs=z_q[b][:, cols].bitcast(FP8X4),
                 rhs_scale=z_s[b][:, cols],
                 start=(b == 0),
-                stop=(b == 1),
+                stop=(b == PASSES - 1),
             )
 
-        for s in range(8):
-            b, t = divmod(s, PACK)
+        def after_scatter(s):
+            if s == 1:
+                load_wgs(3)
+            if s in (2, 3):
+                weave_wd(s - 2)
+            if s == 3:
+                quantise_wd(1, "wd_q1")
+
+        def after_tune(s):
+            if s == PACK - 1:
+                for lo in range(0, M, BANK):
+                    weave_z(nc.scalar.copy, 0, slice(0, PACK), lo, lo + BANK)
+                quantise_z(0, 0, M)
+            if s == PACK + 1:
+                weave_z(nc.scalar.copy, 1, slice(0, 2), 0, M)
+
+        for s in range(LAST):
             if s == 0:
                 scatter(s, h[0, 0][:], 0, BANK)
                 load_page(1)
                 scatter(s, h[0, 1][:], BANK, S)
                 load_w4(1)
                 order_w4_words(1)
-                for later in range(PACK, 2 * PACK):
+                for later in range(PACK, SLICES):
                     project(later)
             else:
                 scatter(s, h[s][:], 0, S)
-            if s == 1:
-                load_wgs(3)
-            if s in (2, 3):
-                weave_wd(s - 2)
-            if s == 3:
-                quantise_wd(1)
-            if s == 7:
-                break
-            x = keep.tile([P, PC], F32, name="x%d" % s, tag="x%d" % s, align_bytes=64)
-            tune(s, x, x, [(0, PC)])
-            nc.scalar.activation(z[b][:, :, t], x[:], ACT.Copy, scale=gain_of(s))
-            if s + 2 < 8:
+            after_scatter(s)
+            x = keep.tile([P, M], F32, name="x%d" % s, align_bytes=64)
+            tune(s, x, [(0, M)])
+            if s + 2 < SLICES:
                 load_page(s + 2)
-            if s == 3:
-                quantise_z(0, 0, PC)
+            after_tune(s)
 
-        quantise_wd(0)
-        for k in range(4):
+        scatter(LAST, h[LAST][:], 0, S)
+        x = keep.tile([P, M], F32, name="x%d" % LAST, align_bytes=64)
+        spans = [(CHUNK * k, CHUNK * (k + 1)) for k in range(CHUNKS)]
+        tune(LAST, x, spans[:2])
+        quantise_wd(0, "h%d" % LAST)
+        for k in range(CHUNKS):
             for j in range(2):
                 res[k, j] = psum.tile([P, 2, CHUNK], F32, name="res", tag="bank%d" % (2 * k + j))
                 out_pass(k, 2 * j, 0)
-        x = keep.tile([P, PC], F32, name="x7", tag="x7", align_bytes=64)
-        e = keep.tile([P, PC], F32, name="e7", tag="x6", align_bytes=64)
-        for lo in range(0, PC, 2 * CHUNK):
-            tune(7, x, e, [(lo, lo + CHUNK), (lo + CHUNK, lo + 2 * CHUNK)])
-        for k in range(4):
-            lo, hi = CHUNK * k, CHUNK * (k + 1)
-            if k < 3:
-                nc.vector.tensor_scalar(z[1][:, lo:hi, PACK - 1], e[:, lo:hi], gain_of(7), None, MULT)
-            else:
-                nc.scalar.activation(z[1][:, lo:hi, PACK - 1], e[:, lo:hi], ACT.Copy, scale=gain_of(7))
+        tune(LAST, x, spans[2:])
+        for k in range(CHUNKS):
+            weave_z(nc.vector.tensor_copy, 1, slice(2, PACK), *spans[k])
             if k > 0:
-                quantise_z(1, lo - CHUNK, lo)
-        quantise_z(1, PC - CHUNK, PC)
+                quantise_z(1, *spans[k - 1])
+        quantise_z(1, *spans[-1])
         out_v = out.rearrange("(j i p) m -> j p i m", j=2, i=2)
-        for k in range(4):
+        for k in range(CHUNKS):
             for j in range(2):
                 out_pass(k, 2 * j, 1)
                 out_pass(k, 2 * j + 1, 0)
                 out_pass(k, 2 * j + 1, 1)
-                staged = keep.tile([P, 2, CHUNK], F32, name="staged", tag="out%d" % (2 * k + j))
-                if k >= 2 and j == 1:
+                staged = keep.tile([P, 2, CHUNK], F32, name="staged%d%d" % (k, j))
+                if k >= CHUNKS - 2 and j == 1:
                     nc.vector.tensor_copy(staged[:], res[k, j][:])
                 else:
                     nc.scalar.copy(staged[:], res[k, j][:])

@@ -39,6 +39,8 @@ def tile_list_place_field_atlas_kernel(
     with ExitStack() as ctx:
         lists = ctx.enter_context(tc.tile_pool(name="lists", bufs=1))
         keep = ctx.enter_context(tc.tile_pool(name="keep", bufs=1))
+        head = ctx.enter_context(tc.tile_pool(name="head", bufs=1))
+        tail = ctx.enter_context(tc.tile_pool(name="tail", bufs=1))
         psum = ctx.enter_context(tc.psum_pool(name="psum", bufs=1))
 
         idx = lists.tile([P, S // PER_COLUMN], U16, name="idx")
@@ -48,20 +50,15 @@ def tile_list_place_field_atlas_kernel(
         def entries(offsets, lo, hi):
             return offsets[:, lo // PER_COLUMN : hi // PER_COLUMN]
 
-        nc.sync.dma_start(idx[:], offs)
-        tab_sc = keep.tile([P, T], U8, name="tab_sc", tag="page0", align_bytes=64)
+        tab_sc = keep.tile([P, T], U8, name="tab_sc", align_bytes=64)
+        w4s_raw = keep.tile([32, H], U8, name="w4s_raw", align_bytes=64)
+        planes = keep.tile([P, PASSES, S + H], U8, name="planes", align_bytes=64)
         nc.vector.memset(tab_sc[32:64, :].bitcast(I32), 0)
         nc.vector.memset(tab_sc[64:128, :].bitcast(I32), 0)
+        nc.vector.memset(planes[:].bitcast(I32), 0)
+        nc.sync.dma_start(idx[:], offs)
         nc.sync.dma_start(tab_sc[0:32, :].bitcast(I32), tab_scales.rearrange("a q t -> q a t").bitcast(I32))
-        w4s_raw = keep.tile([P, PASSES, H], U8, name="w4s_raw", tag="w4s_raw", align_bytes=64)
-        nc.gpsimd.memset(w4s_raw[:].bitcast(I32), 0)
-        for q in range(QUADRANTS):
-            nc.gpsimd.dma_start(
-                w4s_raw[32 * q : 32 * q + 4, :, :].bitcast(I32),
-                w4_scales[:, 4 * q : 4 * q + 4, :].rearrange("a r c -> r a c").bitcast(I32),
-            )
-        v_plane = keep.tile([P, PASSES, S], U8, name="v_plane", align_bytes=64)
-        nc.vector.memset(v_plane[:].bitcast(I32), 0)
+        nc.sync.dma_start(w4s_raw[:].bitcast(I32), w4_scales.rearrange("a q c -> q a c").bitcast(I32))
 
         w4_raw = {}
         w4_src = w4_words.rearrange("a p c -> p a c").bitcast(I32)
@@ -77,41 +74,58 @@ def tile_list_place_field_atlas_kernel(
 
         def load_page(s):
             b, t = divmod(s, PACK)
-            pages[s] = keep.tile([P, T2], F32, name="page%d" % s, tag="page%d" % (s % 2), align_bytes=64)
+            if s % 2 == 0:
+                pages[s] = head.tile([P, T2], F32, name="page%d" % s, tag="page0", offset=4 * 1024)
+            else:
+                pages[s] = keep.tile([P, T2], F32, name="page%d" % s, tag="page1", align_bytes=64)
             nc.sync.dma_start(pages[s][:], page_src[b, t])
 
         wgs_src = wgs.rearrange("(x t y) s -> t x y s", t=PACK, y=RUN)
         wg = {}
 
         def load_wgs(t):
-            wg[t] = keep.tile([P, S], F32, name="wg%d" % t, tag=("wg0", "tab_w", "w4_raw", "h1")[t], align_bytes=64)
-            for q in range(QUADRANTS):
-                nc.sync.dma_start(wg[t][32 * q : 32 * (q + 1), :], wgs_src[t])
+            if t == 0:
+                wg[t] = head.tile([P, S], F32, name="wg0", offset=0)
+                spans = [(0, BANK), (BANK, S)]
+            else:
+                wg[t] = keep.tile([P, S], F32, name="wg%d" % t, tag=("tab_w1", "tab_w0", "h1")[t - 1], align_bytes=64)
+                spans = [(0, S)]
+            for lo, hi in spans:
+                for q in range(QUADRANTS):
+                    nc.sync.dma_start(wg[t][32 * q : 32 * (q + 1), lo:hi], wgs_src[t][:, :, lo:hi])
 
+        tab_w = {}
+
+        def load_table(a):
+            tab_w[a] = keep.tile([P, T], I32, name="tab_w%d" % a, tag="tab_w%d" % a, align_bytes=64)
+            nc.sync.dma_start(tab_w[a][:], tab_words[a].rearrange("p t i -> p (t i)").bitcast(I32))
+
+        load_table(0)
         load_w4(0)
-        tab_w = keep.tile([P, PASSES, T], I32, name="tab_w", tag="tab_w", align_bytes=64)
-        nc.sync.dma_start(tab_w[:], tab_words.rearrange("a p t i -> p a (t i)").bitcast(I32))
         nc.sync.dma_start(idx2[:], offs2)
         nc.sync.dma_start(idx3[:], offs3)
-        load_wgs(0)
+        load_table(1)
 
-        v_sc = keep.tile([P, S], U8, name="v_sc", tag="v_sc", align_bytes=64)
+        v_sc = head.tile([P, S], U8, name="v_sc", offset=3 * 1024 + 512)
+        both_sc = keep.tile([32, S + H], U8, name="both_sc", tag="both_sc", align_bytes=64)
         nc.vector.tensor_copy(v_sc[:], tab_sc[:].indirect(idx[:]))
+        nc.vector.tensor_copy(
+            both_sc[:, S:].bitcast(I32).rearrange("p (b t x) -> p b x t", b=PASSES, t=PACK),
+            w4s_raw[:].bitcast(I32).rearrange("p (b x t) -> p b x t", b=PASSES, t=PACK),
+        )
+        nc.vector.tensor_copy(both_sc[:, :S].bitcast(I32), v_sc[0:32, :].bitcast(I32))
         for q in range(QUADRANTS):
-            nc.scalar.dma_start(
-                v_plane[32 * q : 32 * q + 4, :, :].bitcast(I32), v_sc[8 * q : 8 * q + 8, :].bitcast(I32)
+            nc.sync.dma_start(
+                planes[32 * q : 32 * q + 4, :, :].bitcast(I32), both_sc[8 * q : 8 * q + 8, :].bitcast(I32)
             )
         load_page(0)
-        v_w = {}
+        load_wgs(0)
+        v_w = [keep.tile([P, S], U32, name="v_w%d" % a, align_bytes=64) for a in range(PASSES)]
 
-        def gather_words(a, c, tag):
-            v_w[a, c] = keep.tile([P, BANK], U32, name="v_w%d%d" % (a, c), tag=tag, align_bytes=64)
-            nc.vector.tensor_copy(
-                v_w[a, c][:], tab_w[:, a, :].bitcast(U32).indirect(entries(idx, BANK * c, BANK * (c + 1)))
-            )
+        def gather_words(a, lo, hi):
+            nc.vector.tensor_copy(v_w[a][:, lo:hi], tab_w[a][:].bitcast(U32).indirect(entries(idx, lo, hi)))
 
         w4_w = [keep.tile([P, PASSES, PACK, 2 * P], U8, name="w4_w%d" % b, align_bytes=64) for b in range(PASSES)]
-        w4_s = keep.tile([P, PASSES, PASSES, PACK, P], U8, name="w4_s", align_bytes=64)
 
         def order_w4_words(b):
             nc.vector.tensor_copy(
@@ -119,22 +133,17 @@ def tile_list_place_field_atlas_kernel(
                 w4_raw[b][:].rearrange("p a (x t e) -> p a x t e", t=PACK, e=2),
             )
 
+        gather_words(0, 0, S)
         order_w4_words(0)
-        load_wgs(2)
-        gather_words(0, 0, "v_w00")
-        gather_words(1, 0, "v_w10")
-        nc.vector.tensor_copy(
-            w4_s[:].bitcast(I32).rearrange("p a b t x -> p (a b) x t"),
-            w4s_raw[:].bitcast(I32).rearrange("p a (b x t) -> p (a b) x t", b=PASSES, t=PACK),
-        )
-        gather_words(0, 1, "w4s_raw")
-        gather_words(1, 1, "v_w11")
+        gather_words(1, 0, BANK)
+        gather_words(1, BANK, S)
         load_wgs(1)
+        load_wgs(2)
 
         consts = keep.tile([P, PASSES, 2 * PACK], F32, name="consts")
 
         def make_consts():
-            rows = keep.tile([P, PASSES, P], F32, name="rows", tag="v_sc", align_bytes=64)
+            rows = keep.tile([P, PASSES, P], F32, name="rows", tag="both_sc", align_bytes=64)
             ident = keep.tile([P, P], F32, name="ident")
             nc.gpsimd.memset(rows[:], 0.0)
             make_identity(nc, ident[:])
@@ -158,9 +167,9 @@ def tile_list_place_field_atlas_kernel(
                     nc.tensor.matmul_mx(
                         out=acc[:],
                         lhsT=w4_w[b][:, a, t, :].bitcast(FP4X4),
-                        lhsT_scale=w4_s[:, a, b, t, :],
-                        rhs=v_w[a, c][:].bitcast(FP8X4),
-                        rhs_scale=v_plane[:, a, BANK * c : BANK * (c + 1)],
+                        lhsT_scale=planes[:, a, S + P * s : S + P * (s + 1)],
+                        rhs=v_w[a][:, BANK * c : BANK * (c + 1)].bitcast(FP8X4),
+                        rhs_scale=planes[:, a, BANK * c : BANK * (c + 1)],
                         start=(a == 0),
                         stop=(a == PASSES - 1),
                     )
@@ -189,54 +198,58 @@ def tile_list_place_field_atlas_kernel(
             wd_woven[b] = keep.tile([P, N, PACK], BF16, name="wd_woven%d" % b, align_bytes=64)
             nc.scalar.copy(wd_woven[b][:], raw[:].rearrange("p t n -> p n t"))
 
-        def quantise_wd(b, tag):
-            wd_q[b] = keep.tile([P, N], U32, name="wd_q%d" % b, tag=tag, align_bytes=64)
+        def quantise_wd(b, j, tag):
+            cols = slice(2 * P * j, 2 * P * (j + 1))
+            wd_q[b, j] = keep.tile([P, 2 * P], U32, name="wd_q%d%d" % (b, j), tag=tag, align_bytes=64)
             nc.vector.quantize_mx(
-                out=wd_q[b][:].bitcast(FP8X4), scales=wd_s[b][:], in_=wd_woven[b][:].rearrange("p n t -> p (n t)")
+                out=wd_q[b, j][:].bitcast(FP8X4),
+                scales=wd_s[b][:, cols],
+                in_=wd_woven[b][:, cols, :].rearrange("p n t -> p (n t)"),
             )
 
-        z_rows = [keep.tile([P, PACK, M], BF16, name="z_rows%d" % b) for b in range(PASSES)]
-        z_woven = [keep.tile([P, M, PACK], BF16, name="z_woven%d" % b, align_bytes=64) for b in range(PASSES)]
-        z_q = [keep.tile([P, M], U32, name="z_q%d" % b, align_bytes=64) for b in range(PASSES)]
+        z_rows = [keep.tile([P, PACK, M], BF16, name="z_rows0"), tail.tile([P, 2, M], BF16, name="z_rows1", offset=0)]
+        z_woven = keep.tile([P, M, PACK], BF16, name="z_woven", align_bytes=64)
+        woven = [keep.tile([P, CHUNK, PACK], BF16, name="woven%d" % k, align_bytes=64) for k in range(CHUNKS)]
+        spans = [(CHUNK * k, CHUNK * (k + 1)) for k in range(CHUNKS)]
+        z_q0 = keep.tile([P, M], U32, name="z_q0", align_bytes=64)
+        z_q = {(0, k): z_q0[:, CHUNK * k : CHUNK * (k + 1)] for k in range(CHUNKS)}
         z_s = [keep.tile([P, M], U8, name="z_s%d" % b, align_bytes=64) for b in range(PASSES)]
         res = {}
 
         def scatter(s, values, lo, hi):
             nc.vector.tensor_tensor(pages[s][:].indirect(entries(idx2, lo, hi)), values, wg[s % PACK][:, lo:hi], MULT)
 
-        def tune(s, x, spans):
+        def tune(s, x):
             b, t = divmod(s, PACK)
-            for lo, hi in spans:
-                nc.vector.tensor_copy(x[:, lo:hi], pages[s][:].indirect(entries(idx3, lo, hi)))
-                nc.scalar.activation(x[:, lo:hi], x[:, lo:hi], ACT.Square, bias=consts[:, b, t : t + 1], scale=-1.0)
-            for lo, hi in spans:
-                nc.scalar.activation(x[:, lo:hi], x[:, lo:hi], ACT.Exp, scale=-0.25)
-            for lo, hi in spans:
-                nc.scalar.activation(
-                    z_rows[b][:, t, lo:hi], x[:, lo:hi], ACT.Copy, scale=consts[:, b, PACK + t : PACK + t + 1]
-                )
-
-        def weave_z(copy, b, slots, lo, hi):
-            copy(z_woven[b][:, lo:hi, slots], z_rows[b][:, slots, lo:hi].rearrange("p t m -> p m t"))
-
-        def quantise_z(b, lo, hi):
-            nc.vector.quantize_mx(
-                out=z_q[b][:, lo:hi].bitcast(FP8X4),
-                scales=z_s[b][:, lo:hi],
-                in_=z_woven[b][:, lo:hi, :].rearrange("p m t -> p (m t)"),
-            )
+            gain_t = consts[:, b, PACK + t : PACK + t + 1]
+            nc.vector.tensor_copy(x[:], pages[s][:].indirect(idx3[:]))
+            y = x
+            if s == LAST - 1:
+                y = tail.tile([P, M], F32, name="y", offset=0)
+            nc.scalar.activation(y[:], x[:], ACT.Square, bias=consts[:, b, t : t + 1], scale=-1.0)
+            nc.scalar.activation(y[:], y[:], ACT.Exp, scale=-0.25)
+            if s == LAST - 1:
+                for k in range(CHUNKS):
+                    nc.scalar.activation(woven[k][:, :, t], y[:, slice(*spans[k])], ACT.Copy, scale=gain_t)
+            else:
+                nc.scalar.activation(z_rows[b][:, t, :], y[:], ACT.Copy, scale=gain_t)
 
         def out_pass(k, nt, b):
-            cols = slice(CHUNK * k, CHUNK * (k + 1))
             nc.tensor.matmul_mx(
                 out=res[k, nt // 2][:, nt % 2, :],
-                lhsT=wd_q[b][:, P * nt : P * (nt + 1)].bitcast(FP8X4),
+                lhsT=wd_q[b, nt // 2][:, P * (nt % 2) : P * (nt % 2 + 1)].bitcast(FP8X4),
                 lhsT_scale=wd_s[b][:, P * nt : P * (nt + 1)],
-                rhs=z_q[b][:, cols].bitcast(FP8X4),
-                rhs_scale=z_s[b][:, cols],
-                start=(b == 0),
-                stop=(b == PASSES - 1),
+                rhs=z_q[b, k].bitcast(FP8X4),
+                rhs_scale=z_s[b][:, CHUNK * k : CHUNK * (k + 1)],
+                start=(b == 0 and nt % 2 == 0),
+                stop=(b == PASSES - 1 and nt % 2 == 1),
             )
+
+        def open_sums(j):
+            for k in range(CHUNKS):
+                res[k, j] = psum.tile([P, 2, CHUNK], F32, name="res", tag="bank%d" % (2 * k + j))
+                out_pass(k, 2 * j, 0)
+                out_pass(k, 2 * j + 1, 0)
 
         def after_scatter(s):
             if s == 1:
@@ -244,15 +257,21 @@ def tile_list_place_field_atlas_kernel(
             if s in (2, 3):
                 weave_wd(s - 2)
             if s == 3:
-                quantise_wd(1, "wd_q1")
+                quantise_wd(0, 0, "wd_q00")
+                quantise_wd(1, 0, "wd_q10")
+                quantise_wd(1, 1, "wd_q11")
 
         def after_tune(s):
             if s == PACK - 1:
                 for lo in range(0, M, BANK):
-                    weave_z(nc.scalar.copy, 0, slice(0, PACK), lo, lo + BANK)
-                quantise_z(0, 0, M)
+                    nc.scalar.copy(z_woven[:, lo : lo + BANK, :], z_rows[0][:, :, lo : lo + BANK].rearrange("p t m -> p m t"))
+                nc.vector.quantize_mx(
+                    out=z_q0[:].bitcast(FP8X4), scales=z_s[0][:], in_=z_woven[:].rearrange("p m t -> p (m t)")
+                )
+                open_sums(0)
             if s == PACK + 1:
-                weave_z(nc.scalar.copy, 1, slice(0, 2), 0, M)
+                for k in range(CHUNKS):
+                    nc.scalar.copy(woven[k][:, :, 0:2], z_rows[1][:, :, slice(*spans[k])].rearrange("p t m -> p m t"))
 
         for s in range(LAST):
             if s == 0:
@@ -266,35 +285,68 @@ def tile_list_place_field_atlas_kernel(
             else:
                 scatter(s, h[s][:], 0, S)
             after_scatter(s)
-            x = keep.tile([P, M], F32, name="x%d" % s, align_bytes=64)
-            tune(s, x, [(0, M)])
+            x = keep.tile([P, M], F32, name="x%d" % s, tag="x%d" % s, align_bytes=64)
+            tune(s, x)
             if s + 2 < SLICES:
                 load_page(s + 2)
             after_tune(s)
 
         scatter(LAST, h[LAST][:], 0, S)
-        x = keep.tile([P, M], F32, name="x%d" % LAST, align_bytes=64)
-        spans = [(CHUNK * k, CHUNK * (k + 1)) for k in range(CHUNKS)]
-        tune(LAST, x, spans[:2])
-        quantise_wd(0, "h%d" % LAST)
-        for k in range(CHUNKS):
-            for j in range(2):
-                res[k, j] = psum.tile([P, 2, CHUNK], F32, name="res", tag="bank%d" % (2 * k + j))
-                out_pass(k, 2 * j, 0)
-        tune(LAST, x, spans[2:])
-        for k in range(CHUNKS):
-            weave_z(nc.vector.tensor_copy, 1, slice(2, PACK), *spans[k])
-            if k > 0:
-                quantise_z(1, *spans[k - 1])
-        quantise_z(1, *spans[-1])
+        curve = keep.tile([P, M], F32, name="curve")
+        x_chunk = {}
+        unit = 4 * CHUNK
+
+        def gather_chunk(k):
+            if k < CHUNKS - 1:
+                x_chunk[k] = keep.tile([P, CHUNK], F32, name="x_chunk%d" % k)
+            else:
+                x_chunk[k] = tail.tile([P, CHUNK], F32, name="x_chunk%d" % k, offset=0)
+            nc.vector.tensor_copy(x_chunk[k][:], pages[LAST][:].indirect(entries(idx3, *spans[k])))
+
+        def curve_chunk(k):
+            first, end = ((1, 2), (0, 2), (1, 4), (1, 2))[k]
+            held = tail.tile([P, end - first, CHUNK], F32, name="squares%d" % k, offset=unit * first)
+            squares = held[:, 1 - first, :]
+            nc.scalar.activation(squares, x_chunk[k][:], ACT.Square, bias=consts[:, 1, PACK - 1 : PACK], scale=-1.0)
+            nc.scalar.activation(curve[:, slice(*spans[k])], squares, ACT.Exp, scale=-0.25)
+
+        def gain_chunk(k):
+            cols = slice(*spans[k])
+            gain_t = consts[:, 1, 2 * PACK - 1 : 2 * PACK]
+            nc.vector.tensor_scalar(woven[k][:, :, PACK - 1], curve[:, cols], gain_t, None, MULT)
+
+        def quantise_chunk(k):
+            z_q[1, k] = keep.tile([P, CHUNK], U32, name="z_q1%d" % k, align_bytes=64)[:]
+            nc.vector.quantize_mx(
+                out=z_q[1, k].bitcast(FP8X4),
+                scales=z_s[1][:, slice(*spans[k])],
+                in_=woven[k][:].rearrange("p m t -> p (m t)"),
+            )
+
+        quantise_wd(0, 1, "h%d" % LAST)
+        open_sums(1)
+        for k in range(CHUNKS - 1):
+            gather_chunk(k)
+        curve_chunk(0)
+        gain_chunk(0)
+        quantise_chunk(0)
+        curve_chunk(1)
+        gather_chunk(3)
+        curve_chunk(2)
+        curve_chunk(3)
+        for k in range(1, CHUNKS):
+            gain_chunk(k)
+            quantise_chunk(k)
         out_v = out.rearrange("(j i p) m -> j p i m", j=2, i=2)
         for k in range(CHUNKS):
             for j in range(2):
                 out_pass(k, 2 * j, 1)
-                out_pass(k, 2 * j + 1, 0)
                 out_pass(k, 2 * j + 1, 1)
-                staged = keep.tile([P, 2, CHUNK], F32, name="staged%d%d" % (k, j))
-                if k >= CHUNKS - 2 and j == 1:
+                if k == 0:
+                    staged = tail.tile([P, 2, CHUNK], F32, name="staged%d%d" % (k, j), offset=unit * 2 * (1 - j))
+                else:
+                    staged = keep.tile([P, 2, CHUNK], F32, name="staged%d%d" % (k, j))
+                if k >= 2 and j == 1:
                     nc.vector.tensor_copy(staged[:], res[k, j][:])
                 else:
                     nc.scalar.copy(staged[:], res[k, j][:])

@@ -29,6 +29,9 @@ BANKS = 8
 PER_COLUMN = 16
 CHUNK = 256
 CHUNKS = M // CHUNK
+ROW = 4 * M
+PAD = 32
+W4_BYTES = 4 * BANK
 W4_WORDS = BANK // 2
 
 
@@ -40,6 +43,8 @@ def tile_list_place_field_atlas_kernel(
         lists = ctx.enter_context(tc.tile_pool(name="lists", bufs=1))
         keep = ctx.enter_context(tc.tile_pool(name="keep", bufs=1))
         head = ctx.enter_context(tc.tile_pool(name="head", bufs=1))
+        early = ctx.enter_context(tc.tile_pool(name="early", bufs=1))
+        late = ctx.enter_context(tc.tile_pool(name="late", bufs=1))
         tail = ctx.enter_context(tc.tile_pool(name="tail", bufs=1))
         psum = ctx.enter_context(tc.psum_pool(name="psum", bufs=1))
 
@@ -64,8 +69,8 @@ def tile_list_place_field_atlas_kernel(
         w4_src = w4_words.rearrange("a p c -> p a c").bitcast(I32)
 
         def load_w4(b):
-            w4_raw[b] = keep.tile(
-                [P, PASSES, W4_WORDS], I32, name="w4_raw%d" % b, tag=("w4_raw", "h0")[b], align_bytes=64
+            w4_raw[b] = early.tile(
+                [P, PASSES, W4_WORDS], I32, name="w4_raw%d" % b, offset=(W4_BYTES - 64) * (1 - b), align_bytes=64
             )
             nc.sync.dma_start(w4_raw[b][:], w4_src[:, :, W4_WORDS * b : W4_WORDS * (b + 1)])
 
@@ -74,7 +79,9 @@ def tile_list_place_field_atlas_kernel(
 
         def load_page(s):
             b, t = divmod(s, PACK)
-            if s % 2 == 0:
+            if s == LAST:
+                pages[s] = late.tile([P, T2], F32, name="page%d" % s, offset=0)
+            elif s % 2 == 0:
                 pages[s] = head.tile([P, T2], F32, name="page%d" % s, tag="page0", offset=4 * 1024)
             else:
                 pages[s] = keep.tile([P, T2], F32, name="page%d" % s, tag="page1", align_bytes=64)
@@ -137,6 +144,7 @@ def tile_list_place_field_atlas_kernel(
         order_w4_words(0)
         gather_words(1, 0, BANK)
         gather_words(1, BANK, S)
+        load_w4(1)
         load_wgs(1)
         load_wgs(2)
 
@@ -144,7 +152,7 @@ def tile_list_place_field_atlas_kernel(
 
         def make_consts():
             rows = keep.tile([P, PASSES, P], F32, name="rows", tag="both_sc", align_bytes=64)
-            ident = keep.tile([P, P], F32, name="ident")
+            ident = early.tile([P, P], F32, name="ident", offset=2 * (W4_BYTES - 64), align_bytes=64)
             nc.gpsimd.memset(rows[:], 0.0)
             make_identity(nc, ident[:])
             for i, vec in enumerate((pref, gain)):
@@ -207,7 +215,11 @@ def tile_list_place_field_atlas_kernel(
                 in_=wd_woven[b][:, cols, :].rearrange("p n t -> p (n t)"),
             )
 
-        z_rows = [keep.tile([P, PACK, M], BF16, name="z_rows0"), tail.tile([P, 2, M], BF16, name="z_rows1", offset=0)]
+        z_held = late.tile([P, PACK * M + PAD], BF16, name="z_rows0", offset=0)
+        z_rows = [
+            z_held[:, : PACK * M].rearrange("p (t m) -> p t m", t=PACK),
+            tail.tile([P, 2, M], BF16, name="z_rows1", offset=0),
+        ]
         z_woven = keep.tile([P, M, PACK], BF16, name="z_woven", align_bytes=64)
         woven = [keep.tile([P, CHUNK, PACK], BF16, name="woven%d" % k, align_bytes=64) for k in range(CHUNKS)]
         spans = [(CHUNK * k, CHUNK * (k + 1)) for k in range(CHUNKS)]
@@ -260,15 +272,16 @@ def tile_list_place_field_atlas_kernel(
                 quantise_wd(0, 0, "wd_q00")
                 quantise_wd(1, 0, "wd_q10")
                 quantise_wd(1, 1, "wd_q11")
+            if s == LAST - 1:
+                nc.vector.quantize_mx(
+                    out=z_q0[:].bitcast(FP8X4), scales=z_s[0][:], in_=z_woven[:].rearrange("p m t -> p (m t)")
+                )
+                open_sums(0)
 
         def after_tune(s):
             if s == PACK - 1:
                 for lo in range(0, M, BANK):
                     nc.scalar.copy(z_woven[:, lo : lo + BANK, :], z_rows[0][:, :, lo : lo + BANK].rearrange("p t m -> p m t"))
-                nc.vector.quantize_mx(
-                    out=z_q0[:].bitcast(FP8X4), scales=z_s[0][:], in_=z_woven[:].rearrange("p m t -> p (m t)")
-                )
-                open_sums(0)
             if s == PACK + 1:
                 for k in range(CHUNKS):
                     nc.scalar.copy(woven[k][:, :, 0:2], z_rows[1][:, :, slice(*spans[k])].rearrange("p t m -> p m t"))
@@ -277,15 +290,17 @@ def tile_list_place_field_atlas_kernel(
             if s == 0:
                 scatter(s, h[0, 0][:], 0, BANK)
                 load_page(1)
-                scatter(s, h[0, 1][:], BANK, S)
-                load_w4(1)
                 order_w4_words(1)
+                scatter(s, h[0, 1][:], BANK, S)
                 for later in range(PACK, SLICES):
                     project(later)
             else:
                 scatter(s, h[s][:], 0, S)
             after_scatter(s)
-            x = keep.tile([P, M], F32, name="x%d" % s, tag="x%d" % s, align_bytes=64)
+            if s == LAST - 1:
+                x = late.tile([P, M], F32, name="x%d" % s, offset=2 * ROW)
+            else:
+                x = keep.tile([P, M], F32, name="x%d" % s, align_bytes=64)
             tune(s, x)
             if s + 2 < SLICES:
                 load_page(s + 2)

@@ -31,7 +31,6 @@ CHUNK = 256
 CHUNKS = M // CHUNK
 ROW = 4 * M
 PAD = 32
-W4_BYTES = 4 * BANK
 W4_WORDS = BANK // 2
 
 
@@ -43,7 +42,6 @@ def tile_list_place_field_atlas_kernel(
         lists = ctx.enter_context(tc.tile_pool(name="lists", bufs=1))
         keep = ctx.enter_context(tc.tile_pool(name="keep", bufs=1))
         head = ctx.enter_context(tc.tile_pool(name="head", bufs=1))
-        early = ctx.enter_context(tc.tile_pool(name="early", bufs=1))
         late = ctx.enter_context(tc.tile_pool(name="late", bufs=1))
         tail = ctx.enter_context(tc.tile_pool(name="tail", bufs=1))
         psum = ctx.enter_context(tc.psum_pool(name="psum", bufs=1))
@@ -69,9 +67,10 @@ def tile_list_place_field_atlas_kernel(
         w4_src = w4_words.rearrange("a p c -> p a c").bitcast(I32)
 
         def load_w4(b):
-            w4_raw[b] = early.tile(
-                [P, PASSES, W4_WORDS], I32, name="w4_raw%d" % b, offset=(W4_BYTES - 64) * (1 - b), align_bytes=64
-            )
+            if b == 0:
+                w4_raw[b] = keep.tile([P, PASSES, W4_WORDS], I32, name="w4_raw0", tag="w4_raw0")
+            else:
+                w4_raw[b] = head.tile([P, PASSES, W4_WORDS], I32, name="w4_raw1", offset=5 * ROW)
             nc.sync.dma_start(w4_raw[b][:], w4_src[:, :, W4_WORDS * b : W4_WORDS * (b + 1)])
 
         page_src = page0.rearrange("(b x t y) c -> b t x y c", b=PASSES, t=PACK, y=RUN)
@@ -84,7 +83,7 @@ def tile_list_place_field_atlas_kernel(
             elif s % 2 == 0:
                 pages[s] = head.tile([P, T2], F32, name="page%d" % s, tag="page0", offset=4 * 1024)
             else:
-                pages[s] = keep.tile([P, T2], F32, name="page%d" % s, tag="page1", align_bytes=64)
+                pages[s] = head.tile([P, T2], F32, name="page%d" % s, tag="page1", offset=3 * ROW)
             nc.sync.dma_start(pages[s][:], page_src[b, t])
 
         wgs_src = wgs.rearrange("(x t y) s -> t x y s", t=PACK, y=RUN)
@@ -144,7 +143,6 @@ def tile_list_place_field_atlas_kernel(
         order_w4_words(0)
         gather_words(1, 0, BANK)
         gather_words(1, BANK, S)
-        load_w4(1)
         load_wgs(1)
         load_wgs(2)
 
@@ -152,7 +150,7 @@ def tile_list_place_field_atlas_kernel(
 
         def make_consts():
             rows = keep.tile([P, PASSES, P], F32, name="rows", tag="both_sc", align_bytes=64)
-            ident = early.tile([P, P], F32, name="ident", offset=2 * (W4_BYTES - 64), align_bytes=64)
+            ident = keep.tile([P, P], F32, name="ident", tag="w4_raw0")
             nc.gpsimd.memset(rows[:], 0.0)
             make_identity(nc, ident[:])
             for i, vec in enumerate((pref, gain)):
@@ -182,7 +180,10 @@ def tile_list_place_field_atlas_kernel(
                         stop=(a == PASSES - 1),
                     )
                 if s == 0:
-                    h[s, c] = keep.tile([P, BANK], F32, name="h0%d" % c, tag=("page1", "h0")[c], align_bytes=64)
+                    if c == 0:
+                        h[s, c] = head.tile([P, BANK], F32, name="h00", offset=5 * ROW - ROW // 4)
+                    else:
+                        h[s, c] = keep.tile([P, BANK], F32, name="h01", align_bytes=64)
                     nc.scalar.copy(h[s, c][:], acc[:])
                 else:
                     if c == 0:
@@ -290,8 +291,9 @@ def tile_list_place_field_atlas_kernel(
             if s == 0:
                 scatter(s, h[0, 0][:], 0, BANK)
                 load_page(1)
-                order_w4_words(1)
+                load_w4(1)
                 scatter(s, h[0, 1][:], BANK, S)
+                order_w4_words(1)
                 for later in range(PACK, SLICES):
                     project(later)
             else:

@@ -90,15 +90,11 @@ def tile_list_place_field_atlas_kernel(
         wg = {}
 
         def load_wgs(t):
-            if t == 0:
-                wg[t] = head.tile([P, S], F32, name="wg0", offset=0)
-                spans = [(0, BANK), (BANK, S)]
-            else:
-                wg[t] = keep.tile([P, S], F32, name="wg%d" % t, tag=("tab_w1", "tab_w0", "h1")[t - 1], align_bytes=64)
-                spans = [(0, S)]
-            for lo, hi in spans:
-                for q in range(QUADRANTS):
-                    nc.sync.dma_start(wg[t][32 * q : 32 * (q + 1), lo:hi], wgs_src[t][:, :, lo:hi])
+            tag = ("wg0", "tab_w1", "tab_w0", "h1")[t]
+            wg[t] = keep.tile([P, S], F32, name="wg%d" % t, tag=tag, align_bytes=64)
+            queue = nc.gpsimd if t == 0 else nc.sync
+            for q in range(QUADRANTS):
+                queue.dma_start(wg[t][32 * q : 32 * (q + 1), :], wgs_src[t])
 
         tab_w = {}
 
@@ -106,6 +102,7 @@ def tile_list_place_field_atlas_kernel(
             tab_w[a] = keep.tile([P, T], I32, name="tab_w%d" % a, tag="tab_w%d" % a, align_bytes=64)
             nc.sync.dma_start(tab_w[a][:], tab_words[a].rearrange("p t i -> p (t i)").bitcast(I32))
 
+        load_wgs(0)
         load_table(0)
         load_w4(0)
         nc.sync.dma_start(idx2[:], offs2)
@@ -125,7 +122,6 @@ def tile_list_place_field_atlas_kernel(
                 planes[32 * q : 32 * q + 4, :, :].bitcast(I32), both_sc[8 * q : 8 * q + 8, :].bitcast(I32)
             )
         load_page(0)
-        load_wgs(0)
         v_w = [keep.tile([P, S], U32, name="v_w%d" % a, align_bytes=64) for a in range(PASSES)]
 
         def gather_words(a, lo, hi):

@@ -30,7 +30,8 @@ PER_COLUMN = 16
 CHUNK = 256
 CHUNKS = M // CHUNK
 ROW = 4 * M
-PAD = 32
+LEAD = 256
+BULK = T2 - BANK
 W4_WORDS = BANK // 2
 
 
@@ -41,7 +42,6 @@ def tile_list_place_field_atlas_kernel(
     with ExitStack() as ctx:
         lists = ctx.enter_context(tc.tile_pool(name="lists", bufs=1))
         keep = ctx.enter_context(tc.tile_pool(name="keep", bufs=1))
-        head = ctx.enter_context(tc.tile_pool(name="head", bufs=1))
         late = ctx.enter_context(tc.tile_pool(name="late", bufs=1))
         tail = ctx.enter_context(tc.tile_pool(name="tail", bufs=1))
         psum = ctx.enter_context(tc.psum_pool(name="psum", bufs=1))
@@ -67,34 +67,23 @@ def tile_list_place_field_atlas_kernel(
         w4_src = w4_words.rearrange("a p c -> p a c").bitcast(I32)
 
         def load_w4(b):
-            if b == 0:
-                w4_raw[b] = keep.tile([P, PASSES, W4_WORDS], I32, name="w4_raw0", tag="w4_raw0")
-            else:
-                w4_raw[b] = head.tile([P, PASSES, W4_WORDS], I32, name="w4_raw1", offset=5 * ROW)
+            w4_raw[b] = keep.tile([P, PASSES, W4_WORDS], I32, name="w4_raw%d" % b, tag="w4_raw%d" % b)
             nc.sync.dma_start(w4_raw[b][:], w4_src[:, :, W4_WORDS * b : W4_WORDS * (b + 1)])
 
         page_src = page0.rearrange("(b x t y) c -> b t x y c", b=PASSES, t=PACK, y=RUN)
-        pages = {}
+        pages = [keep.tile([P, T2], F32, name="page%d" % s, tag="page%d" % s, align_bytes=64) for s in range(SLICES)]
 
-        def load_page(s):
+        def load_page(s, lo=0, hi=T2):
             b, t = divmod(s, PACK)
-            if s == LAST:
-                pages[s] = late.tile([P, T2], F32, name="page%d" % s, offset=0)
-            elif s % 2 == 0:
-                pages[s] = head.tile([P, T2], F32, name="page%d" % s, tag="page0", offset=4 * 1024)
-            else:
-                pages[s] = head.tile([P, T2], F32, name="page%d" % s, tag="page1", offset=3 * ROW)
-            nc.sync.dma_start(pages[s][:], page_src[b, t])
+            nc.sync.dma_start(pages[s][:, lo:hi], page_src[b, t][:, :, lo:hi])
 
         wgs_src = wgs.rearrange("(x t y) s -> t x y s", t=PACK, y=RUN)
-        wg = {}
+        wg = [keep.tile([P, S], F32, name="wg%d" % t, align_bytes=64) for t in range(PACK)]
 
-        def load_wgs(t):
-            tag = ("wg0", "tab_w1", "tab_w0", "h1")[t]
-            wg[t] = keep.tile([P, S], F32, name="wg%d" % t, tag=tag, align_bytes=64)
+        def load_wgs(t, lo, hi, quadrants):
             queue = nc.gpsimd if t == 0 else nc.sync
-            for q in range(QUADRANTS):
-                queue.dma_start(wg[t][32 * q : 32 * (q + 1), :], wgs_src[t])
+            for q in quadrants:
+                queue.dma_start(wg[t][32 * q : 32 * (q + 1), lo:hi], wgs_src[t][:, :, lo:hi])
 
         tab_w = {}
 
@@ -102,14 +91,13 @@ def tile_list_place_field_atlas_kernel(
             tab_w[a] = keep.tile([P, T], I32, name="tab_w%d" % a, tag="tab_w%d" % a, align_bytes=64)
             nc.sync.dma_start(tab_w[a][:], tab_words[a].rearrange("p t i -> p (t i)").bitcast(I32))
 
-        load_wgs(0)
+        load_wgs(0, 0, S, range(QUADRANTS))
         load_table(0)
         load_w4(0)
         nc.sync.dma_start(idx2[:], offs2)
-        nc.sync.dma_start(idx3[:], offs3)
         load_table(1)
 
-        v_sc = head.tile([P, S], U8, name="v_sc", offset=3 * 1024 + 512)
+        v_sc = keep.tile([P, S], U8, name="v_sc", align_bytes=64)
         both_sc = keep.tile([32, S + H], U8, name="both_sc", tag="both_sc", align_bytes=64)
         nc.vector.tensor_copy(v_sc[:], tab_sc[:].indirect(idx[:]))
         nc.vector.tensor_copy(
@@ -121,7 +109,6 @@ def tile_list_place_field_atlas_kernel(
             nc.sync.dma_start(
                 planes[32 * q : 32 * q + 4, :, :].bitcast(I32), both_sc[8 * q : 8 * q + 8, :].bitcast(I32)
             )
-        load_page(0)
         v_w = [keep.tile([P, S], U32, name="v_w%d" % a, align_bytes=64) for a in range(PASSES)]
 
         def gather_words(a, lo, hi):
@@ -139,35 +126,56 @@ def tile_list_place_field_atlas_kernel(
         order_w4_words(0)
         gather_words(1, 0, BANK)
         gather_words(1, BANK, S)
-        load_wgs(1)
-        load_wgs(2)
+
+        wd_src = wd.rearrange("(b x t y) n -> b t x y n", b=PASSES, t=PACK, y=RUN)
+        wd_raw = [keep.tile([P, PACK, N], F32, name="wd_raw%d" % b, tag="tab_w%d" % b, align_bytes=64) for b in range(PASSES)]
+        rows = keep.tile([P, PASSES, P], F32, name="rows", tag="both_sc", align_bytes=64)
+        nc.gpsimd.memset(rows[:], 0.0)
+        load_page(0)
+        load_w4(1)
+        load_page(1)
+        load_wgs(1, 0, LEAD, range(QUADRANTS))
+        nc.sync.dma_start(idx3[:], offs3)
+        for i, vec in enumerate((pref, gain)):
+            nc.sync.dma_start(
+                rows[PACK * i : PACK * (i + 1), :, :].rearrange("t b (x y) -> t (b x) y", y=RUN),
+                vec.rearrange("(bx t y) -> t bx y", t=PACK, y=RUN),
+            )
+        for s in (1, 2):
+            load_page(s + 1)
+            load_wgs(s + 1, 0, LEAD, range(QUADRANTS - 1))
+            load_wgs(s, LEAD, S, range(QUADRANTS))
+            load_wgs(s + 1, 0, LEAD, [QUADRANTS - 1])
+        for b in range(PASSES):
+            for t in range(PACK):
+                nc.sync.dma_start(wd_raw[b][:, t, :], wd_src[b, t])
+        load_page(4, 0, BULK)
+        load_page(5, 0, BULK)
+        load_wgs(3, LEAD, S, range(QUADRANTS))
+        load_page(4, BULK, T2)
+        load_page(5, BULK, T2)
+        load_page(6)
+        load_page(7)
 
         consts = keep.tile([P, PASSES, 2 * PACK], F32, name="consts")
 
         def make_consts():
-            rows = keep.tile([P, PASSES, P], F32, name="rows", tag="both_sc", align_bytes=64)
             ident = keep.tile([P, P], F32, name="ident", tag="w4_raw0")
-            nc.gpsimd.memset(rows[:], 0.0)
             make_identity(nc, ident[:])
-            for i, vec in enumerate((pref, gain)):
-                nc.sync.dma_start(
-                    rows[PACK * i : PACK * (i + 1), :, :].rearrange("t b (x y) -> t (b x) y", y=RUN),
-                    vec.rearrange("(bx t y) -> t bx y", t=PACK, y=RUN),
-                )
             turned = psum.tile([P, PASSES, P], F32, name="turned", tag="bank3")
             for b in range(PASSES):
                 nc.tensor.transpose(turned[:, b, :], rows[:, b, :], ident[:])
             nc.scalar.copy(consts[:], turned[:, :, 0 : 2 * PACK])
 
-        h = {}
+        h, acc = {}, {}
 
         def project(s):
             b, t = divmod(s, PACK)
             for c in range(2):
-                acc = psum.tile([P, BANK], F32, name="acc", tag="bank%d" % ((2 * s + c) % BANKS))
+                acc[s, c] = psum.tile([P, BANK], F32, name="acc", tag="bank%d" % ((2 * s + c) % BANKS))
                 for a in range(PASSES):
                     nc.tensor.matmul_mx(
-                        out=acc[:],
+                        out=acc[s, c][:],
                         lhsT=w4_w[b][:, a, t, :].bitcast(FP4X4),
                         lhsT_scale=planes[:, a, S + P * s : S + P * (s + 1)],
                         rhs=v_w[a][:, BANK * c : BANK * (c + 1)].bitcast(FP8X4),
@@ -176,15 +184,12 @@ def tile_list_place_field_atlas_kernel(
                         stop=(a == PASSES - 1),
                     )
                 if s == 0:
-                    if c == 0:
-                        h[s, c] = head.tile([P, BANK], F32, name="h00", offset=5 * ROW - ROW // 4)
-                    else:
-                        h[s, c] = keep.tile([P, BANK], F32, name="h01", align_bytes=64)
-                    nc.scalar.copy(h[s, c][:], acc[:])
-                else:
+                    h[s, c] = keep.tile([P, BANK], F32, name="h0%d" % c, tag="h0%d" % c, align_bytes=64)
+                    nc.scalar.copy(h[s, c][:], acc[s, c][:])
+                elif s < LAST - 1:
                     if c == 0:
                         h[s] = keep.tile([P, S], F32, name="h%d" % s, tag="h%d" % s, align_bytes=64)
-                    nc.scalar.copy(h[s][:, BANK * c : BANK * (c + 1)], acc[:])
+                    nc.scalar.copy(h[s][:, BANK * c : BANK * (c + 1)], acc[s, c][:])
 
         project(0)
         project(1)
@@ -192,30 +197,26 @@ def tile_list_place_field_atlas_kernel(
         project(2)
         project(3)
 
-        wd_src = wd.rearrange("(b x t y) n -> b t x y n", b=PASSES, t=PACK, y=RUN)
         wd_q, wd_woven = {}, {}
         wd_s = [keep.tile([P, N], U8, name="wd_s%d" % b, align_bytes=64) for b in range(PASSES)]
 
         def weave_wd(b):
-            raw = keep.tile([P, PACK, N], F32, name="wd_raw%d" % b, tag="h%d" % (b + 2), align_bytes=64)
-            for t in range(PACK):
-                nc.sync.dma_start(raw[:, t, :], wd_src[b, t])
             wd_woven[b] = keep.tile([P, N, PACK], BF16, name="wd_woven%d" % b, align_bytes=64)
-            nc.scalar.copy(wd_woven[b][:], raw[:].rearrange("p t n -> p n t"))
+            nc.scalar.copy(wd_woven[b][:], wd_raw[b][:].rearrange("p t n -> p n t"))
 
-        def quantise_wd(b, j, tag):
+        def quantise_wd(b, j, codes):
             cols = slice(2 * P * j, 2 * P * (j + 1))
-            wd_q[b, j] = keep.tile([P, 2 * P], U32, name="wd_q%d%d" % (b, j), tag=tag, align_bytes=64)
+            wd_q[b, j] = codes
             nc.vector.quantize_mx(
                 out=wd_q[b, j][:].bitcast(FP8X4),
                 scales=wd_s[b][:, cols],
                 in_=wd_woven[b][:, cols, :].rearrange("p n t -> p (n t)"),
             )
 
-        z_held = late.tile([P, PACK * M + PAD], BF16, name="z_rows0", offset=0)
+        z_held = late.tile([P, 6 * M], BF16, name="z_rows0", offset=0, align_bytes=64)
         z_rows = [
             z_held[:, : PACK * M].rearrange("p (t m) -> p t m", t=PACK),
-            tail.tile([P, 2, M], BF16, name="z_rows1", offset=0),
+            tail.tile([P, 2, M], BF16, name="z_rows1", offset=0, align_bytes=64),
         ]
         z_woven = keep.tile([P, M, PACK], BF16, name="z_woven", align_bytes=64)
         woven = [keep.tile([P, CHUNK, PACK], BF16, name="woven%d" % k, align_bytes=64) for k in range(CHUNKS)]
@@ -228,13 +229,18 @@ def tile_list_place_field_atlas_kernel(
         def scatter(s, values, lo, hi):
             nc.vector.tensor_tensor(pages[s][:].indirect(entries(idx2, lo, hi)), values, wg[s % PACK][:, lo:hi], MULT)
 
-        def tune(s, x):
+        def tune(s):
+            if s == PACK + 1:
+                x = late.tile([P, M], F32, name="x%d" % s, offset=2 * ROW, align_bytes=64)
+            else:
+                x = keep.tile([P, M], F32, name="x%d" % s, tag="x%d" % (s % 4 if s == 6 else s % 3), align_bytes=64)
             b, t = divmod(s, PACK)
             gain_t = consts[:, b, PACK + t : PACK + t + 1]
             nc.vector.tensor_copy(x[:], pages[s][:].indirect(idx3[:]))
-            y = x
-            if s == LAST - 1:
-                y = tail.tile([P, M], F32, name="y", offset=0)
+            if s < LAST - 1:
+                y = keep.tile([P, M], F32, name="y%d" % s, tag="y")
+            else:
+                y = tail.tile([P, M], F32, name="y", offset=0, align_bytes=64)
             nc.scalar.activation(y[:], x[:], ACT.Square, bias=consts[:, b, t : t + 1], scale=-1.0)
             nc.scalar.activation(y[:], y[:], ACT.Exp, scale=-0.25)
             if s == LAST - 1:
@@ -260,66 +266,57 @@ def tile_list_place_field_atlas_kernel(
                 out_pass(k, 2 * j, 0)
                 out_pass(k, 2 * j + 1, 0)
 
-        def after_scatter(s):
-            if s == 1:
-                load_wgs(3)
-            if s in (2, 3):
-                weave_wd(s - 2)
-            if s == 3:
-                quantise_wd(0, 0, "wd_q00")
-                quantise_wd(1, 0, "wd_q10")
-                quantise_wd(1, 1, "wd_q11")
+        def late_tile(name, words, dtype, offset):
+            return late.tile([P, words], dtype, name=name, offset=offset, align_bytes=64)
+
+        scatter(0, h[0, 0][:], 0, BANK)
+        order_w4_words(1)
+        scatter(0, h[0, 1][:], BANK, S)
+        for s in range(PACK, SLICES):
+            project(s)
+        for s in range(1, LAST):
             if s == LAST - 1:
                 nc.vector.quantize_mx(
                     out=z_q0[:].bitcast(FP8X4), scales=z_s[0][:], in_=z_woven[:].rearrange("p m t -> p (m t)")
                 )
-                open_sums(0)
-
-        def after_tune(s):
+                lead, rest = h[s, 0][:], h[s, 1][:]
+            else:
+                lead, rest = h[s][:, :LEAD], h[s][:, LEAD:]
+            scatter(s, lead, 0, LEAD)
+            tune(s - 1)
+            scatter(s, rest, LEAD, S)
             if s == PACK - 1:
+                weave_wd(0)
+                weave_wd(1)
+            if s == PACK:
                 for lo in range(0, M, BANK):
                     nc.scalar.copy(z_woven[:, lo : lo + BANK, :], z_rows[0][:, :, lo : lo + BANK].rearrange("p t m -> p m t"))
-            if s == PACK + 1:
-                for k in range(CHUNKS):
-                    nc.scalar.copy(woven[k][:, :, 0:2], z_rows[1][:, :, slice(*spans[k])].rearrange("p t m -> p m t"))
-
-        for s in range(LAST):
-            if s == 0:
-                scatter(s, h[0, 0][:], 0, BANK)
-                load_page(1)
-                load_w4(1)
-                scatter(s, h[0, 1][:], BANK, S)
-                order_w4_words(1)
-                for later in range(PACK, SLICES):
-                    project(later)
-            else:
-                scatter(s, h[s][:], 0, S)
-            after_scatter(s)
-            if s == LAST - 1:
-                x = late.tile([P, M], F32, name="x%d" % s, offset=2 * ROW)
-            else:
-                x = keep.tile([P, M], F32, name="x%d" % s, align_bytes=64)
-            tune(s, x)
-            if s + 2 < SLICES:
-                load_page(s + 2)
-            after_tune(s)
+                h[6, 0] = late_tile("h60", LEAD, F32, 0)
+                h[6, 1] = late_tile("h61", S - LEAD, F32, 4 * LEAD)
+                h[7] = late_tile("h7", S, F32, ROW)
+                nc.scalar.copy(h[6, 0][:], acc[6, 0][:, :LEAD])
+                nc.scalar.copy(h[6, 1][:, : BANK - LEAD], acc[6, 0][:, LEAD:])
+                nc.scalar.copy(h[6, 1][:, BANK - LEAD :], acc[6, 1][:])
+                for c in range(2):
+                    nc.scalar.copy(h[7][:, BANK * c : BANK * (c + 1)], acc[7, c][:])
+        for k in range(CHUNKS):
+            nc.scalar.copy(woven[k][:, :, 0:2], z_rows[1][:, :, slice(*spans[k])].rearrange("p t m -> p m t"))
+        quantise_wd(0, 0, late_tile("wd_q00", 2 * P, U32, 0))
+        open_sums(0)
+        tune(LAST - 1)
 
         scatter(LAST, h[LAST][:], 0, S)
         curve = keep.tile([P, M], F32, name="curve")
-        x_chunk = {}
+        x_chunk = [keep.tile([P, CHUNK], F32, name="x_chunk%d" % k) for k in range(CHUNKS)]
         unit = 4 * CHUNK
 
         def gather_chunk(k):
-            if k < CHUNKS - 1:
-                x_chunk[k] = keep.tile([P, CHUNK], F32, name="x_chunk%d" % k)
-            else:
-                x_chunk[k] = tail.tile([P, CHUNK], F32, name="x_chunk%d" % k, offset=0)
             nc.vector.tensor_copy(x_chunk[k][:], pages[LAST][:].indirect(entries(idx3, *spans[k])))
 
         def curve_chunk(k):
-            first, end = ((1, 2), (0, 2), (1, 4), (1, 2))[k]
-            held = tail.tile([P, end - first, CHUNK], F32, name="squares%d" % k, offset=unit * first)
-            squares = held[:, 1 - first, :]
+            units = 3 if k == 0 else 1
+            held = tail.tile([P, units, CHUNK], F32, name="squares%d" % k, offset=unit * ((k - 1) % CHUNKS), align_bytes=64)
+            squares = held[:, 0, :]
             nc.scalar.activation(squares, x_chunk[k][:], ACT.Square, bias=consts[:, 1, PACK - 1 : PACK], scale=-1.0)
             nc.scalar.activation(curve[:, slice(*spans[k])], squares, ACT.Exp, scale=-0.25)
 
@@ -336,29 +333,28 @@ def tile_list_place_field_atlas_kernel(
                 in_=woven[k][:].rearrange("p m t -> p (m t)"),
             )
 
-        quantise_wd(0, 1, "h%d" % LAST)
+        quantise_wd(0, 1, keep.tile([P, 2 * P], U32, name="wd_q01", tag="page%d" % (LAST - 1), align_bytes=64))
         open_sums(1)
-        for k in range(CHUNKS - 1):
+        for k in range(CHUNKS):
             gather_chunk(k)
-        curve_chunk(0)
+        for k in range(CHUNKS):
+            curve_chunk(k)
         gain_chunk(0)
+        quantise_wd(1, 0, tail.tile([P, 2 * P], U32, name="wd_q10", offset=unit * CHUNKS, align_bytes=64))
         quantise_chunk(0)
-        curve_chunk(1)
-        gather_chunk(3)
-        curve_chunk(2)
-        curve_chunk(3)
-        for k in range(1, CHUNKS):
+        quantise_wd(1, 1, tail.tile([P, 2 * P], U32, name="wd_q11", offset=unit * (CHUNKS + 1), align_bytes=64))
+        gain_chunk(1)
+        for k in range(2, CHUNKS):
             gain_chunk(k)
-            quantise_chunk(k)
+            quantise_chunk(k - 1)
+        quantise_chunk(CHUNKS - 1)
         out_v = out.rearrange("(j i p) m -> j p i m", j=2, i=2)
         for k in range(CHUNKS):
             for j in range(2):
                 out_pass(k, 2 * j, 1)
                 out_pass(k, 2 * j + 1, 1)
-                if k == 0:
-                    staged = tail.tile([P, 2, CHUNK], F32, name="staged%d%d" % (k, j), offset=unit * 2 * (1 - j))
-                else:
-                    staged = keep.tile([P, 2, CHUNK], F32, name="staged%d%d" % (k, j))
+                tag = ("h00", "h01", "h1", "h2", "h3", "h4", "h5", "x0")[2 * k + j]
+                staged = keep.tile([P, 2, CHUNK], F32, name="staged%d%d" % (k, j), tag=tag, align_bytes=64)
                 if k >= 2 and j == 1:
                     nc.vector.tensor_copy(staged[:], res[k, j][:])
                 else:

@@ -55,10 +55,11 @@ def tile_list_place_field_atlas_kernel(
 
         tab_sc = keep.tile([P, T], U8, name="tab_sc", align_bytes=64)
         w4s_raw = keep.tile([32, H], U8, name="w4s_raw", align_bytes=64)
-        planes = keep.tile([P, PASSES, S + H], U8, name="planes", align_bytes=64)
+        planes = [keep.tile([P, PASSES, 2 * BANK], U8, name="planes%d" % c, align_bytes=64) for c in range(2)]
         nc.vector.memset(tab_sc[32:64, :].bitcast(I32), 0)
         nc.vector.memset(tab_sc[64:128, :].bitcast(I32), 0)
-        nc.vector.memset(planes[:].bitcast(I32), 0)
+        for c in range(2):
+            nc.vector.memset(planes[c][:].bitcast(I32), 0)
         nc.sync.dma_start(idx[:], offs)
         nc.sync.dma_start(tab_sc[0:32, :].bitcast(I32), tab_scales.rearrange("a q t -> q a t").bitcast(I32))
         nc.sync.dma_start(w4s_raw[:].bitcast(I32), w4_scales.rearrange("a q c -> q a c").bitcast(I32))
@@ -80,8 +81,7 @@ def tile_list_place_field_atlas_kernel(
         wgs_src = wgs.rearrange("(x t y) s -> t x y s", t=PACK, y=RUN)
         wg = [keep.tile([P, S], F32, name="wg%d" % t, align_bytes=64) for t in range(PACK)]
 
-        def load_wgs(t, lo, hi, quadrants):
-            queue = nc.gpsimd if t == 0 else nc.sync
+        def load_wgs(t, lo, hi, quadrants, queue=nc.sync):
             for q in quadrants:
                 queue.dma_start(wg[t][32 * q : 32 * (q + 1), lo:hi], wgs_src[t][:, :, lo:hi])
 
@@ -91,7 +91,7 @@ def tile_list_place_field_atlas_kernel(
             tab_w[a] = keep.tile([P, T], I32, name="tab_w%d" % a, tag="tab_w%d" % a, align_bytes=64)
             nc.sync.dma_start(tab_w[a][:], tab_words[a].rearrange("p t i -> p (t i)").bitcast(I32))
 
-        load_wgs(0, 0, S, range(QUADRANTS))
+        load_wgs(0, 0, BANK, range(QUADRANTS), nc.gpsimd)
         load_table(0)
         load_w4(0)
         nc.sync.dma_start(idx2[:], offs2)
@@ -100,15 +100,21 @@ def tile_list_place_field_atlas_kernel(
         v_sc = keep.tile([P, S], U8, name="v_sc", align_bytes=64)
         both_sc = keep.tile([32, S + H], U8, name="both_sc", tag="both_sc", align_bytes=64)
         nc.vector.tensor_copy(v_sc[:], tab_sc[:].indirect(idx[:]))
+        halves = both_sc[:].bitcast(I32).rearrange("p (c u w) -> p c u w", c=2, u=2)
         nc.vector.tensor_copy(
-            both_sc[:, S:].bitcast(I32).rearrange("p (b t x) -> p b x t", b=PASSES, t=PACK),
+            halves[:, :, 1, :].rearrange("p b (t x) -> p b x t", t=PACK),
             w4s_raw[:].bitcast(I32).rearrange("p (b x t) -> p b x t", b=PASSES, t=PACK),
         )
-        nc.vector.tensor_copy(both_sc[:, :S].bitcast(I32), v_sc[0:32, :].bitcast(I32))
-        for q in range(QUADRANTS):
-            nc.sync.dma_start(
-                planes[32 * q : 32 * q + 4, :, :].bitcast(I32), both_sc[8 * q : 8 * q + 8, :].bitcast(I32)
-            )
+        nc.vector.tensor_copy(halves[:, :, 0, :], v_sc[0:32, :].bitcast(I32).rearrange("p (c w) -> p c w", c=2))
+
+        def carry_scales(c):
+            cols = slice(2 * BANK * c, 2 * BANK * (c + 1))
+            for q in range(QUADRANTS):
+                nc.sync.dma_start(
+                    planes[c][32 * q : 32 * q + 4, :, :].bitcast(I32), both_sc[8 * q : 8 * q + 8, cols].bitcast(I32)
+                )
+
+        carry_scales(0)
         v_w = [keep.tile([P, S], U32, name="v_w%d" % a, align_bytes=64) for a in range(PASSES)]
 
         def gather_words(a, lo, hi):
@@ -129,11 +135,13 @@ def tile_list_place_field_atlas_kernel(
 
         wd_src = wd.rearrange("(b x t y) n -> b t x y n", b=PASSES, t=PACK, y=RUN)
         wd_raw = [keep.tile([P, PACK, N], F32, name="wd_raw%d" % b, tag="tab_w%d" % b, align_bytes=64) for b in range(PASSES)]
+        load_page(0)
+        carry_scales(1)
+        load_w4(1)
+        load_wgs(0, BANK, S, range(QUADRANTS))
+        load_page(1)
         rows = keep.tile([P, PASSES, P], F32, name="rows", tag="both_sc", align_bytes=64)
         nc.gpsimd.memset(rows[:], 0.0)
-        load_page(0)
-        load_w4(1)
-        load_page(1)
         load_wgs(1, 0, LEAD, range(QUADRANTS))
         nc.sync.dma_start(idx3[:], offs3)
         for i, vec in enumerate((pref, gain)):
@@ -177,9 +185,9 @@ def tile_list_place_field_atlas_kernel(
                     nc.tensor.matmul_mx(
                         out=acc[s, c][:],
                         lhsT=w4_w[b][:, a, t, :].bitcast(FP4X4),
-                        lhsT_scale=planes[:, a, S + P * s : S + P * (s + 1)],
+                        lhsT_scale=planes[b][:, a, BANK + P * t : BANK + P * (t + 1)],
                         rhs=v_w[a][:, BANK * c : BANK * (c + 1)].bitcast(FP8X4),
-                        rhs_scale=planes[:, a, BANK * c : BANK * (c + 1)],
+                        rhs_scale=planes[c][:, a, :BANK],
                         start=(a == 0),
                         stop=(a == PASSES - 1),
                     )

@@ -60,6 +60,8 @@ def tile_list_place_field_atlas_kernel(
         nc.vector.memset(tab_sc[64:128, :].bitcast(I32), 0)
         for c in range(2):
             nc.vector.memset(planes[c][:].bitcast(I32), 0)
+        rows = keep.tile([P, PACK, P], F32, name="rows")
+        nc.vector.memset(rows[:], 0.0)
         nc.sync.dma_start(idx[:], offs)
         nc.sync.dma_start(tab_sc[0:32, :].bitcast(I32), tab_scales.rearrange("a q t -> q a t").bitcast(I32))
         nc.sync.dma_start(w4s_raw[:].bitcast(I32), w4_scales.rearrange("a q c -> q a c").bitcast(I32))
@@ -140,20 +142,17 @@ def tile_list_place_field_atlas_kernel(
         load_w4(1)
         load_wgs(0, BANK, S, range(QUADRANTS))
         load_page(1)
-        rows = keep.tile([P, PASSES, P], F32, name="rows", tag="both_sc", align_bytes=64)
-        nc.gpsimd.memset(rows[:], 0.0)
+        vecs = keep.tile([2 * PASSES, BANK], F32, name="vecs")
         load_wgs(1, 0, LEAD, range(QUADRANTS))
         nc.sync.dma_start(idx3[:], offs3)
-        for i, vec in enumerate((pref, gain)):
-            nc.sync.dma_start(
-                rows[PACK * i : PACK * (i + 1), :, :].rearrange("t b (x y) -> t (b x) y", y=RUN),
-                vec.rearrange("(bx t y) -> t bx y", t=PACK, y=RUN),
-            )
         for s in (1, 2):
             load_page(s + 1)
             load_wgs(s + 1, 0, LEAD, range(QUADRANTS - 1))
             load_wgs(s, LEAD, S, range(QUADRANTS))
             load_wgs(s + 1, 0, LEAD, [QUADRANTS - 1])
+            if s == 1:
+                for i, vec in enumerate((pref, gain)):
+                    nc.sync.dma_start(vecs[PASSES * i : PASSES * (i + 1), :], vec.rearrange("(b r) -> b r", b=PASSES))
         for b in range(PASSES):
             for t in range(PACK):
                 nc.sync.dma_start(wd_raw[b][:, t, :], wd_src[b, t])
@@ -165,15 +164,19 @@ def tile_list_place_field_atlas_kernel(
         load_page(6)
         load_page(7)
 
-        consts = keep.tile([P, PASSES, 2 * PACK], F32, name="consts")
+        consts = keep.tile([P, PACK, 2 * PASSES], F32, name="consts")
 
         def make_consts():
             ident = keep.tile([P, P], F32, name="ident", tag="w4_raw0")
             make_identity(nc, ident[:])
-            turned = psum.tile([P, PASSES, P], F32, name="turned", tag="bank3")
-            for b in range(PASSES):
-                nc.tensor.transpose(turned[:, b, :], rows[:, b, :], ident[:])
-            nc.scalar.copy(consts[:], turned[:, :, 0 : 2 * PACK])
+            nc.scalar.copy(
+                rows[0 : 2 * PASSES].rearrange("p t (x y) -> p t x y", y=RUN),
+                vecs[:].rearrange("p (x t y) -> p t x y", t=PACK, y=RUN),
+            )
+            turned = psum.tile([P, PACK, P], F32, name="turned", tag="bank3")
+            for t in range(PACK):
+                nc.tensor.transpose(turned[:, t, :], rows[:, t, :], ident[:])
+            nc.scalar.copy(consts[:], turned[:, :, 0 : 2 * PASSES])
 
         h, acc = {}, {}
 
@@ -221,7 +224,7 @@ def tile_list_place_field_atlas_kernel(
                 in_=wd_woven[b][:, cols, :].rearrange("p n t -> p (n t)"),
             )
 
-        z_held = late.tile([P, 6 * M], BF16, name="z_rows0", offset=0, align_bytes=64)
+        z_held = late.tile([P, 10 * M], BF16, name="z_rows0", offset=0, align_bytes=64)
         z_rows = [
             z_held[:, : PACK * M].rearrange("p (t m) -> p t m", t=PACK),
             tail.tile([P, 2, M], BF16, name="z_rows1", offset=0, align_bytes=64),
@@ -229,8 +232,7 @@ def tile_list_place_field_atlas_kernel(
         z_woven = keep.tile([P, M, PACK], BF16, name="z_woven", align_bytes=64)
         woven = [keep.tile([P, CHUNK, PACK], BF16, name="woven%d" % k, align_bytes=64) for k in range(CHUNKS)]
         spans = [(CHUNK * k, CHUNK * (k + 1)) for k in range(CHUNKS)]
-        z_q0 = keep.tile([P, M], U32, name="z_q0", align_bytes=64)
-        z_q = {(0, k): z_q0[:, CHUNK * k : CHUNK * (k + 1)] for k in range(CHUNKS)}
+        z_q = {}
         z_s = [keep.tile([P, M], U8, name="z_s%d" % b, align_bytes=64) for b in range(PASSES)]
         res = {}
 
@@ -243,13 +245,15 @@ def tile_list_place_field_atlas_kernel(
             else:
                 x = keep.tile([P, M], F32, name="x%d" % s, tag="x%d" % (s % 4 if s == 6 else s % 3), align_bytes=64)
             b, t = divmod(s, PACK)
-            gain_t = consts[:, b, PACK + t : PACK + t + 1]
+            gain_t = consts[:, t, PASSES + b : PASSES + b + 1]
             nc.vector.tensor_copy(x[:], pages[s][:].indirect(idx3[:]))
-            if s < LAST - 1:
+            if s < PACK:
                 y = keep.tile([P, M], F32, name="y%d" % s, tag="y")
+            elif s < LAST - 1:
+                y = late.tile([P, M], F32, name="y%d" % s, offset=4 * ROW, align_bytes=64)
             else:
                 y = tail.tile([P, M], F32, name="y", offset=0, align_bytes=64)
-            nc.scalar.activation(y[:], x[:], ACT.Square, bias=consts[:, b, t : t + 1], scale=-1.0)
+            nc.scalar.activation(y[:], x[:], ACT.Square, bias=consts[:, t, b : b + 1], scale=-1.0)
             nc.scalar.activation(y[:], y[:], ACT.Exp, scale=-0.25)
             if s == LAST - 1:
                 for k in range(CHUNKS):
@@ -268,11 +272,16 @@ def tile_list_place_field_atlas_kernel(
                 stop=(b == PASSES - 1 and nt % 2 == 1),
             )
 
-        def open_sums(j):
-            for k in range(CHUNKS):
+        def open_sums(j, chunks):
+            for k in chunks:
                 res[k, j] = psum.tile([P, 2, CHUNK], F32, name="res", tag="bank%d" % (2 * k + j))
                 out_pass(k, 2 * j, 0)
                 out_pass(k, 2 * j + 1, 0)
+
+        def quantise_z0(codes, lo, hi):
+            nc.vector.quantize_mx(
+                out=codes.bitcast(FP8X4), scales=z_s[0][:, lo:hi], in_=z_woven[:, lo:hi, :].rearrange("p m t -> p (m t)")
+            )
 
         def late_tile(name, words, dtype, offset):
             return late.tile([P, words], dtype, name=name, offset=offset, align_bytes=64)
@@ -284,33 +293,28 @@ def tile_list_place_field_atlas_kernel(
             project(s)
         for s in range(1, LAST):
             if s == LAST - 1:
-                nc.vector.quantize_mx(
-                    out=z_q0[:].bitcast(FP8X4), scales=z_s[0][:], in_=z_woven[:].rearrange("p m t -> p (m t)")
-                )
-                lead, rest = h[s, 0][:], h[s, 1][:]
-            else:
-                lead, rest = h[s][:, :LEAD], h[s][:, LEAD:]
-            scatter(s, lead, 0, LEAD)
+                z_q0 = late_tile("z_q0", M - CHUNK, U32, 3 * ROW)
+                for k in range(CHUNKS - 1):
+                    z_q[0, k] = z_q0[:, slice(*spans[k])]
+                quantise_z0(z_q0[:, :BANK], 0, BANK)
+                quantise_z0(z_q0[:, BANK:], BANK, M - CHUNK)
+            scatter(s, h[s][:, :LEAD], 0, LEAD)
             tune(s - 1)
-            scatter(s, rest, LEAD, S)
+            scatter(s, h[s][:, LEAD:], LEAD, S)
             if s == PACK - 1:
                 weave_wd(0)
                 weave_wd(1)
             if s == PACK:
                 for lo in range(0, M, BANK):
                     nc.scalar.copy(z_woven[:, lo : lo + BANK, :], z_rows[0][:, :, lo : lo + BANK].rearrange("p t m -> p m t"))
-                h[6, 0] = late_tile("h60", LEAD, F32, 0)
-                h[6, 1] = late_tile("h61", S - LEAD, F32, 4 * LEAD)
-                h[7] = late_tile("h7", S, F32, ROW)
-                nc.scalar.copy(h[6, 0][:], acc[6, 0][:, :LEAD])
-                nc.scalar.copy(h[6, 1][:, : BANK - LEAD], acc[6, 0][:, LEAD:])
-                nc.scalar.copy(h[6, 1][:, BANK - LEAD :], acc[6, 1][:])
-                for c in range(2):
-                    nc.scalar.copy(h[7][:, BANK * c : BANK * (c + 1)], acc[7, c][:])
+                for later in (LAST - 1, LAST):
+                    h[later] = late_tile("h%d" % later, S, F32, ROW * (later - LAST + 1))
+                    for c in range(2):
+                        nc.scalar.copy(h[later][:, BANK * c : BANK * (c + 1)], acc[later, c][:])
         for k in range(CHUNKS):
             nc.scalar.copy(woven[k][:, :, 0:2], z_rows[1][:, :, slice(*spans[k])].rearrange("p t m -> p m t"))
-        quantise_wd(0, 0, late_tile("wd_q00", 2 * P, U32, 0))
-        open_sums(0)
+        quantise_wd(0, 0, keep.tile([P, 2 * P], U32, name="wd_q00", tag="page%d" % (LAST - 2), align_bytes=64))
+        open_sums(0, range(CHUNKS - 1))
         tune(LAST - 1)
 
         scatter(LAST, h[LAST][:], 0, S)
@@ -325,12 +329,12 @@ def tile_list_place_field_atlas_kernel(
             units = 3 if k == 0 else 1
             held = tail.tile([P, units, CHUNK], F32, name="squares%d" % k, offset=unit * ((k - 1) % CHUNKS), align_bytes=64)
             squares = held[:, 0, :]
-            nc.scalar.activation(squares, x_chunk[k][:], ACT.Square, bias=consts[:, 1, PACK - 1 : PACK], scale=-1.0)
+            nc.scalar.activation(squares, x_chunk[k][:], ACT.Square, bias=consts[:, PACK - 1, 1:2], scale=-1.0)
             nc.scalar.activation(curve[:, slice(*spans[k])], squares, ACT.Exp, scale=-0.25)
 
         def gain_chunk(k):
             cols = slice(*spans[k])
-            gain_t = consts[:, 1, 2 * PACK - 1 : 2 * PACK]
+            gain_t = consts[:, PACK - 1, 2 * PASSES - 1 : 2 * PASSES]
             nc.vector.tensor_scalar(woven[k][:, :, PACK - 1], curve[:, cols], gain_t, None, MULT)
 
         def quantise_chunk(k):
@@ -342,7 +346,7 @@ def tile_list_place_field_atlas_kernel(
             )
 
         quantise_wd(0, 1, keep.tile([P, 2 * P], U32, name="wd_q01", tag="page%d" % (LAST - 1), align_bytes=64))
-        open_sums(1)
+        open_sums(1, range(CHUNKS - 1))
         for k in range(CHUNKS):
             gather_chunk(k)
         for k in range(CHUNKS):
@@ -350,15 +354,20 @@ def tile_list_place_field_atlas_kernel(
         gain_chunk(0)
         quantise_wd(1, 0, tail.tile([P, 2 * P], U32, name="wd_q10", offset=unit * CHUNKS, align_bytes=64))
         quantise_chunk(0)
-        quantise_wd(1, 1, tail.tile([P, 2 * P], U32, name="wd_q11", offset=unit * (CHUNKS + 1), align_bytes=64))
         gain_chunk(1)
-        for k in range(2, CHUNKS):
-            gain_chunk(k)
-            quantise_chunk(k - 1)
-        quantise_chunk(CHUNKS - 1)
+        quantise_wd(1, 1, tail.tile([P, 2 * P], U32, name="wd_q11", offset=unit * (CHUNKS + 1), align_bytes=64))
+        quantise_chunk(1)
+        gain_chunk(2)
+        gain_chunk(3)
+        quantise_chunk(2)
+        z_q[0, 3] = tail.tile([P, CHUNK], U32, name="z_q03", offset=unit * 2, align_bytes=64)[:]
+        quantise_z0(z_q[0, 3], M - CHUNK, M)
+        quantise_chunk(3)
         out_v = out.rearrange("(j i p) m -> j p i m", j=2, i=2)
         for k in range(CHUNKS):
             for j in range(2):
+                if k == CHUNKS - 1:
+                    open_sums(j, [k])
                 out_pass(k, 2 * j, 1)
                 out_pass(k, 2 * j + 1, 1)
                 tag = ("h00", "h01", "h1", "h2", "h3", "h4", "h5", "x0")[2 * k + j]

@@ -213,7 +213,13 @@ def tile_list_place_field_atlas_kernel(
 
         def weave_wd(b):
             wd_woven[b] = keep.tile([P, N, PACK], BF16, name="wd_woven%d" % b, align_bytes=64)
-            nc.scalar.copy(wd_woven[b][:], wd_raw[b][:].rearrange("p t n -> p n t"))
+            if b == 0:
+                nc.scalar.copy(
+                    wd_woven[b][:].rearrange("p (i j n) t -> p j i n t", i=2, j=2),
+                    wd_raw[b][:].rearrange("p t (j i n) -> p j i n t", i=2, j=2),
+                )
+            else:
+                nc.scalar.copy(wd_woven[b][:], wd_raw[b][:].rearrange("p t n -> p n t"))
 
         def quantise_wd(b, j, codes):
             cols = slice(2 * P * j, 2 * P * (j + 1))
@@ -262,10 +268,12 @@ def tile_list_place_field_atlas_kernel(
                 nc.scalar.activation(z_rows[b][:, t, :], y[:], ACT.Copy, scale=gain_t)
 
         def out_pass(k, nt, b):
+            half, part = divmod(nt, 2) if b == 1 else (nt % 2, nt // 2)
+            place = 2 * half + part
             nc.tensor.matmul_mx(
                 out=res[k, nt // 2][:, nt % 2, :],
-                lhsT=wd_q[b, nt // 2][:, P * (nt % 2) : P * (nt % 2 + 1)].bitcast(FP8X4),
-                lhsT_scale=wd_s[b][:, P * nt : P * (nt + 1)],
+                lhsT=wd_q[b, half][:, P * part : P * (part + 1)].bitcast(FP8X4),
+                lhsT_scale=wd_s[b][:, P * place : P * (place + 1)],
                 rhs=z_q[b, k].bitcast(FP8X4),
                 rhs_scale=z_s[b][:, CHUNK * k : CHUNK * (k + 1)],
                 start=(b == 0 and nt % 2 == 0),
@@ -313,8 +321,7 @@ def tile_list_place_field_atlas_kernel(
                         nc.scalar.copy(h[later][:, BANK * c : BANK * (c + 1)], acc[later, c][:])
         for k in range(CHUNKS):
             nc.scalar.copy(woven[k][:, :, 0:2], z_rows[1][:, :, slice(*spans[k])].rearrange("p t m -> p m t"))
-        quantise_wd(0, 0, keep.tile([P, 2 * P], U32, name="wd_q00", tag="page%d" % (LAST - 2), align_bytes=64))
-        open_sums(0, range(CHUNKS - 1))
+        quantise_wd(0, 1, keep.tile([P, 2 * P], U32, name="wd_q01", tag="page%d" % (LAST - 2), align_bytes=64))
         tune(LAST - 1)
 
         scatter(LAST, h[LAST][:], 0, S)
@@ -345,8 +352,10 @@ def tile_list_place_field_atlas_kernel(
                 in_=woven[k][:].rearrange("p m t -> p (m t)"),
             )
 
-        quantise_wd(0, 1, keep.tile([P, 2 * P], U32, name="wd_q01", tag="page%d" % (LAST - 1), align_bytes=64))
-        open_sums(1, range(CHUNKS - 1))
+        quantise_wd(0, 0, keep.tile([P, 2 * P], U32, name="wd_q00", tag="page%d" % (LAST - 1), align_bytes=64))
+        for k in range(CHUNKS - 1):
+            open_sums(0, [k])
+            open_sums(1, [k])
         for k in range(CHUNKS):
             gather_chunk(k)
         for k in range(CHUNKS):

@@ -58,13 +58,10 @@ def tile_list_place_field_atlas_kernel(
         planes = [keep.tile([P, PASSES, 2 * BANK], U8, name="planes%d" % c, align_bytes=64) for c in range(2)]
         nc.vector.memset(tab_sc[32:64, :].bitcast(I32), 0)
         nc.vector.memset(tab_sc[64:128, :].bitcast(I32), 0)
-        for c in range(2):
-            nc.vector.memset(planes[c][:].bitcast(I32), 0)
-        rows = keep.tile([P, PACK, P], F32, name="rows")
-        nc.vector.memset(rows[:], 0.0)
+        nc.gpsimd.memset(planes[0][:].bitcast(I32), 0)
+        nc.sync.dma_start(w4s_raw[:].bitcast(I32), w4_scales.rearrange("a q c -> q a c").bitcast(I32))
         nc.sync.dma_start(idx[:], offs)
         nc.sync.dma_start(tab_sc[0:32, :].bitcast(I32), tab_scales.rearrange("a q t -> q a t").bitcast(I32))
-        nc.sync.dma_start(w4s_raw[:].bitcast(I32), w4_scales.rearrange("a q c -> q a c").bitcast(I32))
 
         w4_raw = {}
         w4_src = w4_words.rearrange("a p c -> p a c").bitcast(I32)
@@ -94,20 +91,33 @@ def tile_list_place_field_atlas_kernel(
             nc.sync.dma_start(tab_w[a][:], tab_words[a].rearrange("p t i -> p (t i)").bitcast(I32))
 
         load_wgs(0, 0, BANK, range(QUADRANTS), nc.gpsimd)
-        load_table(0)
+        nc.gpsimd.memset(planes[1][:].bitcast(I32), 0)
         load_w4(0)
+        load_table(0)
         nc.sync.dma_start(idx2[:], offs2)
         load_table(1)
 
         v_sc = keep.tile([P, S], U8, name="v_sc", align_bytes=64)
         both_sc = keep.tile([32, S + H], U8, name="both_sc", tag="both_sc", align_bytes=64)
-        nc.vector.tensor_copy(v_sc[:], tab_sc[:].indirect(idx[:]))
+        w4_w = [keep.tile([P, PASSES, PACK, 2 * P], U8, name="w4_w%d" % b, align_bytes=64) for b in range(PASSES)]
+
+        def order_w4_words(b):
+            nc.vector.tensor_copy(
+                w4_w[b][:].bitcast(I32).rearrange("p a t (x e) -> p a x t e", e=2),
+                w4_raw[b][:].rearrange("p a (x t e) -> p a x t e", t=PACK, e=2),
+            )
+
         halves = both_sc[:].bitcast(I32).rearrange("p (c u w) -> p c u w", c=2, u=2)
         nc.vector.tensor_copy(
             halves[:, :, 1, :].rearrange("p b (t x) -> p b x t", t=PACK),
             w4s_raw[:].bitcast(I32).rearrange("p (b x t) -> p b x t", b=PASSES, t=PACK),
         )
-        nc.vector.tensor_copy(halves[:, :, 0, :], v_sc[0:32, :].bitcast(I32).rearrange("p (c w) -> p c w", c=2))
+        for c in range(2):
+            cols = slice(BANK * c, BANK * (c + 1))
+            nc.vector.tensor_copy(v_sc[:, cols], tab_sc[:].indirect(entries(idx, cols.start, cols.stop)))
+        nc.vector.tensor_copy(halves[:, 0, 0, :], v_sc[0:32, :BANK].bitcast(I32))
+        order_w4_words(0)
+        nc.vector.tensor_copy(halves[:, 1, 0, :], v_sc[0:32, BANK:].bitcast(I32))
 
         def carry_scales(c):
             cols = slice(2 * BANK * c, 2 * BANK * (c + 1))
@@ -122,17 +132,9 @@ def tile_list_place_field_atlas_kernel(
         def gather_words(a, lo, hi):
             nc.vector.tensor_copy(v_w[a][:, lo:hi], tab_w[a][:].bitcast(U32).indirect(entries(idx, lo, hi)))
 
-        w4_w = [keep.tile([P, PASSES, PACK, 2 * P], U8, name="w4_w%d" % b, align_bytes=64) for b in range(PASSES)]
-
-        def order_w4_words(b):
-            nc.vector.tensor_copy(
-                w4_w[b][:].bitcast(I32).rearrange("p a t (x e) -> p a x t e", e=2),
-                w4_raw[b][:].rearrange("p a (x t e) -> p a x t e", t=PACK, e=2),
-            )
-
         gather_words(0, 0, S)
-        order_w4_words(0)
-        gather_words(1, 0, BANK)
+        gather_words(1, 0, LEAD)
+        gather_words(1, LEAD, BANK)
         gather_words(1, BANK, S)
 
         wd_src = wd.rearrange("(b x t y) n -> b t x y n", b=PASSES, t=PACK, y=RUN)
@@ -169,6 +171,8 @@ def tile_list_place_field_atlas_kernel(
         def make_consts():
             ident = keep.tile([P, P], F32, name="ident", tag="w4_raw0")
             make_identity(nc, ident[:])
+            rows = keep.tile([P, PACK, P], F32, name="rows", tag="both_sc", align_bytes=64)
+            nc.gpsimd.memset(rows[:], 0.0)
             nc.scalar.copy(
                 rows[0 : 2 * PASSES].rearrange("p t (x y) -> p t x y", y=RUN),
                 vecs[:].rearrange("p (x t y) -> p t x y", t=PACK, y=RUN),
@@ -182,7 +186,7 @@ def tile_list_place_field_atlas_kernel(
 
         def project(s):
             b, t = divmod(s, PACK)
-            for c in range(2):
+            for c in range(s == 0, 2):
                 acc[s, c] = psum.tile([P, BANK], F32, name="acc", tag="bank%d" % ((2 * s + c) % BANKS))
                 for a in range(PASSES):
                     nc.tensor.matmul_mx(
@@ -202,6 +206,25 @@ def tile_list_place_field_atlas_kernel(
                         h[s] = keep.tile([P, S], F32, name="h%d" % s, tag="h%d" % s, align_bytes=64)
                     nc.scalar.copy(h[s][:, BANK * c : BANK * (c + 1)], acc[s, c][:])
 
+        def project_first():
+            h[0, 0] = keep.tile([P, BANK], F32, name="h00", tag="h00", align_bytes=64)
+            for quarter in range(2):
+                first = psum.tile([P, BANK], F32, name="first", tag="bank%d" % (0, BANKS - 1)[quarter])
+                for a in range(PASSES):
+                    for i in range(2):
+                        lo = LEAD * quarter + P * i
+                        nc.tensor.matmul_mx(
+                            out=first[:, P * i : P * (i + 1)],
+                            lhsT=w4_w[0][:, a, 0, :].bitcast(FP4X4),
+                            lhsT_scale=planes[0][:, a, BANK : BANK + P],
+                            rhs=v_w[a][:, lo : lo + P].bitcast(FP8X4),
+                            rhs_scale=planes[0][:, a, lo : lo + P],
+                            start=(a == 0 and i == 0),
+                            stop=(a == PASSES - 1 and i == 1),
+                        )
+                nc.scalar.copy(h[0, 0][:, LEAD * quarter : LEAD * (quarter + 1)], first[:, :LEAD])
+
+        project_first()
         project(0)
         project(1)
         make_consts()

@@ -31,6 +31,7 @@ CHUNK = 256
 CHUNKS = M // CHUNK
 ROW = 4 * M
 LEAD = 256
+FIRST_LEAD = 512
 BULK = T2 - BANK
 W4_WORDS = BANK // 2
 
@@ -54,12 +55,25 @@ def tile_list_place_field_atlas_kernel(
             return offsets[:, lo // PER_COLUMN : hi // PER_COLUMN]
 
         tab_sc = keep.tile([P, T], U8, name="tab_sc", align_bytes=64)
-        w4s_raw = keep.tile([32, H], U8, name="w4s_raw", align_bytes=64)
-        planes = [keep.tile([P, PASSES, 2 * BANK], U8, name="planes%d" % c, align_bytes=64) for c in range(2)]
+        w4s_raw = [keep.tile([32, BANK], U8, name="w4s_raw%d" % b, align_bytes=64) for b in range(PASSES)]
+        w4s_src = w4_scales.rearrange("a q c -> q a c").bitcast(I32)
+        widths = (BANK + P, BANK + 3 * P, BANK)
+        planes = [keep.tile([P, PASSES, w], U8, name="planes%d" % c, align_bytes=64) for c, w in enumerate(widths)]
+
+        def v_plane(a, lo, hi):
+            return planes[0][:, a, lo:hi] if lo < BANK else planes[1][:, a, lo - P : hi - P]
+
+        def w4_plane(a, s):
+            c, lo = (0, BANK) if s == 0 else (1, P * (s - 1)) if s < PACK else (2, P * (s - PACK))
+            return planes[c][:, a, lo : lo + P]
+
+        def load_w4_scales(b):
+            nc.sync.dma_start(w4s_raw[b][:].bitcast(I32), w4s_src[:, :, P * b : P * (b + 1)])
+
         nc.vector.memset(tab_sc[32:64, :].bitcast(I32), 0)
         nc.vector.memset(tab_sc[64:128, :].bitcast(I32), 0)
         nc.gpsimd.memset(planes[0][:].bitcast(I32), 0)
-        nc.sync.dma_start(w4s_raw[:].bitcast(I32), w4_scales.rearrange("a q c -> q a c").bitcast(I32))
+        load_w4_scales(0)
         nc.sync.dma_start(idx[:], offs)
         nc.sync.dma_start(tab_sc[0:32, :].bitcast(I32), tab_scales.rearrange("a q t -> q a t").bitcast(I32))
 
@@ -92,13 +106,15 @@ def tile_list_place_field_atlas_kernel(
 
         load_wgs(0, 0, BANK, range(QUADRANTS), nc.gpsimd)
         nc.gpsimd.memset(planes[1][:].bitcast(I32), 0)
+        nc.gpsimd.memset(planes[2][:].bitcast(I32), 0)
         load_w4(0)
         load_table(0)
         nc.sync.dma_start(idx2[:], offs2)
         load_table(1)
 
         v_sc = keep.tile([P, S], U8, name="v_sc", align_bytes=64)
-        both_sc = keep.tile([32, S + H], U8, name="both_sc", tag="both_sc", align_bytes=64)
+        both_sc = keep.tile([32, S + BANK], U8, name="both_sc", tag="both_sc", align_bytes=64)
+        late_sc = keep.tile([32, BANK], U8, name="late_sc", align_bytes=64)
         w4_w = [keep.tile([P, PASSES, PACK, 2 * P], U8, name="w4_w%d" % b, align_bytes=64) for b in range(PASSES)]
 
         def order_w4_words(b):
@@ -107,23 +123,25 @@ def tile_list_place_field_atlas_kernel(
                 w4_raw[b][:].rearrange("p a (x t e) -> p a x t e", t=PACK, e=2),
             )
 
-        halves = both_sc[:].bitcast(I32).rearrange("p (c u w) -> p c u w", c=2, u=2)
-        nc.vector.tensor_copy(
-            halves[:, :, 1, :].rearrange("p b (t x) -> p b x t", t=PACK),
-            w4s_raw[:].bitcast(I32).rearrange("p (b x t) -> p b x t", b=PASSES, t=PACK),
-        )
+        def order_w4_scales(b, dst):
+            nc.vector.tensor_copy(
+                dst.bitcast(I32).rearrange("p (t x) -> p x t", t=PACK),
+                w4s_raw[b][:].bitcast(I32).rearrange("p (x t) -> p x t", t=PACK),
+            )
+
+        order_w4_scales(0, both_sc[:, BANK : 2 * BANK])
         for c in range(2):
             cols = slice(BANK * c, BANK * (c + 1))
             nc.vector.tensor_copy(v_sc[:, cols], tab_sc[:].indirect(entries(idx, cols.start, cols.stop)))
-        nc.vector.tensor_copy(halves[:, 0, 0, :], v_sc[0:32, :BANK].bitcast(I32))
+        nc.vector.tensor_copy(both_sc[:, :BANK].bitcast(I32), v_sc[0:32, :BANK].bitcast(I32))
         order_w4_words(0)
-        nc.vector.tensor_copy(halves[:, 1, 0, :], v_sc[0:32, BANK:].bitcast(I32))
+        nc.vector.tensor_copy(both_sc[:, 2 * BANK :].bitcast(I32), v_sc[0:32, BANK:].bitcast(I32))
 
         def carry_scales(c):
-            cols = slice(2 * BANK * c, 2 * BANK * (c + 1))
-            for q in range(QUADRANTS):
+            rows_sc = (both_sc[:, : widths[0]], both_sc[:, widths[0] :], late_sc[:])[c]
+            for q in (0, 2, 1, 3):
                 nc.sync.dma_start(
-                    planes[c][32 * q : 32 * q + 4, :, :].bitcast(I32), both_sc[8 * q : 8 * q + 8, cols].bitcast(I32)
+                    planes[c][32 * q : 32 * q + 4, :, :].bitcast(I32), rows_sc[8 * q : 8 * q + 8, :].bitcast(I32)
                 )
 
         carry_scales(0)
@@ -140,18 +158,22 @@ def tile_list_place_field_atlas_kernel(
         wd_src = wd.rearrange("(b x t y) n -> b t x y n", b=PASSES, t=PACK, y=RUN)
         wd_raw = [keep.tile([P, PACK, N], F32, name="wd_raw%d" % b, tag="tab_w%d" % b, align_bytes=64) for b in range(PASSES)]
         load_page(0)
+        load_w4_scales(1)
         carry_scales(1)
-        load_w4(1)
         load_wgs(0, BANK, S, range(QUADRANTS))
         load_page(1)
         vecs = keep.tile([2 * PASSES, BANK], F32, name="vecs")
-        load_wgs(1, 0, LEAD, range(QUADRANTS))
+        load_wgs(1, 0, FIRST_LEAD, range(QUADRANTS))
         nc.sync.dma_start(idx3[:], offs3)
+        load_w4(1)
+        order_w4_scales(1, late_sc[:])
+        carry_scales(2)
+        order_w4_words(1)
         for s in (1, 2):
             load_page(s + 1)
-            load_wgs(s + 1, 0, LEAD, range(QUADRANTS - 1))
-            load_wgs(s, LEAD, S, range(QUADRANTS))
-            load_wgs(s + 1, 0, LEAD, [QUADRANTS - 1])
+            load_wgs(s + 1, 0, FIRST_LEAD, range(QUADRANTS - 1))
+            load_wgs(s, FIRST_LEAD, S, range(QUADRANTS))
+            load_wgs(s + 1, 0, FIRST_LEAD, [QUADRANTS - 1])
             if s == 1:
                 for i, vec in enumerate((pref, gain)):
                     nc.sync.dma_start(vecs[PASSES * i : PASSES * (i + 1), :], vec.rearrange("(b r) -> b r", b=PASSES))
@@ -160,7 +182,7 @@ def tile_list_place_field_atlas_kernel(
                 nc.sync.dma_start(wd_raw[b][:, t, :], wd_src[b, t])
         load_page(4, 0, BULK)
         load_page(5, 0, BULK)
-        load_wgs(3, LEAD, S, range(QUADRANTS))
+        load_wgs(3, FIRST_LEAD, S, range(QUADRANTS))
         load_page(4, BULK, T2)
         load_page(5, BULK, T2)
         load_page(6)
@@ -192,9 +214,9 @@ def tile_list_place_field_atlas_kernel(
                     nc.tensor.matmul_mx(
                         out=acc[s, c][:],
                         lhsT=w4_w[b][:, a, t, :].bitcast(FP4X4),
-                        lhsT_scale=planes[b][:, a, BANK + P * t : BANK + P * (t + 1)],
+                        lhsT_scale=w4_plane(a, s),
                         rhs=v_w[a][:, BANK * c : BANK * (c + 1)].bitcast(FP8X4),
-                        rhs_scale=planes[c][:, a, :BANK],
+                        rhs_scale=v_plane(a, BANK * c, BANK * (c + 1)),
                         start=(a == 0),
                         stop=(a == PASSES - 1),
                     )
@@ -216,9 +238,9 @@ def tile_list_place_field_atlas_kernel(
                         nc.tensor.matmul_mx(
                             out=first[:, P * i : P * (i + 1)],
                             lhsT=w4_w[0][:, a, 0, :].bitcast(FP4X4),
-                            lhsT_scale=planes[0][:, a, BANK : BANK + P],
+                            lhsT_scale=w4_plane(a, 0),
                             rhs=v_w[a][:, lo : lo + P].bitcast(FP8X4),
-                            rhs_scale=planes[0][:, a, lo : lo + P],
+                            rhs_scale=v_plane(a, lo, lo + P),
                             start=(a == 0 and i == 0),
                             stop=(a == PASSES - 1 and i == 1),
                         )
@@ -318,7 +340,6 @@ def tile_list_place_field_atlas_kernel(
             return late.tile([P, words], dtype, name=name, offset=offset, align_bytes=64)
 
         scatter(0, h[0, 0][:], 0, BANK)
-        order_w4_words(1)
         scatter(0, h[0, 1][:], BANK, S)
         for s in range(PACK, SLICES):
             project(s)
@@ -329,9 +350,10 @@ def tile_list_place_field_atlas_kernel(
                     z_q[0, k] = z_q0[:, slice(*spans[k])]
                 quantise_z0(z_q0[:, :BANK], 0, BANK)
                 quantise_z0(z_q0[:, BANK:], BANK, M - CHUNK)
-            scatter(s, h[s][:, :LEAD], 0, LEAD)
+            lead = FIRST_LEAD if s < PACK else LEAD
+            scatter(s, h[s][:, :lead], 0, lead)
             tune(s - 1)
-            scatter(s, h[s][:, LEAD:], LEAD, S)
+            scatter(s, h[s][:, lead:], lead, S)
             if s == PACK - 1:
                 weave_wd(0)
                 weave_wd(1)
@@ -390,16 +412,16 @@ def tile_list_place_field_atlas_kernel(
         quantise_wd(1, 1, tail.tile([P, 2 * P], U32, name="wd_q11", offset=unit * (CHUNKS + 1), align_bytes=64))
         quantise_chunk(1)
         gain_chunk(2)
-        gain_chunk(3)
-        quantise_chunk(2)
-        z_q[0, 3] = tail.tile([P, CHUNK], U32, name="z_q03", offset=unit * 2, align_bytes=64)[:]
+        z_q[0, 3] = tail.tile([P, CHUNK], U32, name="z_q03", offset=unit, align_bytes=64)[:]
         quantise_z0(z_q[0, 3], M - CHUNK, M)
+        quantise_chunk(2)
+        gain_chunk(3)
         quantise_chunk(3)
+        for j in range(2):
+            open_sums(j, [CHUNKS - 1])
         out_v = out.rearrange("(j i p) m -> j p i m", j=2, i=2)
         for k in range(CHUNKS):
             for j in range(2):
-                if k == CHUNKS - 1:
-                    open_sums(j, [k])
                 out_pass(k, 2 * j, 1)
                 out_pass(k, 2 * j + 1, 1)
                 tag = ("h00", "h01", "h1", "h2", "h3", "h4", "h5", "x0")[2 * k + j]

@@ -350,8 +350,9 @@ def tile_list_place_field_atlas_kernel(
                     z_q[0, k] = z_q0[:, slice(*spans[k])]
                 quantise_z0(z_q0[:, :BANK], 0, BANK)
                 quantise_z0(z_q0[:, BANK:], BANK, M - CHUNK)
-            lead = FIRST_LEAD if s < PACK else LEAD
-            scatter(s, h[s][:, :lead], 0, lead)
+            lead = FIRST_LEAD if s < PACK else LEAD if s < LAST - 1 else 0
+            if lead:
+                scatter(s, h[s][:, :lead], 0, lead)
             tune(s - 1)
             scatter(s, h[s][:, lead:], lead, S)
             if s == PACK - 1:
@@ -379,7 +380,7 @@ def tile_list_place_field_atlas_kernel(
 
         def curve_chunk(k):
             units = 3 if k == 0 else 1
-            held = tail.tile([P, units, CHUNK], F32, name="squares%d" % k, offset=unit * ((k - 1) % CHUNKS), align_bytes=64)
+            held = tail.tile([P, units, CHUNK], F32, name="squares%d" % k, offset=3 * unit * ((k + 1) % 2), align_bytes=64)
             squares = held[:, 0, :]
             nc.scalar.activation(squares, x_chunk[k][:], ACT.Square, bias=consts[:, PACK - 1, 1:2], scale=-1.0)
             nc.scalar.activation(curve[:, slice(*spans[k])], squares, ACT.Exp, scale=-0.25)
@@ -412,7 +413,7 @@ def tile_list_place_field_atlas_kernel(
         quantise_wd(1, 1, tail.tile([P, 2 * P], U32, name="wd_q11", offset=unit * (CHUNKS + 1), align_bytes=64))
         quantise_chunk(1)
         gain_chunk(2)
-        z_q[0, 3] = tail.tile([P, CHUNK], U32, name="z_q03", offset=unit, align_bytes=64)[:]
+        z_q[0, 3] = tail.tile([P, CHUNK], U32, name="z_q03", offset=3 * unit, align_bytes=64)[:]
         quantise_z0(z_q[0, 3], M - CHUNK, M)
         quantise_chunk(2)
         gain_chunk(3)

@@ -72,11 +72,15 @@ def tile_list_place_field_atlas_kernel(
 
         nc.vector.memset(tab_sc[32:64, :].bitcast(I32), 0)
         nc.vector.memset(tab_sc[64:128, :].bitcast(I32), 0)
+        wg0_rows = keep.tile([P, S // 4], F32, name="wg0_rows", tag="x1", align_bytes=64)
+        ident = keep.tile([P, P], F32, name="ident")
+        make_identity(nc, ident[:])
         nc.gpsimd.memset(planes[0][:].bitcast(I32), 0)
         load_w4_scales(0)
         nc.sync.dma_start(idx[:], offs)
         nc.sync.dma_start(tab_sc[0:32, :].bitcast(I32), tab_scales.rearrange("a q t -> q a t").bitcast(I32))
 
+        nc.sync.dma_start(wg0_rows[:], wgs.rearrange("(x t y) (c s) -> t (y c) x s", t=PACK, y=RUN, c=4)[0])
         w4_raw = {}
         w4_src = w4_words.rearrange("a p c -> p a c").bitcast(I32)
 
@@ -94,17 +98,37 @@ def tile_list_place_field_atlas_kernel(
         wgs_src = wgs.rearrange("(x t y) s -> t x y s", t=PACK, y=RUN)
         wg = [keep.tile([P, S], F32, name="wg%d" % t, align_bytes=64) for t in range(PACK)]
 
-        def load_wgs(t, lo, hi, quadrants, queue=nc.sync):
+        def load_wgs(t, lo, hi, quadrants):
             for q in quadrants:
-                queue.dma_start(wg[t][32 * q : 32 * (q + 1), lo:hi], wgs_src[t][:, :, lo:hi])
+                nc.sync.dma_start(wg[t][32 * q : 32 * (q + 1), lo:hi], wgs_src[t][:, :, lo:hi])
 
+        def spread_wg0():
+            across = psum.tile([P, 2, P], F32, name="across", tag="bank4")
+            for i in range(2):
+                nc.tensor.transpose(across[:, i, :], wg0_rows[:, P * i : P * (i + 1)], ident[:])
+            fourfold = keep.tile([P, 4, 2, QUADRANTS, 32], F32, name="fourfold", tag="x0", align_bytes=64)
+            for i in range(2):
+                nc.scalar.copy(
+                    fourfold[:, :, i, :, :].rearrange("p c q (x y) -> p c q x y", y=RUN),
+                    across[:, i, :]
+                    .rearrange("p (y c x) -> p c x y", y=RUN, c=4)
+                    .unsqueeze(2)
+                    .to_broadcast([P, 4, QUADRANTS, 8, RUN]),
+                )
+            for half in range(2):
+                back = psum.tile([P, 4, P], F32, name="back", tag="bank%d" % (5 + half))
+                for n in range(4):
+                    c, i = divmod(4 * half + n, 2)
+                    nc.tensor.transpose(back[:, n, :], fourfold[:, c, i, :, :].rearrange("p q u -> p (q u)"), ident[:])
+                nc.scalar.copy(wg[0][:, BANK * half : BANK * (half + 1)], back[:].rearrange("p n j -> p (n j)"))
+
+        spread_wg0()
         tab_w = {}
 
         def load_table(a):
             tab_w[a] = keep.tile([P, T], I32, name="tab_w%d" % a, tag="tab_w%d" % a, align_bytes=64)
             nc.sync.dma_start(tab_w[a][:], tab_words[a].rearrange("p t i -> p (t i)").bitcast(I32))
 
-        load_wgs(0, 0, BANK, range(QUADRANTS), nc.gpsimd)
         nc.gpsimd.memset(planes[1][:].bitcast(I32), 0)
         nc.gpsimd.memset(planes[2][:].bitcast(I32), 0)
         load_w4(0)
@@ -160,7 +184,6 @@ def tile_list_place_field_atlas_kernel(
         load_page(0)
         load_w4_scales(1)
         carry_scales(1)
-        load_wgs(0, BANK, S, range(QUADRANTS))
         load_page(1)
         vecs = keep.tile([2 * PASSES, BANK], F32, name="vecs")
         load_wgs(1, 0, FIRST_LEAD, range(QUADRANTS))
@@ -191,8 +214,6 @@ def tile_list_place_field_atlas_kernel(
         consts = keep.tile([P, PACK, 2 * PASSES], F32, name="consts")
 
         def make_consts():
-            ident = keep.tile([P, P], F32, name="ident", tag="w4_raw0")
-            make_identity(nc, ident[:])
             rows = keep.tile([P, PACK, P], F32, name="rows", tag="both_sc", align_bytes=64)
             nc.gpsimd.memset(rows[:], 0.0)
             nc.scalar.copy(
@@ -297,14 +318,18 @@ def tile_list_place_field_atlas_kernel(
                 x = keep.tile([P, M], F32, name="x%d" % s, tag="x%d" % (s % 4 if s == 6 else s % 3), align_bytes=64)
             b, t = divmod(s, PACK)
             gain_t = consts[:, t, PASSES + b : PASSES + b + 1]
-            nc.vector.tensor_copy(x[:], pages[s][:].indirect(idx3[:]))
+            step = BANK if s == LAST - 1 else M
+            for lo in range(0, M, step):
+                nc.vector.tensor_copy(x[:, lo : lo + step], pages[s][:].indirect(entries(idx3, lo, lo + step)))
             if s < PACK:
                 y = keep.tile([P, M], F32, name="y%d" % s, tag="y")
             elif s < LAST - 1:
                 y = late.tile([P, M], F32, name="y%d" % s, offset=4 * ROW, align_bytes=64)
             else:
                 y = tail.tile([P, M], F32, name="y", offset=0, align_bytes=64)
-            nc.scalar.activation(y[:], x[:], ACT.Square, bias=consts[:, t, b : b + 1], scale=-1.0)
+            for lo in range(0, M, step):
+                cols = slice(lo, lo + step)
+                nc.scalar.activation(y[:, cols], x[:, cols], ACT.Square, bias=consts[:, t, b : b + 1], scale=-1.0)
             nc.scalar.activation(y[:], y[:], ACT.Exp, scale=-0.25)
             if s == LAST - 1:
                 for k in range(CHUNKS):

@@ -25,15 +25,15 @@ LAST = SLICES - 1
 QUADRANTS = 4
 RUN = 4
 BANK = 512
-BANKS = 8
 PER_COLUMN = 16
 CHUNK = 256
 CHUNKS = M // CHUNK
 ROW = 4 * M
 LEAD = 256
-FIRST_LEAD = 512
-BULK = T2 - BANK
 W4_WORDS = BANK // 2
+SLOT = 2 * ROW
+SLOTS = 3
+OVERLAP = 64
 
 
 def tile_list_place_field_atlas_kernel(
@@ -43,8 +43,7 @@ def tile_list_place_field_atlas_kernel(
     with ExitStack() as ctx:
         lists = ctx.enter_context(tc.tile_pool(name="lists", bufs=1))
         keep = ctx.enter_context(tc.tile_pool(name="keep", bufs=1))
-        late = ctx.enter_context(tc.tile_pool(name="late", bufs=1))
-        tail = ctx.enter_context(tc.tile_pool(name="tail", bufs=1))
+        ring = ctx.enter_context(tc.tile_pool(name="ring", bufs=1))
         psum = ctx.enter_context(tc.psum_pool(name="psum", bufs=1))
 
         idx = lists.tile([P, S // PER_COLUMN], U16, name="idx")
@@ -54,59 +53,95 @@ def tile_list_place_field_atlas_kernel(
         def entries(offsets, lo, hi):
             return offsets[:, lo // PER_COLUMN : hi // PER_COLUMN]
 
-        tab_sc = keep.tile([P, T], U8, name="tab_sc", align_bytes=64)
-        w4s_raw = [keep.tile([32, BANK], U8, name="w4s_raw%d" % b, align_bytes=64) for b in range(PASSES)]
-        w4s_src = w4_scales.rearrange("a q c -> q a c").bitcast(I32)
-        widths = (BANK + P, BANK + 3 * P, BANK)
-        planes = [keep.tile([P, PASSES, w], U8, name="planes%d" % c, align_bytes=64) for c, w in enumerate(widths)]
+        def kept(name, shape, dtype, tag=""):
+            return keep.tile([P] + shape, dtype, name=name, tag=tag or name, align_bytes=64)
 
-        def v_plane(a, lo, hi):
-            return planes[0][:, a, lo:hi] if lo < BANK else planes[1][:, a, lo - P : hi - P]
+        def placed(name, shape, dtype, offset):
+            return ring.tile([P] + shape, dtype, name=name, offset=offset, align_bytes=64)
 
-        def w4_plane(a, s):
-            c, lo = (0, BANK) if s == 0 else (1, P * (s - 1)) if s < PACK else (2, P * (s - PACK))
-            return planes[c][:, a, lo : lo + P]
+        def bank(name, shape, number):
+            return psum.tile([P] + shape, F32, name=name, tag="bank%d" % number)
 
-        def load_w4_scales(b):
-            nc.sync.dma_start(w4s_raw[b][:].bitcast(I32), w4s_src[:, :, P * b : P * (b + 1)])
+        def slot(s):
+            return SLOT * (s % SLOTS)
 
+        def curve_at(s):
+            return SLOT * SLOTS + ROW * s
+
+        tab_sc = kept("tab_sc", [T], U8)
+        w4s_raw = [kept("w4s_raw%d" % b, [PASSES, BANK], U8) for b in range(PASSES)]
+        v_plane = [kept("v_plane%d" % c, [PASSES, BANK], U8) for c in range(2)]
+        w4_plane = {}
+        nc.vector.memset(w4s_raw[0][:].bitcast(I32), 0)
         nc.vector.memset(tab_sc[32:64, :].bitcast(I32), 0)
         nc.vector.memset(tab_sc[64:128, :].bitcast(I32), 0)
-        wg0_rows = keep.tile([P, S // 4], F32, name="wg0_rows", tag="x1", align_bytes=64)
         ident = keep.tile([P, P], F32, name="ident")
         make_identity(nc, ident[:])
-        nc.gpsimd.memset(planes[0][:].bitcast(I32), 0)
-        load_w4_scales(0)
+        for plane in (v_plane[0], v_plane[1], w4s_raw[1]):
+            nc.gpsimd.memset(plane[:].bitcast(I32), 0)
+        rows = kept("rows", [PACK, P], F32)
+        nc.gpsimd.memset(rows[:], 0.0)
+
         nc.sync.dma_start(idx[:], offs)
         nc.sync.dma_start(tab_sc[0:32, :].bitcast(I32), tab_scales.rearrange("a q t -> q a t").bitcast(I32))
-
+        wg0_rows = placed("wg0_rows", [S // 4], F32, curve_at(SLICES) + BANK)
         nc.sync.dma_start(wg0_rows[:], wgs.rearrange("(x t y) (c s) -> t (y c) x s", t=PACK, y=RUN, c=4)[0])
-        w4_raw = {}
+
+        tab_w, w4_raw, w4_w = {}, {}, {}
         w4_src = w4_words.rearrange("a p c -> p a c").bitcast(I32)
 
+        def load_table(a):
+            tab_w[a] = kept("tab_w%d" % a, [T], I32)
+            nc.sync.dma_start(tab_w[a][:], tab_words[a].rearrange("p t i -> p (t i)").bitcast(I32))
+
         def load_w4(b):
-            w4_raw[b] = keep.tile([P, PASSES, W4_WORDS], I32, name="w4_raw%d" % b, tag="w4_raw%d" % b)
+            w4_raw[b] = kept("w4_raw%d" % b, [PASSES, W4_WORDS], I32)
             nc.sync.dma_start(w4_raw[b][:], w4_src[:, :, W4_WORDS * b : W4_WORDS * (b + 1)])
 
-        page_src = page0.rearrange("(b x t y) c -> b t x y c", b=PASSES, t=PACK, y=RUN)
-        pages = [keep.tile([P, T2], F32, name="page%d" % s, tag="page%d" % s, align_bytes=64) for s in range(SLICES)]
+        w4s_src = w4_scales.rearrange("a q c -> q a c").bitcast(I32)
 
-        def load_page(s, lo=0, hi=T2):
+        def load_w4_scales(b):
+            for q in (0, 2, 1, 3):
+                nc.sync.dma_start(
+                    w4s_raw[b][32 * q : 32 * q + 4, :, :].bitcast(I32), w4s_src[4 * q : 4 * q + 4, :, P * b : P * (b + 1)]
+                )
+
+        def order_w4(b):
+            w4_plane[b] = placed("w4_plane%d" % b, [PASSES, BANK], U8, curve_at(SLICES + b))
+            nc.scalar.copy(
+                w4_plane[b][:].bitcast(U32).rearrange("p a (t x) -> p a t x", t=PACK),
+                w4s_raw[b][:].bitcast(U32).rearrange("p a (x t) -> p a t x", t=PACK),
+            )
+            w4_w[b] = placed("w4_w%d" % b, [PASSES, PACK, 2 * P], U8, curve_at(SLICES + b) + PASSES * BANK)
+            for ts in (slice(0, 1), slice(1, PACK)) if b == 0 else (slice(0, PACK),):
+                nc.scalar.copy(
+                    w4_w[b][:].bitcast(U32).rearrange("p a t (x e) -> p a t x e", e=2)[:, :, ts],
+                    w4_raw[b][:].bitcast(U32).rearrange("p a (x t e) -> p a t x e", t=PACK, e=2)[:, :, ts],
+                )
+
+        def carry(plane, scale_rows):
+            for q in (0, 2, 1, 3):
+                nc.sync.dma_start(plane[32 * q : 32 * q + 4, :, :].bitcast(I32), scale_rows[8 * q : 8 * q + 8, :].bitcast(I32))
+
+        page_src = page0.rearrange("(b x t y) c -> b t x y c", b=PASSES, t=PACK, y=RUN)
+        pages = [kept("page%d" % s, [T2], F32) for s in range(SLICES)]
+
+        def load_page(s):
             b, t = divmod(s, PACK)
-            nc.sync.dma_start(pages[s][:, lo:hi], page_src[b, t][:, :, lo:hi])
+            nc.sync.dma_start(pages[s][:], page_src[b, t])
 
         wgs_src = wgs.rearrange("(x t y) s -> t x y s", t=PACK, y=RUN)
-        wg = [keep.tile([P, S], F32, name="wg%d" % t, align_bytes=64) for t in range(PACK)]
+        wg = [kept("wg%d" % t, [S], F32) for t in range(PACK)]
 
-        def load_wgs(t, lo, hi, quadrants):
-            for q in quadrants:
+        def load_wgs(t, lo, hi):
+            for q in (0, 2, 1, 3):
                 nc.sync.dma_start(wg[t][32 * q : 32 * (q + 1), lo:hi], wgs_src[t][:, :, lo:hi])
 
         def spread_wg0():
-            across = psum.tile([P, 2, P], F32, name="across", tag="bank4")
+            across = bank("across", [2, P], 6)
             for i in range(2):
                 nc.tensor.transpose(across[:, i, :], wg0_rows[:, P * i : P * (i + 1)], ident[:])
-            fourfold = keep.tile([P, 4, 2, QUADRANTS, 32], F32, name="fourfold", tag="x0", align_bytes=64)
+            fourfold = kept("fourfold", [4, 2, QUADRANTS, 32], F32)
             for i in range(2):
                 nc.scalar.copy(
                     fourfold[:, :, i, :, :].rearrange("p c q (x y) -> p c q x y", y=RUN),
@@ -116,342 +151,254 @@ def tile_list_place_field_atlas_kernel(
                     .to_broadcast([P, 4, QUADRANTS, 8, RUN]),
                 )
             for half in range(2):
-                back = psum.tile([P, 4, P], F32, name="back", tag="bank%d" % (5 + half))
+                back = bank("back", [4, P], (7, 4)[half])
                 for n in range(4):
                     c, i = divmod(4 * half + n, 2)
                     nc.tensor.transpose(back[:, n, :], fourfold[:, c, i, :, :].rearrange("p q u -> p (q u)"), ident[:])
                 nc.scalar.copy(wg[0][:, BANK * half : BANK * (half + 1)], back[:].rearrange("p n j -> p (n j)"))
 
         spread_wg0()
-        tab_w = {}
-
-        def load_table(a):
-            tab_w[a] = keep.tile([P, T], I32, name="tab_w%d" % a, tag="tab_w%d" % a, align_bytes=64)
-            nc.sync.dma_start(tab_w[a][:], tab_words[a].rearrange("p t i -> p (t i)").bitcast(I32))
-
-        nc.gpsimd.memset(planes[1][:].bitcast(I32), 0)
-        nc.gpsimd.memset(planes[2][:].bitcast(I32), 0)
-        load_w4(0)
         load_table(0)
-        nc.sync.dma_start(idx2[:], offs2)
+        load_w4_scales(0)
         load_table(1)
+        load_w4(0)
+        order_w4(0)
 
-        v_sc = keep.tile([P, S], U8, name="v_sc", align_bytes=64)
-        both_sc = keep.tile([32, S + BANK], U8, name="both_sc", tag="both_sc", align_bytes=64)
-        late_sc = keep.tile([32, BANK], U8, name="late_sc", align_bytes=64)
-        w4_w = [keep.tile([P, PASSES, PACK, 2 * P], U8, name="w4_w%d" % b, align_bytes=64) for b in range(PASSES)]
-
-        def order_w4_words(b):
-            nc.vector.tensor_copy(
-                w4_w[b][:].bitcast(I32).rearrange("p a t (x e) -> p a x t e", e=2),
-                w4_raw[b][:].rearrange("p a (x t e) -> p a x t e", t=PACK, e=2),
-            )
-
-        def order_w4_scales(b, dst):
-            nc.vector.tensor_copy(
-                dst.bitcast(I32).rearrange("p (t x) -> p x t", t=PACK),
-                w4s_raw[b][:].bitcast(I32).rearrange("p (x t) -> p x t", t=PACK),
-            )
-
-        order_w4_scales(0, both_sc[:, BANK : 2 * BANK])
+        v_sc = kept("v_sc", [S], U8)
         for c in range(2):
             cols = slice(BANK * c, BANK * (c + 1))
             nc.vector.tensor_copy(v_sc[:, cols], tab_sc[:].indirect(entries(idx, cols.start, cols.stop)))
-        nc.vector.tensor_copy(both_sc[:, :BANK].bitcast(I32), v_sc[0:32, :BANK].bitcast(I32))
-        order_w4_words(0)
-        nc.vector.tensor_copy(both_sc[:, 2 * BANK :].bitcast(I32), v_sc[0:32, BANK:].bitcast(I32))
-
-        def carry_scales(c):
-            rows_sc = (both_sc[:, : widths[0]], both_sc[:, widths[0] :], late_sc[:])[c]
-            for q in (0, 2, 1, 3):
-                nc.sync.dma_start(
-                    planes[c][32 * q : 32 * q + 4, :, :].bitcast(I32), rows_sc[8 * q : 8 * q + 8, :].bitcast(I32)
-                )
-
-        carry_scales(0)
-        v_w = [keep.tile([P, S], U32, name="v_w%d" % a, align_bytes=64) for a in range(PASSES)]
+        carry(v_plane[0], v_sc[:, :BANK])
+        v_w = [kept("v_w%d" % a, [S], U32) for a in range(PASSES)]
 
         def gather_words(a, lo, hi):
             nc.vector.tensor_copy(v_w[a][:, lo:hi], tab_w[a][:].bitcast(U32).indirect(entries(idx, lo, hi)))
 
-        gather_words(0, 0, S)
+        gather_words(0, 0, S - LEAD)
         gather_words(1, 0, LEAD)
         gather_words(1, LEAD, BANK)
         gather_words(1, BANK, S)
+        gather_words(0, S - LEAD, S)
 
         wd_src = wd.rearrange("(b x t y) n -> b t x y n", b=PASSES, t=PACK, y=RUN)
-        wd_raw = [keep.tile([P, PACK, N], F32, name="wd_raw%d" % b, tag="tab_w%d" % b, align_bytes=64) for b in range(PASSES)]
-        load_page(0)
-        load_w4_scales(1)
-        carry_scales(1)
-        load_page(1)
+        wd_raw = [placed("wd_raw0", [PACK, N], F32, slot(1)), kept("wd_raw1", [PACK, N], F32, tag="tab_w1")]
         vecs = keep.tile([2 * PASSES, BANK], F32, name="vecs")
-        load_wgs(1, 0, FIRST_LEAD, range(QUADRANTS))
-        nc.sync.dma_start(idx3[:], offs3)
-        load_w4(1)
-        order_w4_scales(1, late_sc[:])
-        carry_scales(2)
-        order_w4_words(1)
-        for s in (1, 2):
-            load_page(s + 1)
-            load_wgs(s + 1, 0, FIRST_LEAD, range(QUADRANTS - 1))
-            load_wgs(s, FIRST_LEAD, S, range(QUADRANTS))
-            load_wgs(s + 1, 0, FIRST_LEAD, [QUADRANTS - 1])
-            if s == 1:
-                for i, vec in enumerate((pref, gain)):
-                    nc.sync.dma_start(vecs[PASSES * i : PASSES * (i + 1), :], vec.rearrange("(b r) -> b r", b=PASSES))
-        for b in range(PASSES):
+
+        def load_wd(b):
             for t in range(PACK):
                 nc.sync.dma_start(wd_raw[b][:, t, :], wd_src[b, t])
-        load_page(4, 0, BULK)
-        load_page(5, 0, BULK)
-        load_wgs(3, FIRST_LEAD, S, range(QUADRANTS))
-        load_page(4, BULK, T2)
-        load_page(5, BULK, T2)
+
+        nc.sync.dma_start(idx2[:], offs2)
+        load_page(0)
+        carry(v_plane[1], v_sc[:, BANK:])
+        load_page(1)
+        load_wgs(1, 0, LEAD)
+        nc.sync.dma_start(idx3[:], offs3)
+        load_wgs(1, LEAD, S)
+        load_w4_scales(1)
+        load_w4(1)
+        load_wgs(2, 0, S)
+        for i, vec in enumerate((pref, gain)):
+            nc.sync.dma_start(vecs[PASSES * i : PASSES * (i + 1), :], vec.rearrange("(b r) -> b r", b=PASSES))
+        load_page(2)
+        load_wgs(3, 0, S)
+        load_wd(0)
+        load_page(3)
+        load_page(4)
+        load_page(5)
+        load_wd(1)
         load_page(6)
         load_page(7)
 
         consts = keep.tile([P, PACK, 2 * PASSES], F32, name="consts")
 
         def make_consts():
-            rows = keep.tile([P, PACK, P], F32, name="rows", tag="both_sc", align_bytes=64)
-            nc.gpsimd.memset(rows[:], 0.0)
             nc.scalar.copy(
                 rows[0 : 2 * PASSES].rearrange("p t (x y) -> p t x y", y=RUN),
                 vecs[:].rearrange("p (x t y) -> p t x y", t=PACK, y=RUN),
             )
-            turned = psum.tile([P, PACK, P], F32, name="turned", tag="bank3")
+            turned = bank("turned", [PACK, P], 6)
             for t in range(PACK):
                 nc.tensor.transpose(turned[:, t, :], rows[:, t, :], ident[:])
             nc.scalar.copy(consts[:], turned[:, :, 0 : 2 * PASSES])
 
-        h, acc = {}, {}
+        acc = {}
+
+        def passes(dst, s, lo, hi):
+            b, t = divmod(s, PACK)
+            c = lo // BANK
+            for a in range(PASSES):
+                nc.tensor.matmul_mx(
+                    out=dst,
+                    lhsT=w4_w[b][:, a, t, :].bitcast(FP4X4),
+                    lhsT_scale=w4_plane[b][:, a, P * t : P * (t + 1)],
+                    rhs=v_w[a][:, lo:hi].bitcast(FP8X4),
+                    rhs_scale=v_plane[c][:, a, lo - BANK * c : hi - BANK * c],
+                    start=(a == 0),
+                    stop=(a == PASSES - 1),
+                )
 
         def project(s):
-            b, t = divmod(s, PACK)
             for c in range(s == 0, 2):
-                acc[s, c] = psum.tile([P, BANK], F32, name="acc", tag="bank%d" % ((2 * s + c) % BANKS))
-                for a in range(PASSES):
-                    nc.tensor.matmul_mx(
-                        out=acc[s, c][:],
-                        lhsT=w4_w[b][:, a, t, :].bitcast(FP4X4),
-                        lhsT_scale=w4_plane(a, s),
-                        rhs=v_w[a][:, BANK * c : BANK * (c + 1)].bitcast(FP8X4),
-                        rhs_scale=v_plane(a, BANK * c, BANK * (c + 1)),
-                        start=(a == 0),
-                        stop=(a == PASSES - 1),
-                    )
-                if s == 0:
-                    h[s, c] = keep.tile([P, BANK], F32, name="h0%d" % c, tag="h0%d" % c, align_bytes=64)
-                    nc.scalar.copy(h[s, c][:], acc[s, c][:])
-                elif s < LAST - 1:
-                    if c == 0:
-                        h[s] = keep.tile([P, S], F32, name="h%d" % s, tag="h%d" % s, align_bytes=64)
-                    nc.scalar.copy(h[s][:, BANK * c : BANK * (c + 1)], acc[s, c][:])
+                acc[s, c] = bank("acc", [BANK], 2 * (s % 3) + c)
+                passes(acc[s, c][:], s, BANK * c, BANK * (c + 1))
 
-        def project_first():
-            h[0, 0] = keep.tile([P, BANK], F32, name="h00", tag="h00", align_bytes=64)
-            for quarter in range(2):
-                first = psum.tile([P, BANK], F32, name="first", tag="bank%d" % (0, BANKS - 1)[quarter])
-                for a in range(PASSES):
-                    for i in range(2):
-                        lo = LEAD * quarter + P * i
-                        nc.tensor.matmul_mx(
-                            out=first[:, P * i : P * (i + 1)],
-                            lhsT=w4_w[0][:, a, 0, :].bitcast(FP4X4),
-                            lhsT_scale=w4_plane(a, 0),
-                            rhs=v_w[a][:, lo : lo + P].bitcast(FP8X4),
-                            rhs_scale=v_plane(a, lo, lo + P),
-                            start=(a == 0 and i == 0),
-                            stop=(a == PASSES - 1 and i == 1),
-                        )
-                nc.scalar.copy(h[0, 0][:, LEAD * quarter : LEAD * (quarter + 1)], first[:, :LEAD])
+        def copy_h(dst, s, lo, hi):
+            for c in range(lo // BANK, (hi - 1) // BANK + 1):
+                first, last = max(lo, BANK * c), min(hi, BANK * (c + 1))
+                nc.scalar.copy(dst[:, first - lo : last - lo], acc[s, c][:, first - BANK * c : last - BANK * c])
 
-        project_first()
+        def scatter(s, values, lo, hi):
+            nc.vector.tensor_tensor(pages[s][:].indirect(entries(idx2, lo, hi)), values, wg[s % PACK][:, lo:hi], MULT)
+
+        h0 = [kept("h0%d" % c, [BANK], F32) for c in range(2)]
+        for quarter in range(2):
+            first = bank("first", [BANK], (0, 5)[quarter])
+            passes(first[:, :LEAD], 0, LEAD * quarter, LEAD * (quarter + 1))
+            nc.scalar.copy(h0[0][:, LEAD * quarter : LEAD * (quarter + 1)], first[:, :LEAD])
+        scatter(0, h0[0][:], 0, BANK)
         project(0)
+        copy_h(h0[1], 0, BANK, S)
+        scatter(0, h0[1][:], BANK, S)
         project(1)
-        make_consts()
+        h1 = kept("h1", [S], F32)
+        copy_h(h1, 1, 0, S)
+        scatter(1, h1[:, :LEAD], 0, LEAD)
         project(2)
         project(3)
+        order_w4(1)
+        project(4)
+        make_consts()
 
-        wd_q, wd_woven = {}, {}
-        wd_s = [keep.tile([P, N], U8, name="wd_s%d" % b, align_bytes=64) for b in range(PASSES)]
+        woven0 = kept("woven0", [M, PACK], BF16)
+        woven = [kept("woven1%d" % k, [CHUNK, PACK], BF16) for k in range(CHUNKS)]
+        spans = [(CHUNK * k, CHUNK * (k + 1)) for k in range(CHUNKS)]
+        wd_woven, wd_q, z_q, res = {}, {}, {}, {}
+        wd_s = [kept("wd_s%d" % b, [N], U8) for b in range(PASSES)]
+        z_s = [kept("z_s%d" % b, [M], U8) for b in range(PASSES)]
 
-        def weave_wd(b):
-            wd_woven[b] = keep.tile([P, N, PACK], BF16, name="wd_woven%d" % b, align_bytes=64)
-            if b == 0:
-                nc.scalar.copy(
-                    wd_woven[b][:].rearrange("p (i j n) t -> p j i n t", i=2, j=2),
-                    wd_raw[b][:].rearrange("p t (j i n) -> p j i n t", i=2, j=2),
-                )
-            else:
-                nc.scalar.copy(wd_woven[b][:], wd_raw[b][:].rearrange("p t n -> p n t"))
+        def pref_of(s):
+            b, t = divmod(s, PACK)
+            return consts[:, t, b : b + 1]
+
+        def gain_of(s):
+            b, t = divmod(s, PACK)
+            return consts[:, t, PASSES + b : PASSES + b + 1]
+
+        def weave_wd(b, offset):
+            wd_woven[b] = placed("wd_woven%d" % b, [N, PACK], BF16, offset)
+            nc.scalar.copy(wd_woven[b][:], wd_raw[b][:].rearrange("p t n -> p n t"))
 
         def quantise_wd(b, j, codes):
             cols = slice(2 * P * j, 2 * P * (j + 1))
             wd_q[b, j] = codes
             nc.vector.quantize_mx(
-                out=wd_q[b, j][:].bitcast(FP8X4),
-                scales=wd_s[b][:, cols],
-                in_=wd_woven[b][:, cols, :].rearrange("p n t -> p (n t)"),
+                out=codes[:].bitcast(FP8X4), scales=wd_s[b][:, cols], in_=wd_woven[b][:, cols, :].rearrange("p n t -> p (n t)")
             )
-
-        z_held = late.tile([P, 10 * M], BF16, name="z_rows0", offset=0, align_bytes=64)
-        z_rows = [
-            z_held[:, : PACK * M].rearrange("p (t m) -> p t m", t=PACK),
-            tail.tile([P, 2, M], BF16, name="z_rows1", offset=0, align_bytes=64),
-        ]
-        z_woven = keep.tile([P, M, PACK], BF16, name="z_woven", align_bytes=64)
-        woven = [keep.tile([P, CHUNK, PACK], BF16, name="woven%d" % k, align_bytes=64) for k in range(CHUNKS)]
-        spans = [(CHUNK * k, CHUNK * (k + 1)) for k in range(CHUNKS)]
-        z_q = {}
-        z_s = [keep.tile([P, M], U8, name="z_s%d" % b, align_bytes=64) for b in range(PASSES)]
-        res = {}
-
-        def scatter(s, values, lo, hi):
-            nc.vector.tensor_tensor(pages[s][:].indirect(entries(idx2, lo, hi)), values, wg[s % PACK][:, lo:hi], MULT)
-
-        def tune(s):
-            if s == PACK + 1:
-                x = late.tile([P, M], F32, name="x%d" % s, offset=2 * ROW, align_bytes=64)
-            else:
-                x = keep.tile([P, M], F32, name="x%d" % s, tag="x%d" % (s % 4 if s == 6 else s % 3), align_bytes=64)
-            b, t = divmod(s, PACK)
-            gain_t = consts[:, t, PASSES + b : PASSES + b + 1]
-            step = BANK if s == LAST - 1 else M
-            for lo in range(0, M, step):
-                nc.vector.tensor_copy(x[:, lo : lo + step], pages[s][:].indirect(entries(idx3, lo, lo + step)))
-            if s < PACK:
-                y = keep.tile([P, M], F32, name="y%d" % s, tag="y")
-            elif s < LAST - 1:
-                y = late.tile([P, M], F32, name="y%d" % s, offset=4 * ROW, align_bytes=64)
-            else:
-                y = tail.tile([P, M], F32, name="y", offset=0, align_bytes=64)
-            for lo in range(0, M, step):
-                cols = slice(lo, lo + step)
-                nc.scalar.activation(y[:, cols], x[:, cols], ACT.Square, bias=consts[:, t, b : b + 1], scale=-1.0)
-            nc.scalar.activation(y[:], y[:], ACT.Exp, scale=-0.25)
-            if s == LAST - 1:
-                for k in range(CHUNKS):
-                    nc.scalar.activation(woven[k][:, :, t], y[:, slice(*spans[k])], ACT.Copy, scale=gain_t)
-            else:
-                nc.scalar.activation(z_rows[b][:, t, :], y[:], ACT.Copy, scale=gain_t)
 
         def out_pass(k, nt, b):
-            half, part = divmod(nt, 2) if b == 1 else (nt % 2, nt // 2)
-            place = 2 * half + part
+            j, part = divmod(nt, 2)
             nc.tensor.matmul_mx(
-                out=res[k, nt // 2][:, nt % 2, :],
-                lhsT=wd_q[b, half][:, P * part : P * (part + 1)].bitcast(FP8X4),
-                lhsT_scale=wd_s[b][:, P * place : P * (place + 1)],
+                out=res[k, j][:, part, :],
+                lhsT=wd_q[b, j][:, P * part : P * (part + 1)].bitcast(FP8X4),
+                lhsT_scale=wd_s[b][:, P * nt : P * (nt + 1)],
                 rhs=z_q[b, k].bitcast(FP8X4),
                 rhs_scale=z_s[b][:, CHUNK * k : CHUNK * (k + 1)],
-                start=(b == 0 and nt % 2 == 0),
-                stop=(b == PASSES - 1 and nt % 2 == 1),
+                start=(b == 0 and part == 0),
+                stop=(b == PASSES - 1 and part == 1),
             )
 
-        def open_sums(j, chunks):
-            for k in chunks:
-                res[k, j] = psum.tile([P, 2, CHUNK], F32, name="res", tag="bank%d" % (2 * k + j))
+        def open_sums(j):
+            for k in range(CHUNKS):
+                res[k, j] = bank("res", [2, CHUNK], 2 * k + j)
                 out_pass(k, 2 * j, 0)
                 out_pass(k, 2 * j + 1, 0)
 
-        def quantise_z0(codes, lo, hi):
-            nc.vector.quantize_mx(
-                out=codes.bitcast(FP8X4), scales=z_s[0][:, lo:hi], in_=z_woven[:, lo:hi, :].rearrange("p m t -> p (m t)")
-            )
-
-        def late_tile(name, words, dtype, offset):
-            return late.tile([P, words], dtype, name=name, offset=offset, align_bytes=64)
-
-        scatter(0, h[0, 0][:], 0, BANK)
-        scatter(0, h[0, 1][:], BANK, S)
-        for s in range(PACK, SLICES):
-            project(s)
-        for s in range(1, LAST):
-            if s == LAST - 1:
-                z_q0 = late_tile("z_q0", M - CHUNK, U32, 3 * ROW)
-                for k in range(CHUNKS - 1):
+        rest = {1: h1[:, LEAD:]}
+        for s in range(LAST):
+            step = BANK if s == LAST - 1 else M
+            x = placed("x%d" % s, [M], F32, slot(s - 1))
+            for lo in range(0, M, step):
+                nc.vector.tensor_copy(x[:, lo : lo + step], pages[s][:].indirect(entries(idx3, lo, lo + step)))
+            if s < LAST - 1:
+                scatter(s + 1, rest[s + 1], LEAD, S)
+            else:
+                scatter(LAST, rest[LAST], 0, S - LEAD)
+                quantise_wd(0, 0, placed("wd_q00", [2 * P], U32, curve_at(s - 1) + 4 * LEAD))
+                scatter(LAST, end[:], S - LEAD, S)
+                open_sums(0)
+            squares = placed("squares%d" % s, [M], F32, slot(s) + OVERLAP)
+            for lo in range(0, M, step):
+                nc.scalar.activation(squares[:, lo : lo + step], x[:, lo : lo + step], ACT.Square, bias=pref_of(s), scale=-1.0)
+            if s + 2 < LAST:
+                lead = placed("lead%d" % (s + 2), [LEAD], F32, slot(s - 1))
+                copy_h(lead, s + 2, 0, LEAD)
+                scatter(s + 2, lead[:], 0, LEAD)
+            elif s + 2 == LAST:
+                z_q0 = placed("z_q0", [M], U32, curve_at(s - 1))
+                for k in range(CHUNKS):
                     z_q[0, k] = z_q0[:, slice(*spans[k])]
-                quantise_z0(z_q0[:, :BANK], 0, BANK)
-                quantise_z0(z_q0[:, BANK:], BANK, M - CHUNK)
-            lead = FIRST_LEAD if s < PACK else LEAD if s < LAST - 1 else 0
-            if lead:
-                scatter(s, h[s][:, :lead], 0, lead)
-            tune(s - 1)
-            scatter(s, h[s][:, lead:], lead, S)
-            if s == PACK - 1:
-                weave_wd(0)
-                weave_wd(1)
-            if s == PACK:
-                for lo in range(0, M, BANK):
-                    nc.scalar.copy(z_woven[:, lo : lo + BANK, :], z_rows[0][:, :, lo : lo + BANK].rearrange("p t m -> p m t"))
-                for later in (LAST - 1, LAST):
-                    h[later] = late_tile("h%d" % later, S, F32, ROW * (later - LAST + 1))
-                    for c in range(2):
-                        nc.scalar.copy(h[later][:, BANK * c : BANK * (c + 1)], acc[later, c][:])
-        for k in range(CHUNKS):
-            nc.scalar.copy(woven[k][:, :, 0:2], z_rows[1][:, :, slice(*spans[k])].rearrange("p t m -> p m t"))
-        quantise_wd(0, 1, keep.tile([P, 2 * P], U32, name="wd_q01", tag="page%d" % (LAST - 2), align_bytes=64))
-        tune(LAST - 1)
+                nc.vector.quantize_mx(out=z_q0[:].bitcast(FP8X4), scales=z_s[0][:], in_=woven0[:].rearrange("p m t -> p (m t)"))
+                quantise_wd(1, 0, placed("wd_q10", [2 * P], U32, slot(s - 1)))
+            else:
+                quantise_wd(0, 1, placed("wd_q01", [2 * P], U32, slot(s - 1)))
+                open_sums(1)
+            curve = placed("curve%d" % s, [M], F32, curve_at(s))
+            nc.scalar.activation(curve[:], squares[:], ACT.Exp, scale=-0.25)
+            if s + 2 <= LAST:
+                held = placed("rest%d" % (s + 2), [S - LEAD], F32, slot(s) + ROW)
+                lo = LEAD if s + 2 < LAST else 0
+                copy_h(held, s + 2, lo, lo + S - LEAD)
+                rest[s + 2] = held[:]
+            if s + 5 <= LAST:
+                project(s + 5)
+            if s < PACK:
+                nc.scalar.activation(woven0[:, :, s], curve[:], ACT.Copy, scale=gain_of(s))
+            else:
+                for k in range(CHUNKS):
+                    nc.scalar.activation(woven[k][:, :, s - PACK], curve[:, slice(*spans[k])], ACT.Copy, scale=gain_of(s))
+            if s in (0, 2):
+                weave_wd(s // 2, curve_at(s))
+            if s + 2 == LAST:
+                end = placed("end", [LEAD], F32, curve_at(s))
+                copy_h(end, LAST, S - LEAD, S)
 
-        scatter(LAST, h[LAST][:], 0, S)
-        curve = keep.tile([P, M], F32, name="curve")
-        x_chunk = [keep.tile([P, CHUNK], F32, name="x_chunk%d" % k) for k in range(CHUNKS)]
+        x_chunk = [placed("x_chunk%d" % k, [CHUNK], F32, curve_at(LAST - 1) + 4 * CHUNK * k) for k in range(CHUNKS)]
         unit = 4 * CHUNK
-
-        def gather_chunk(k):
+        starts = (unit - OVERLAP, 3 * unit, 0, 3 * unit)
+        squares = {}
+        curve = kept("curve", [M], F32)
+        for k in range(CHUNKS):
             nc.vector.tensor_copy(x_chunk[k][:], pages[LAST][:].indirect(entries(idx3, *spans[k])))
-
-        def curve_chunk(k):
-            units = 3 if k == 0 else 1
-            held = tail.tile([P, units, CHUNK], F32, name="squares%d" % k, offset=3 * unit * ((k + 1) % 2), align_bytes=64)
-            squares = held[:, 0, :]
-            nc.scalar.activation(squares, x_chunk[k][:], ACT.Square, bias=consts[:, PACK - 1, 1:2], scale=-1.0)
-            nc.scalar.activation(curve[:, slice(*spans[k])], squares, ACT.Exp, scale=-0.25)
+        for k in range(CHUNKS):
+            squares[k] = placed("square_chunk%d" % k, [CHUNK], F32, curve_at(LAST) + starts[k])
+            nc.scalar.activation(squares[k][:], x_chunk[k][:], ACT.Square, bias=pref_of(LAST), scale=-1.0)
+            nc.scalar.activation(curve[:, slice(*spans[k])], squares[k][:], ACT.Exp, scale=-0.25)
 
         def gain_chunk(k):
-            cols = slice(*spans[k])
-            gain_t = consts[:, PACK - 1, 2 * PASSES - 1 : 2 * PASSES]
-            nc.vector.tensor_scalar(woven[k][:, :, PACK - 1], curve[:, cols], gain_t, None, MULT)
+            nc.vector.tensor_scalar(woven[k][:, :, PACK - 1], curve[:, slice(*spans[k])], gain_of(LAST), None, MULT)
 
         def quantise_chunk(k):
-            z_q[1, k] = keep.tile([P, CHUNK], U32, name="z_q1%d" % k, align_bytes=64)[:]
+            z_q[1, k] = kept("z_q1%d" % k, [CHUNK], U32)[:]
             nc.vector.quantize_mx(
-                out=z_q[1, k].bitcast(FP8X4),
-                scales=z_s[1][:, slice(*spans[k])],
-                in_=woven[k][:].rearrange("p m t -> p (m t)"),
+                out=z_q[1, k].bitcast(FP8X4), scales=z_s[1][:, slice(*spans[k])], in_=woven[k][:].rearrange("p m t -> p (m t)")
             )
 
-        quantise_wd(0, 0, keep.tile([P, 2 * P], U32, name="wd_q00", tag="page%d" % (LAST - 1), align_bytes=64))
-        for k in range(CHUNKS - 1):
-            open_sums(0, [k])
-            open_sums(1, [k])
-        for k in range(CHUNKS):
-            gather_chunk(k)
-        for k in range(CHUNKS):
-            curve_chunk(k)
         gain_chunk(0)
-        quantise_wd(1, 0, tail.tile([P, 2 * P], U32, name="wd_q10", offset=unit * CHUNKS, align_bytes=64))
+        quantise_wd(1, 1, placed("wd_q11", [2 * P], U32, curve_at(LAST) + unit))
         quantise_chunk(0)
         gain_chunk(1)
-        quantise_wd(1, 1, tail.tile([P, 2 * P], U32, name="wd_q11", offset=unit * (CHUNKS + 1), align_bytes=64))
-        quantise_chunk(1)
         gain_chunk(2)
-        z_q[0, 3] = tail.tile([P, CHUNK], U32, name="z_q03", offset=3 * unit, align_bytes=64)[:]
-        quantise_z0(z_q[0, 3], M - CHUNK, M)
-        quantise_chunk(2)
+        quantise_chunk(1)
         gain_chunk(3)
+        quantise_chunk(2)
         quantise_chunk(3)
-        for j in range(2):
-            open_sums(j, [CHUNKS - 1])
         out_v = out.rearrange("(j i p) m -> j p i m", j=2, i=2)
         for k in range(CHUNKS):
             for j in range(2):
                 out_pass(k, 2 * j, 1)
                 out_pass(k, 2 * j + 1, 1)
-                tag = ("h00", "h01", "h1", "h2", "h3", "h4", "h5", "x0")[2 * k + j]
-                staged = keep.tile([P, 2, CHUNK], F32, name="staged%d%d" % (k, j), tag=tag, align_bytes=64)
+                staged = kept("staged%d%d" % (k, j), [2, CHUNK], F32, tag="page%d" % (2 * k + j))
                 if k >= 2 and j == 1:
                     nc.vector.tensor_copy(staged[:], res[k, j][:])
                 else:

@@ -287,7 +287,13 @@ def tile_list_place_field_atlas_kernel(
 
         def weave_wd(b, offset):
             wd_woven[b] = placed("wd_woven%d" % b, [N, PACK], BF16, offset)
-            nc.scalar.copy(wd_woven[b][:], wd_raw[b][:].rearrange("p t n -> p n t"))
+            if b == 0:
+                nc.scalar.copy(
+                    wd_woven[b][:].rearrange("p (i j n) t -> p j i n t", i=2, j=2),
+                    wd_raw[b][:].rearrange("p t (j i n) -> p j i n t", i=2, j=2),
+                )
+            else:
+                nc.scalar.copy(wd_woven[b][:], wd_raw[b][:].rearrange("p t n -> p n t"))
 
         def quantise_wd(b, j, codes):
             cols = slice(2 * P * j, 2 * P * (j + 1))
@@ -296,23 +302,29 @@ def tile_list_place_field_atlas_kernel(
                 out=codes[:].bitcast(FP8X4), scales=wd_s[b][:, cols], in_=wd_woven[b][:, cols, :].rearrange("p n t -> p (n t)")
             )
 
-        def out_pass(k, nt, b):
+        def out_pass(dst, k, nt, b, lo=0, hi=CHUNK):
             j, part = divmod(nt, 2)
+            half, place = (j, part) if b == 1 else (part, j)
             nc.tensor.matmul_mx(
-                out=res[k, j][:, part, :],
-                lhsT=wd_q[b, j][:, P * part : P * (part + 1)].bitcast(FP8X4),
-                lhsT_scale=wd_s[b][:, P * nt : P * (nt + 1)],
-                rhs=z_q[b, k].bitcast(FP8X4),
-                rhs_scale=z_s[b][:, CHUNK * k : CHUNK * (k + 1)],
+                out=dst[:, part, :],
+                lhsT=wd_q[b, half][:, P * place : P * (place + 1)].bitcast(FP8X4),
+                lhsT_scale=wd_s[b][:, P * (2 * half + place) : P * (2 * half + place + 1)],
+                rhs=z_q[b, k][:, lo:hi].bitcast(FP8X4),
+                rhs_scale=z_s[b][:, CHUNK * k + lo : CHUNK * k + hi],
                 start=(b == 0 and part == 0),
                 stop=(b == PASSES - 1 and part == 1),
             )
 
-        def open_sums(j):
-            for k in range(CHUNKS):
+        def quantise_z0(codes, lo, hi):
+            nc.vector.quantize_mx(
+                out=codes.bitcast(FP8X4), scales=z_s[0][:, lo:hi], in_=woven0[:, lo:hi, :].rearrange("p m t -> p (m t)")
+            )
+
+        def open_sums(j, chunks):
+            for k in chunks:
                 res[k, j] = bank("res", [2, CHUNK], 2 * k + j)
-                out_pass(k, 2 * j, 0)
-                out_pass(k, 2 * j + 1, 0)
+                out_pass(res[k, j], k, 2 * j, 0)
+                out_pass(res[k, j], k, 2 * j + 1, 0)
 
         rest = {1: h1[:, LEAD:]}
         for s in range(LAST):
@@ -324,9 +336,8 @@ def tile_list_place_field_atlas_kernel(
                 scatter(s + 1, rest[s + 1], LEAD, S)
             else:
                 scatter(LAST, rest[LAST], 0, S - LEAD)
-                quantise_wd(0, 0, placed("wd_q00", [2 * P], U32, curve_at(s - 1) + 4 * LEAD))
+                quantise_wd(0, 1, placed("wd_q01", [2 * P], U32, curve_at(s - 1) + 4 * LEAD))
                 scatter(LAST, end[:], S - LEAD, S)
-                open_sums(0)
             squares = placed("squares%d" % s, [M], F32, slot(s) + OVERLAP)
             for lo in range(0, M, step):
                 nc.scalar.activation(squares[:, lo : lo + step], x[:, lo : lo + step], ACT.Square, bias=pref_of(s), scale=-1.0)
@@ -335,14 +346,16 @@ def tile_list_place_field_atlas_kernel(
                 copy_h(lead, s + 2, 0, LEAD)
                 scatter(s + 2, lead[:], 0, LEAD)
             elif s + 2 == LAST:
-                z_q0 = placed("z_q0", [M], U32, curve_at(s - 1))
-                for k in range(CHUNKS):
+                z_q0 = placed("z_q0", [BANK], U32, curve_at(s - 1))
+                for k in range(2):
                     z_q[0, k] = z_q0[:, slice(*spans[k])]
-                nc.vector.quantize_mx(out=z_q0[:].bitcast(FP8X4), scales=z_s[0][:], in_=woven0[:].rearrange("p m t -> p (m t)"))
+                quantise_z0(z_q0[:], 0, BANK)
                 quantise_wd(1, 0, placed("wd_q10", [2 * P], U32, slot(s - 1)))
             else:
-                quantise_wd(0, 1, placed("wd_q01", [2 * P], U32, slot(s - 1)))
-                open_sums(1)
+                quantise_wd(0, 0, placed("wd_q00", [2 * P], U32, slot(s - 1)))
+                for k in range(2):
+                    open_sums(0, [k])
+                    open_sums(1, [k])
             curve = placed("curve%d" % s, [M], F32, curve_at(s))
             nc.scalar.activation(curve[:], squares[:], ACT.Exp, scale=-0.25)
             if s + 2 <= LAST:
@@ -363,44 +376,103 @@ def tile_list_place_field_atlas_kernel(
                 end = placed("end", [LEAD], F32, curve_at(s))
                 copy_h(end, LAST, S - LEAD, S)
 
-        x_chunk = [placed("x_chunk%d" % k, [CHUNK], F32, curve_at(LAST - 1) + 4 * CHUNK * k) for k in range(CHUNKS)]
         unit = 4 * CHUNK
-        starts = (unit - OVERLAP, 3 * unit, 0, 3 * unit)
-        squares = {}
+        pieces = {"0a": (0, P), "0b": (P, CHUNK), "1": spans[1], "2": spans[2], "3": spans[3], "3a": (M - CHUNK, M - P), "3b": (M - P, M)}
         curve = kept("curve", [M], F32)
-        for k in range(CHUNKS):
-            nc.vector.tensor_copy(x_chunk[k][:], pages[LAST][:].indirect(entries(idx3, *spans[k])))
-        for k in range(CHUNKS):
-            squares[k] = placed("square_chunk%d" % k, [CHUNK], F32, curve_at(LAST) + starts[k])
-            nc.scalar.activation(squares[k][:], x_chunk[k][:], ACT.Square, bias=pref_of(LAST), scale=-1.0)
-            nc.scalar.activation(curve[:, slice(*spans[k])], squares[k][:], ACT.Exp, scale=-0.25)
+        x_piece, squares = {}, {}
 
-        def gain_chunk(k):
-            nc.vector.tensor_scalar(woven[k][:, :, PACK - 1], curve[:, slice(*spans[k])], gain_of(LAST), None, MULT)
+        def gather_piece(name, offset):
+            lo, hi = pieces[name]
+            x_piece[name] = placed("x_piece" + name, [hi - lo], F32, offset)
+            nc.vector.tensor_copy(x_piece[name][:], pages[LAST][:].indirect(entries(idx3, lo, hi)))
 
-        def quantise_chunk(k):
-            z_q[1, k] = kept("z_q1%d" % k, [CHUNK], U32)[:]
+        def square_piece(name, offset, units):
+            lo, hi = pieces[name]
+            squares[name] = placed("squares_" + name, [units * CHUNK], F32, offset)[:, : hi - lo]
+            nc.scalar.activation(squares[name], x_piece[name][:], ACT.Square, bias=pref_of(LAST), scale=-1.0)
+
+        def exp_piece(name):
+            nc.scalar.activation(curve[:, slice(*pieces[name])], squares[name], ACT.Exp, scale=-0.25)
+
+        def gain_piece(name):
+            lo, hi = pieces[name]
+            k = lo // CHUNK
+            nc.vector.tensor_scalar(woven[k][:, lo - CHUNK * k : hi - CHUNK * k, PACK - 1], curve[:, lo:hi], gain_of(LAST), None, MULT)
+
+        def late_z0(k, offset):
+            z_q[0, k] = placed("z_q0%d" % k, [CHUNK], U32, offset)[:]
+            quantise_z0(z_q[0, k], *spans[k])
+
+        def quantise_chunk(k, codes, lo=0, hi=CHUNK):
+            z_q[1, k] = codes[:]
             nc.vector.quantize_mx(
-                out=z_q[1, k].bitcast(FP8X4), scales=z_s[1][:, slice(*spans[k])], in_=woven[k][:].rearrange("p m t -> p (m t)")
+                out=z_q[1, k][:, lo:hi].bitcast(FP8X4),
+                scales=z_s[1][:, CHUNK * k + lo : CHUNK * k + hi],
+                in_=woven[k][:, lo:hi, :].rearrange("p m t -> p (m t)"),
             )
 
-        gain_chunk(0)
-        quantise_wd(1, 1, placed("wd_q11", [2 * P], U32, curve_at(LAST) + unit))
-        quantise_chunk(0)
-        gain_chunk(1)
-        gain_chunk(2)
-        quantise_chunk(1)
-        gain_chunk(3)
-        quantise_chunk(2)
-        quantise_chunk(3)
+        here, there = slot(LAST - 1), slot(LAST) + unit
+        for name in ("0a", "0b", "1", "2"):
+            gather_piece(name, curve_at(LAST - 1) + 4 * pieces[name][0])
+        square_piece("0a", here, 1)
+        square_piece("0b", here + unit, 3)
+        exp_piece("0a")
+        exp_piece("0b")
+        square_piece("1", here, 1)
+        square_piece("2", here + 3 * unit, 1)
+        exp_piece("1")
+        exp_piece("2")
+        gain_piece("0a")
+        gain_piece("0b")
+        quantise_wd(1, 1, placed("wd_q11", [2 * P], U32, here + unit))
+        quantise_chunk(0, kept("z_q10", [CHUNK], U32))
+        gather_piece("3", here + 2 * unit)
+        square_piece("3", there, 1)
+        exp_piece("3")
+        gain_piece("1")
+        late_z0(2, here)
+        quantise_chunk(1, kept("z_q11", [CHUNK], U32))
+        gain_piece("2")
+        late_z0(3, here + 3 * unit)
+        quantise_chunk(2, kept("z_q12", [CHUNK], U32))
+        gain_piece("3a")
+        gain_piece("3b")
+        last_codes = kept("z_q13", [CHUNK], U32)
+        quantise_chunk(3, last_codes, 0, P)
+        quantise_chunk(3, last_codes, P, CHUNK)
         out_v = out.rearrange("(j i p) m -> j p i m", j=2, i=2)
+        staged = {}
         for k in range(CHUNKS):
             for j in range(2):
-                out_pass(k, 2 * j, 1)
-                out_pass(k, 2 * j + 1, 1)
-                staged = kept("staged%d%d" % (k, j), [2, CHUNK], F32, tag="page%d" % (2 * k + j))
-                if k >= 2 and j == 1:
-                    nc.vector.tensor_copy(staged[:], res[k, j][:])
-                else:
-                    nc.scalar.copy(staged[:], res[k, j][:])
-                nc.sync.dma_start(out_v[j][:, :, CHUNK * k : CHUNK * (k + 1)], staged[:])
+                staged[k, j] = kept("staged%d%d" % (k, j), [2, CHUNK], F32, tag="page%d" % (2 * k + j))
+
+        def empty(k, j, dst, src):
+            if k >= 2 and j == 1:
+                nc.vector.tensor_copy(dst, src)
+            else:
+                nc.scalar.copy(dst, src)
+
+        def store(k, j):
+            nc.sync.dma_start(out_v[j][:, :, CHUNK * k : CHUNK * (k + 1)], staged[k, j][:])
+
+        for k in range(CHUNKS - 1):
+            for j in range(2):
+                if k == 2:
+                    open_sums(j, [k])
+                out_pass(res[k, j], k, 2 * j, 1)
+                out_pass(res[k, j], k, 2 * j + 1, 1)
+                empty(k, j, staged[k, j][:], res[k, j][:])
+                store(k, j)
+        halves = {}
+        for h in range(2):
+            for j in range(2):
+                halves[h, j] = bank("half", [2, P], (6, 0)[h] + j)
+                for part in range(2):
+                    out_pass(halves[h, j], 3, 2 * j + part, 0, P * h, P * (h + 1))
+        for h in range(2):
+            for j in range(2):
+                for part in range(2):
+                    out_pass(halves[h, j], 3, 2 * j + part, 1, P * h, P * (h + 1))
+                empty(3, j, staged[3, j][:, :, P * h : P * (h + 1)], halves[h, j][:])
+        for j in range(2):
+            store(3, j)

@@ -33,6 +33,7 @@ LEAD = 256
 W4_WORDS = BANK // 2
 SLOT = 2 * ROW
 SLOTS = 3
+FIRST_PIECES = ((0, 256), (256, 384), (384, 512))
 OVERLAP = 64
 
 
@@ -163,6 +164,7 @@ def tile_list_place_field_atlas_kernel(
         load_table(1)
         load_w4(0)
         order_w4(0)
+        nc.sync.dma_start(idx2[:], offs2)
 
         v_sc = kept("v_sc", [S], U8)
         for c in range(2):
@@ -174,11 +176,10 @@ def tile_list_place_field_atlas_kernel(
         def gather_words(a, lo, hi):
             nc.vector.tensor_copy(v_w[a][:, lo:hi], tab_w[a][:].bitcast(U32).indirect(entries(idx, lo, hi)))
 
-        gather_words(0, 0, S - LEAD)
+        gather_words(0, 0, S)
         gather_words(1, 0, LEAD)
         gather_words(1, LEAD, BANK)
         gather_words(1, BANK, S)
-        gather_words(0, S - LEAD, S)
 
         wd_src = wd.rearrange("(b x t y) n -> b t x y n", b=PASSES, t=PACK, y=RUN)
         wd_raw = [placed("wd_raw0", [PACK, N], F32, slot(1)), kept("wd_raw1", [PACK, N], F32, tag="tab_w1")]
@@ -188,7 +189,6 @@ def tile_list_place_field_atlas_kernel(
             for t in range(PACK):
                 nc.sync.dma_start(wd_raw[b][:, t, :], wd_src[b, t])
 
-        nc.sync.dma_start(idx2[:], offs2)
         load_page(0)
         carry(v_plane[1], v_sc[:, BANK:])
         load_page(1)
@@ -240,7 +240,7 @@ def tile_list_place_field_atlas_kernel(
 
         def project(s):
             for c in range(s == 0, 2):
-                acc[s, c] = bank("acc", [BANK], 2 * (s % 3) + c)
+                acc[s, c] = bank("acc", [BANK], 2 * (s % 3) + (1 - c if s == 3 else c))
                 passes(acc[s, c][:], s, BANK * c, BANK * (c + 1))
 
         def copy_h(dst, s, lo, hi):
@@ -252,10 +252,10 @@ def tile_list_place_field_atlas_kernel(
             nc.vector.tensor_tensor(pages[s][:].indirect(entries(idx2, lo, hi)), values, wg[s % PACK][:, lo:hi], MULT)
 
         h0 = [kept("h0%d" % c, [BANK], F32) for c in range(2)]
-        for quarter in range(2):
-            first = bank("first", [BANK], (0, 5)[quarter])
-            passes(first[:, :LEAD], 0, LEAD * quarter, LEAD * (quarter + 1))
-            nc.scalar.copy(h0[0][:, LEAD * quarter : LEAD * (quarter + 1)], first[:, :LEAD])
+        for number, (lo, hi) in zip((0, 5, 6), FIRST_PIECES):
+            first = bank("first", [hi - lo], number)
+            passes(first[:], 0, lo, hi)
+            nc.scalar.copy(h0[0][:, lo:hi], first[:])
         scatter(0, h0[0][:], 0, BANK)
         project(0)
         copy_h(h0[1], 0, BANK, S)

@@ -302,17 +302,17 @@ def tile_list_place_field_atlas_kernel(
                 out=codes[:].bitcast(FP8X4), scales=wd_s[b][:, cols], in_=wd_woven[b][:, cols, :].rearrange("p n t -> p (n t)")
             )
 
-        def out_pass(dst, k, nt, b, lo=0, hi=CHUNK):
+        def out_pass(k, nt, b, alone=None):
             j, part = divmod(nt, 2)
             half, place = (j, part) if b == 1 else (part, j)
             nc.tensor.matmul_mx(
-                out=dst[:, part, :],
+                out=res[k, j][:, part, :] if alone is None else alone,
                 lhsT=wd_q[b, half][:, P * place : P * (place + 1)].bitcast(FP8X4),
                 lhsT_scale=wd_s[b][:, P * (2 * half + place) : P * (2 * half + place + 1)],
-                rhs=z_q[b, k][:, lo:hi].bitcast(FP8X4),
-                rhs_scale=z_s[b][:, CHUNK * k + lo : CHUNK * k + hi],
-                start=(b == 0 and part == 0),
-                stop=(b == PASSES - 1 and part == 1),
+                rhs=z_q[b, k].bitcast(FP8X4),
+                rhs_scale=z_s[b][:, CHUNK * k : CHUNK * (k + 1)],
+                start=(b == 0 and (part == 0 or alone is not None)),
+                stop=(b == PASSES - 1 and (part == 1 or alone is not None)),
             )
 
         def quantise_z0(codes, lo, hi):
@@ -322,9 +322,9 @@ def tile_list_place_field_atlas_kernel(
 
         def open_sums(j, chunks):
             for k in chunks:
-                res[k, j] = bank("res", [2, CHUNK], 2 * k + j)
-                out_pass(res[k, j], k, 2 * j, 0)
-                out_pass(res[k, j], k, 2 * j + 1, 0)
+                res[k, j] = bank("res", [2, CHUNK], 2 * (k % 2) + j)
+                out_pass(k, 2 * j, 0)
+                out_pass(k, 2 * j + 1, 0)
 
         rest = {1: h1[:, LEAD:]}
         for s in range(LAST):
@@ -376,103 +376,83 @@ def tile_list_place_field_atlas_kernel(
                 end = placed("end", [LEAD], F32, curve_at(s))
                 copy_h(end, LAST, S - LEAD, S)
 
+        x_chunk = [placed("x_chunk%d" % k, [CHUNK], F32, curve_at(LAST - 1) + 4 * CHUNK * k) for k in range(CHUNKS)]
         unit = 4 * CHUNK
-        pieces = {"0a": (0, P), "0b": (P, CHUNK), "1": spans[1], "2": spans[2], "3": spans[3], "3a": (M - CHUNK, M - P), "3b": (M - P, M)}
+        tail = curve_at(SLICES + 2)
+        starts = (0, unit, 2 * unit, 3 * unit)
+        units = (4, 1, 1, 6)
+        squares = {}
         curve = kept("curve", [M], F32)
-        x_piece, squares = {}, {}
+        for k in range(CHUNKS):
+            nc.vector.tensor_copy(x_chunk[k][:], pages[LAST][:].indirect(entries(idx3, *spans[k])))
 
-        def gather_piece(name, offset):
-            lo, hi = pieces[name]
-            x_piece[name] = placed("x_piece" + name, [hi - lo], F32, offset)
-            nc.vector.tensor_copy(x_piece[name][:], pages[LAST][:].indirect(entries(idx3, lo, hi)))
+        def square_chunk(k):
+            squares[k] = placed("square_chunk%d" % k, [units[k] * CHUNK], F32, tail + starts[k])[:, :CHUNK]
+            nc.scalar.activation(squares[k], x_chunk[k][:], ACT.Square, bias=pref_of(LAST), scale=-1.0)
 
-        def square_piece(name, offset, units):
-            lo, hi = pieces[name]
-            squares[name] = placed("squares_" + name, [units * CHUNK], F32, offset)[:, : hi - lo]
-            nc.scalar.activation(squares[name], x_piece[name][:], ACT.Square, bias=pref_of(LAST), scale=-1.0)
+        def exp_chunk(k):
+            nc.scalar.activation(curve[:, slice(*spans[k])], squares[k], ACT.Exp, scale=-0.25)
 
-        def exp_piece(name):
-            nc.scalar.activation(curve[:, slice(*pieces[name])], squares[name], ACT.Exp, scale=-0.25)
+        square_chunk(0)
+        exp_chunk(0)
+        square_chunk(1)
+        square_chunk(2)
+        exp_chunk(1)
+        square_chunk(3)
+        exp_chunk(2)
+        exp_chunk(3)
 
-        def gain_piece(name):
-            lo, hi = pieces[name]
-            k = lo // CHUNK
-            nc.vector.tensor_scalar(woven[k][:, lo - CHUNK * k : hi - CHUNK * k, PACK - 1], curve[:, lo:hi], gain_of(LAST), None, MULT)
+        def gain_chunk(k):
+            nc.vector.tensor_scalar(woven[k][:, :, PACK - 1], curve[:, slice(*spans[k])], gain_of(LAST), None, MULT)
 
         def late_z0(k, offset):
             z_q[0, k] = placed("z_q0%d" % k, [CHUNK], U32, offset)[:]
             quantise_z0(z_q[0, k], *spans[k])
 
-        def quantise_chunk(k, codes, lo=0, hi=CHUNK):
-            z_q[1, k] = codes[:]
+        def quantise_chunk(k):
+            if k == 2:
+                z_q[1, k] = placed("z_q1%d" % k, [CHUNK], U32, tail + starts[3] + 4 * unit)[:]
+            else:
+                z_q[1, k] = kept("z_q1%d" % k, [CHUNK], U32)[:]
             nc.vector.quantize_mx(
-                out=z_q[1, k][:, lo:hi].bitcast(FP8X4),
-                scales=z_s[1][:, CHUNK * k + lo : CHUNK * k + hi],
-                in_=woven[k][:, lo:hi, :].rearrange("p m t -> p (m t)"),
+                out=z_q[1, k].bitcast(FP8X4), scales=z_s[1][:, slice(*spans[k])], in_=woven[k][:].rearrange("p m t -> p (m t)")
             )
 
-        here, there = slot(LAST - 1), slot(LAST) + unit
-        for name in ("0a", "0b", "1", "2"):
-            gather_piece(name, curve_at(LAST - 1) + 4 * pieces[name][0])
-        square_piece("0a", here, 1)
-        square_piece("0b", here + unit, 3)
-        exp_piece("0a")
-        exp_piece("0b")
-        square_piece("1", here, 1)
-        square_piece("2", here + 3 * unit, 1)
-        exp_piece("1")
-        exp_piece("2")
-        gain_piece("0a")
-        gain_piece("0b")
-        quantise_wd(1, 1, placed("wd_q11", [2 * P], U32, here + unit))
-        quantise_chunk(0, kept("z_q10", [CHUNK], U32))
-        gather_piece("3", here + 2 * unit)
-        square_piece("3", there, 1)
-        exp_piece("3")
-        gain_piece("1")
-        late_z0(2, here)
-        quantise_chunk(1, kept("z_q11", [CHUNK], U32))
-        gain_piece("2")
-        late_z0(3, here + 3 * unit)
-        quantise_chunk(2, kept("z_q12", [CHUNK], U32))
-        gain_piece("3a")
-        gain_piece("3b")
-        last_codes = kept("z_q13", [CHUNK], U32)
-        quantise_chunk(3, last_codes, 0, P)
-        quantise_chunk(3, last_codes, P, CHUNK)
+        gain_chunk(0)
+        quantise_wd(1, 1, placed("wd_q11", [2 * P], U32, tail))
+        quantise_chunk(0)
+        gain_chunk(1)
+        late_z0(2, tail + starts[1])
+        quantise_chunk(1)
+        gain_chunk(2)
+        gain_chunk(3)
+        quantise_chunk(2)
+        late_z0(3, tail + starts[3] + 5 * unit)
+        quantise_chunk(3)
         out_v = out.rearrange("(j i p) m -> j p i m", j=2, i=2)
-        staged = {}
-        for k in range(CHUNKS):
-            for j in range(2):
-                staged[k, j] = kept("staged%d%d" % (k, j), [2, CHUNK], F32, tag="page%d" % (2 * k + j))
-
-        def empty(k, j, dst, src):
-            if k >= 2 and j == 1:
-                nc.vector.tensor_copy(dst, src)
-            else:
-                nc.scalar.copy(dst, src)
-
-        def store(k, j):
-            nc.sync.dma_start(out_v[j][:, :, CHUNK * k : CHUNK * (k + 1)], staged[k, j][:])
-
         for k in range(CHUNKS - 1):
+            if k >= 2:
+                open_sums(0, [k])
+                open_sums(1, [k])
             for j in range(2):
-                if k == 2:
-                    open_sums(j, [k])
-                out_pass(res[k, j], k, 2 * j, 1)
-                out_pass(res[k, j], k, 2 * j + 1, 1)
-                empty(k, j, staged[k, j][:], res[k, j][:])
-                store(k, j)
-        halves = {}
-        for h in range(2):
-            for j in range(2):
-                halves[h, j] = bank("half", [2, P], (6, 0)[h] + j)
-                for part in range(2):
-                    out_pass(halves[h, j], 3, 2 * j + part, 0, P * h, P * (h + 1))
-        for h in range(2):
-            for j in range(2):
-                for part in range(2):
-                    out_pass(halves[h, j], 3, 2 * j + part, 1, P * h, P * (h + 1))
-                empty(3, j, staged[3, j][:, :, P * h : P * (h + 1)], halves[h, j][:])
+                out_pass(k, 2 * j, 1)
+                out_pass(k, 2 * j + 1, 1)
+                if k == 0:
+                    staged = placed("staged0%d" % j, [2, CHUNK], F32, tail + starts[3] + 2 * unit * j)
+                else:
+                    staged = kept("staged%d%d" % (k, j), [2, CHUNK], F32, tag="page%d" % (2 * k + j))
+                if k >= 2 and j == 1:
+                    nc.vector.tensor_copy(staged[:], res[k, j][:])
+                else:
+                    nc.scalar.copy(staged[:], res[k, j][:])
+                nc.sync.dma_start(out_v[j][:, :, CHUNK * k : CHUNK * (k + 1)], staged[:])
+        k = CHUNKS - 1
+        single = [bank("single", [CHUNK], 4 + nt) for nt in range(4)]
         for j in range(2):
-            store(3, j)
+            staged = kept("staged%d%d" % (k, j), [2, CHUNK], F32, tag="page%d" % (2 * k + j))
+            for part in range(2):
+                for b in range(PASSES):
+                    out_pass(k, 2 * j + part, b, single[2 * j + part][:])
+            nc.scalar.copy(staged[:, 0, :], single[2 * j][:])
+            nc.vector.tensor_copy(staged[:, 1, :], single[2 * j + 1][:])
+            nc.sync.dma_start(out_v[j][:, :, CHUNK * k : CHUNK * (k + 1)], staged[:])

@@ -167,9 +167,7 @@ def tile_list_place_field_atlas_kernel(
         nc.sync.dma_start(idx2[:], offs2)
 
         v_sc = kept("v_sc", [S], U8)
-        for c in range(2):
-            cols = slice(BANK * c, BANK * (c + 1))
-            nc.vector.tensor_copy(v_sc[:, cols], tab_sc[:].indirect(entries(idx, cols.start, cols.stop)))
+        nc.vector.tensor_copy(v_sc[:], tab_sc[:].indirect(idx[:]))
         carry(v_plane[0], v_sc[:, :BANK])
         v_w = [kept("v_w%d" % a, [S], U32) for a in range(PASSES)]
 
@@ -270,11 +268,13 @@ def tile_list_place_field_atlas_kernel(
         project(4)
         make_consts()
 
-        woven0 = kept("woven0", [M, PACK], BF16)
+        joined = kept("joined", [M, PACK], BF16)
+        woven0 = kept("woven0", [BANK, PACK], BF16)
+        joined_s = kept("joined_s", [M], U8)
         woven = [kept("woven1%d" % k, [CHUNK, PACK], BF16) for k in range(CHUNKS)]
         spans = [(CHUNK * k, CHUNK * (k + 1)) for k in range(CHUNKS)]
         wd_woven, wd_q, z_q, res = {}, {}, {}, {}
-        wd_s = [kept("wd_s%d" % b, [N], U8) for b in range(PASSES)]
+        wd_s = {}
         z_s = [kept("z_s%d" % b, [M], U8) for b in range(PASSES)]
 
         def pref_of(s):
@@ -286,20 +286,21 @@ def tile_list_place_field_atlas_kernel(
             return consts[:, t, PASSES + b : PASSES + b + 1]
 
         def weave_wd(b, offset):
-            wd_woven[b] = placed("wd_woven%d" % b, [N, PACK], BF16, offset)
+            wd_woven[b] = placed("wd_woven%d" % b, [2 * P, PACK], BF16, offset)
+            early = joined[:, BANK + 2 * P * b : BANK + 2 * P * (b + 1), :]
             if b == 0:
-                nc.scalar.copy(
-                    wd_woven[b][:].rearrange("p (i j n) t -> p j i n t", i=2, j=2),
-                    wd_raw[b][:].rearrange("p t (j i n) -> p j i n t", i=2, j=2),
-                )
+                halves = wd_raw[b][:].rearrange("p t (j i n) -> p i j n t", i=2, j=2)
+                nc.scalar.copy(wd_woven[b][:].rearrange("p (j n) t -> p j n t", j=2), halves[:, 0])
+                nc.scalar.copy(early.rearrange("p (j n) t -> p j n t", j=2), halves[:, 1])
             else:
-                nc.scalar.copy(wd_woven[b][:], wd_raw[b][:].rearrange("p t n -> p n t"))
+                halves = wd_raw[b][:].rearrange("p t (j n) -> p j n t", j=2)
+                nc.scalar.copy(wd_woven[b][:], halves[:, 1])
+                nc.scalar.copy(early, halves[:, 0])
 
         def quantise_wd(b, j, codes):
-            cols = slice(2 * P * j, 2 * P * (j + 1))
-            wd_q[b, j] = codes
+            wd_q[b, j], wd_s[b, j] = codes, kept("wd_s%d" % b, [2 * P], U8)
             nc.vector.quantize_mx(
-                out=codes[:].bitcast(FP8X4), scales=wd_s[b][:, cols], in_=wd_woven[b][:, cols, :].rearrange("p n t -> p (n t)")
+                out=codes[:].bitcast(FP8X4), scales=wd_s[b, j][:], in_=wd_woven[b][:].rearrange("p n t -> p (n t)")
             )
 
         def out_pass(k, nt, b, alone=None):
@@ -308,36 +309,34 @@ def tile_list_place_field_atlas_kernel(
             nc.tensor.matmul_mx(
                 out=res[k, j][:, part, :] if alone is None else alone,
                 lhsT=wd_q[b, half][:, P * place : P * (place + 1)].bitcast(FP8X4),
-                lhsT_scale=wd_s[b][:, P * (2 * half + place) : P * (2 * half + place + 1)],
+                lhsT_scale=wd_s[b, half][:, P * place : P * (place + 1)],
                 rhs=z_q[b, k].bitcast(FP8X4),
-                rhs_scale=z_s[b][:, CHUNK * k : CHUNK * (k + 1)],
+                rhs_scale=(joined_s if b == 0 and k < 2 else z_s[b])[:, CHUNK * k : CHUNK * (k + 1)],
                 start=(b == 0 and (part == 0 or alone is not None)),
                 stop=(b == PASSES - 1 and (part == 1 or alone is not None)),
             )
 
         def quantise_z0(codes, lo, hi):
             nc.vector.quantize_mx(
-                out=codes.bitcast(FP8X4), scales=z_s[0][:, lo:hi], in_=woven0[:, lo:hi, :].rearrange("p m t -> p (m t)")
+                out=codes.bitcast(FP8X4), scales=z_s[0][:, lo:hi], in_=woven0[:, lo - BANK : hi - BANK, :].rearrange("p m t -> p (m t)")
             )
 
         def open_sums(j, chunks):
             for k in chunks:
-                res[k, j] = bank("res", [2, CHUNK], 2 * (k % 2) + j)
+                res[k, j] = bank("res", [2, CHUNK], 2 * k + j if k < 2 else (4, 0)[j])
                 out_pass(k, 2 * j, 0)
                 out_pass(k, 2 * j + 1, 0)
 
         rest = {1: h1[:, LEAD:]}
         for s in range(LAST):
-            step = BANK if s == LAST - 1 else M
+            step = M
             x = placed("x%d" % s, [M], F32, slot(s - 1))
             for lo in range(0, M, step):
                 nc.vector.tensor_copy(x[:, lo : lo + step], pages[s][:].indirect(entries(idx3, lo, lo + step)))
             if s < LAST - 1:
                 scatter(s + 1, rest[s + 1], LEAD, S)
             else:
-                scatter(LAST, rest[LAST], 0, S - LEAD)
-                quantise_wd(0, 1, placed("wd_q01", [2 * P], U32, curve_at(s - 1) + 4 * LEAD))
-                scatter(LAST, end[:], S - LEAD, S)
+                scatter(LAST, rest[LAST], 0, S)
             squares = placed("squares%d" % s, [M], F32, slot(s) + OVERLAP)
             for lo in range(0, M, step):
                 nc.scalar.activation(squares[:, lo : lo + step], x[:, lo : lo + step], ACT.Square, bias=pref_of(s), scale=-1.0)
@@ -346,11 +345,14 @@ def tile_list_place_field_atlas_kernel(
                 copy_h(lead, s + 2, 0, LEAD)
                 scatter(s + 2, lead[:], 0, LEAD)
             elif s + 2 == LAST:
-                z_q0 = placed("z_q0", [BANK], U32, curve_at(s - 1))
+                joined_q = placed("joined_q", [M], U32, curve_at(s - 1))
+                nc.vector.quantize_mx(
+                    out=joined_q[:].bitcast(FP8X4), scales=joined_s[:], in_=joined[:].rearrange("p m t -> p (m t)")
+                )
                 for k in range(2):
-                    z_q[0, k] = z_q0[:, slice(*spans[k])]
-                quantise_z0(z_q0[:], 0, BANK)
-                quantise_wd(1, 0, placed("wd_q10", [2 * P], U32, slot(s - 1)))
+                    z_q[0, k] = joined_q[:, slice(*spans[k])]
+                    cols = slice(*spans[2 + k])
+                    wd_q[k, 1 - k], wd_s[k, 1 - k] = joined_q[:, cols], joined_s[:, cols]
             else:
                 quantise_wd(0, 0, placed("wd_q00", [2 * P], U32, slot(s - 1)))
                 for k in range(2):
@@ -359,76 +361,83 @@ def tile_list_place_field_atlas_kernel(
             curve = placed("curve%d" % s, [M], F32, curve_at(s))
             nc.scalar.activation(curve[:], squares[:], ACT.Exp, scale=-0.25)
             if s + 2 <= LAST:
-                held = placed("rest%d" % (s + 2), [S - LEAD], F32, slot(s) + ROW)
                 lo = LEAD if s + 2 < LAST else 0
-                copy_h(held, s + 2, lo, lo + S - LEAD)
+                held = placed("rest%d" % (s + 2), [S - lo], F32, slot(s) + ROW)
+                copy_h(held, s + 2, lo, S)
                 rest[s + 2] = held[:]
             if s + 5 <= LAST:
                 project(s + 5)
             if s < PACK:
-                nc.scalar.activation(woven0[:, :, s], curve[:], ACT.Copy, scale=gain_of(s))
+                nc.scalar.activation(joined[:, :BANK, s], curve[:, :BANK], ACT.Copy, scale=gain_of(s))
+                nc.scalar.activation(woven0[:, :, s], curve[:, BANK:], ACT.Copy, scale=gain_of(s))
             else:
                 for k in range(CHUNKS):
                     nc.scalar.activation(woven[k][:, :, s - PACK], curve[:, slice(*spans[k])], ACT.Copy, scale=gain_of(s))
             if s in (0, 2):
                 weave_wd(s // 2, curve_at(s))
-            if s + 2 == LAST:
-                end = placed("end", [LEAD], F32, curve_at(s))
-                copy_h(end, LAST, S - LEAD, S)
 
-        x_chunk = [placed("x_chunk%d" % k, [CHUNK], F32, curve_at(LAST - 1) + 4 * CHUNK * k) for k in range(CHUNKS)]
         unit = 4 * CHUNK
         tail = curve_at(SLICES + 2)
-        starts = (0, unit, 2 * unit, 3 * unit)
-        units = (4, 1, 1, 6)
-        squares = {}
-        curve = kept("curve", [M], F32)
-        for k in range(CHUNKS):
-            nc.vector.tensor_copy(x_chunk[k][:], pages[LAST][:].indirect(entries(idx3, *spans[k])))
+        pieces = {"0a": (0, P), "0b": (P, CHUNK), "1": spans[1], "2": spans[2], "3": spans[3]}
+        x_piece, squares, curves = {}, {}, {}
 
-        def square_chunk(k):
-            squares[k] = placed("square_chunk%d" % k, [units[k] * CHUNK], F32, tail + starts[k])[:, :CHUNK]
-            nc.scalar.activation(squares[k], x_chunk[k][:], ACT.Square, bias=pref_of(LAST), scale=-1.0)
+        def gather_piece(name):
+            lo, hi = pieces[name]
+            x_piece[name] = placed("x_piece" + name, [hi - lo], F32, curve_at(LAST - 1) + 4 * lo)
+            nc.vector.tensor_copy(x_piece[name][:], pages[LAST][:].indirect(entries(idx3, lo, hi)))
 
-        def exp_chunk(k):
-            nc.scalar.activation(curve[:, slice(*spans[k])], squares[k], ACT.Exp, scale=-0.25)
+        def square_piece(name, offset, units):
+            lo, hi = pieces[name]
+            squares[name] = placed("squares_" + name, [units * CHUNK], F32, offset)[:, : hi - lo]
+            nc.scalar.activation(squares[name], x_piece[name][:], ACT.Square, bias=pref_of(LAST), scale=-1.0)
 
-        square_chunk(0)
-        exp_chunk(0)
-        square_chunk(1)
-        square_chunk(2)
-        exp_chunk(1)
-        square_chunk(3)
-        exp_chunk(2)
-        exp_chunk(3)
+        def exp_piece(name):
+            lo, hi = pieces[name]
+            curves[name] = placed("curve_" + name, [CHUNK], F32, curve_at(1) + unit * (lo // P) if lo < CHUNK else curve_at(3) + 4 * lo)[:, : hi - lo]
+            nc.scalar.activation(curves[name], squares[name], ACT.Exp, scale=-0.25)
+
+        def gain_half(name):
+            lo, hi = pieces[name]
+            nc.scalar.activation(woven[0][:, lo:hi, PACK - 1], curves[name], ACT.Copy, scale=gain_of(LAST))
 
         def gain_chunk(k):
-            nc.vector.tensor_scalar(woven[k][:, :, PACK - 1], curve[:, slice(*spans[k])], gain_of(LAST), None, MULT)
+            nc.vector.tensor_scalar(woven[k][:, :, PACK - 1], curves[str(k)], gain_of(LAST), None, MULT)
 
         def late_z0(k, offset):
             z_q[0, k] = placed("z_q0%d" % k, [CHUNK], U32, offset)[:]
             quantise_z0(z_q[0, k], *spans[k])
 
-        def quantise_chunk(k):
-            if k == 2:
-                z_q[1, k] = placed("z_q1%d" % k, [CHUNK], U32, tail + starts[3] + 4 * unit)[:]
-            else:
-                z_q[1, k] = kept("z_q1%d" % k, [CHUNK], U32)[:]
+        def quantise_chunk(k, codes):
+            z_q[1, k] = codes[:]
             nc.vector.quantize_mx(
                 out=z_q[1, k].bitcast(FP8X4), scales=z_s[1][:, slice(*spans[k])], in_=woven[k][:].rearrange("p m t -> p (m t)")
             )
 
-        gain_chunk(0)
+        starts = (0, unit, 2 * unit, 7 * unit)
+        for name in pieces:
+            gather_piece(name)
+        square_piece("0a", slot(LAST - 1), 1)
+        square_piece("0b", tail, 8)
+        exp_piece("0a")
+        exp_piece("0b")
+        gain_half("0a")
+        square_piece("1", tail + starts[1], 1)
+        gain_half("0b")
+        exp_piece("1")
+        square_piece("2", tail + starts[2], 5)
+        square_piece("3", tail + starts[3], 1)
+        exp_piece("2")
+        exp_piece("3")
         quantise_wd(1, 1, placed("wd_q11", [2 * P], U32, tail))
-        quantise_chunk(0)
+        quantise_chunk(0, kept("z_q10", [CHUNK], U32))
         gain_chunk(1)
         late_z0(2, tail + starts[1])
-        quantise_chunk(1)
+        quantise_chunk(1, kept("z_q11", [CHUNK], U32))
         gain_chunk(2)
+        late_z0(3, tail + starts[2] + 4 * unit)
+        quantise_chunk(2, kept("z_q12", [CHUNK], U32))
         gain_chunk(3)
-        quantise_chunk(2)
-        late_z0(3, tail + starts[3] + 5 * unit)
-        quantise_chunk(3)
+        quantise_chunk(3, kept("z_q13", [CHUNK], U32))
         out_v = out.rearrange("(j i p) m -> j p i m", j=2, i=2)
         for k in range(CHUNKS - 1):
             if k >= 2:
@@ -438,7 +447,7 @@ def tile_list_place_field_atlas_kernel(
                 out_pass(k, 2 * j, 1)
                 out_pass(k, 2 * j + 1, 1)
                 if k == 0:
-                    staged = placed("staged0%d" % j, [2, CHUNK], F32, tail + starts[3] + 2 * unit * j)
+                    staged = placed("staged0%d" % j, [2, CHUNK], F32, tail + starts[2] + 2 * unit * j)
                 else:
                     staged = kept("staged%d%d" % (k, j), [2, CHUNK], F32, tag="page%d" % (2 * k + j))
                 if k >= 2 and j == 1:
@@ -447,12 +456,13 @@ def tile_list_place_field_atlas_kernel(
                     nc.scalar.copy(staged[:], res[k, j][:])
                 nc.sync.dma_start(out_v[j][:, :, CHUNK * k : CHUNK * (k + 1)], staged[:])
         k = CHUNKS - 1
-        single = [bank("single", [CHUNK], 4 + nt) for nt in range(4)]
+        single = [bank("single", [CHUNK], (5, 1, 2, 3)[nt]) for nt in range(4)]
+        for nt in range(4):
+            out_pass(k, nt, 0, single[nt][:])
         for j in range(2):
             staged = kept("staged%d%d" % (k, j), [2, CHUNK], F32, tag="page%d" % (2 * k + j))
             for part in range(2):
-                for b in range(PASSES):
-                    out_pass(k, 2 * j + part, b, single[2 * j + part][:])
+                out_pass(k, 2 * j + part, 1, single[2 * j + part][:])
             nc.scalar.copy(staged[:, 0, :], single[2 * j][:])
             nc.vector.tensor_copy(staged[:, 1, :], single[2 * j + 1][:])
             nc.sync.dma_start(out_v[j][:, :, CHUNK * k : CHUNK * (k + 1)], staged[:])

@@ -33,7 +33,8 @@ LEAD = 256
 W4_WORDS = BANK // 2
 SLOT = 2 * ROW
 SLOTS = 3
-FIRST_PIECES = ((0, 256), (256, 384), (384, 512))
+FIRST_PIECES = ((0, 256), (256, 384))
+FIRST = 384
 OVERLAP = 64
 
 
@@ -167,7 +168,8 @@ def tile_list_place_field_atlas_kernel(
         nc.sync.dma_start(idx2[:], offs2)
 
         v_sc = kept("v_sc", [S], U8)
-        nc.vector.tensor_copy(v_sc[:], tab_sc[:].indirect(idx[:]))
+        for lo in (0, BANK):
+            nc.vector.tensor_copy(v_sc[:, lo : lo + BANK], tab_sc[:].indirect(entries(idx, lo, lo + BANK)))
         carry(v_plane[0], v_sc[:, :BANK])
         v_w = [kept("v_w%d" % a, [S], U32) for a in range(PASSES)]
 
@@ -176,8 +178,8 @@ def tile_list_place_field_atlas_kernel(
 
         gather_words(0, 0, S)
         gather_words(1, 0, LEAD)
-        gather_words(1, LEAD, BANK)
-        gather_words(1, BANK, S)
+        gather_words(1, LEAD, FIRST)
+        gather_words(1, FIRST, S)
 
         wd_src = wd.rearrange("(b x t y) n -> b t x y n", b=PASSES, t=PACK, y=RUN)
         wd_raw = [placed("wd_raw0", [PACK, N], F32, slot(1)), kept("wd_raw1", [PACK, N], F32, tag="tab_w1")]
@@ -224,21 +226,20 @@ def tile_list_place_field_atlas_kernel(
 
         def passes(dst, s, lo, hi):
             b, t = divmod(s, PACK)
-            c = lo // BANK
             for a in range(PASSES):
                 nc.tensor.matmul_mx(
                     out=dst,
                     lhsT=w4_w[b][:, a, t, :].bitcast(FP4X4),
                     lhsT_scale=w4_plane[b][:, a, P * t : P * (t + 1)],
                     rhs=v_w[a][:, lo:hi].bitcast(FP8X4),
-                    rhs_scale=v_plane[c][:, a, lo - BANK * c : hi - BANK * c],
+                    rhs_scale=v_plane[lo // BANK][:, a, lo % BANK : (hi - 1) % BANK + 1],
                     start=(a == 0),
                     stop=(a == PASSES - 1),
                 )
 
         def project(s):
             for c in range(s == 0, 2):
-                acc[s, c] = bank("acc", [BANK], 2 * (s % 3) + (1 - c if s == 3 else c))
+                acc[s, c] = bank("acc", [BANK], (s + c) % 6)
                 passes(acc[s, c][:], s, BANK * c, BANK * (c + 1))
 
         def copy_h(dst, s, lo, hi):
@@ -249,15 +250,18 @@ def tile_list_place_field_atlas_kernel(
         def scatter(s, values, lo, hi):
             nc.vector.tensor_tensor(pages[s][:].indirect(entries(idx2, lo, hi)), values, wg[s % PACK][:, lo:hi], MULT)
 
-        h0 = [kept("h0%d" % c, [BANK], F32) for c in range(2)]
-        for number, (lo, hi) in zip((0, 5, 6), FIRST_PIECES):
+        h0 = [kept("h00", [FIRST], F32), kept("h01", [S - FIRST], F32)]
+        for number, (lo, hi) in zip((0, 5), FIRST_PIECES):
             first = bank("first", [hi - lo], number)
             passes(first[:], 0, lo, hi)
             nc.scalar.copy(h0[0][:, lo:hi], first[:])
-        scatter(0, h0[0][:], 0, BANK)
+        scatter(0, h0[0][:], 0, FIRST)
+        first = bank("first", [BANK - FIRST], 6)
+        passes(first[:], 0, FIRST, BANK)
+        nc.scalar.copy(h0[1][:, : BANK - FIRST], first[:])
         project(0)
-        copy_h(h0[1], 0, BANK, S)
-        scatter(0, h0[1][:], BANK, S)
+        copy_h(h0[1][:, BANK - FIRST :], 0, BANK, S)
+        scatter(0, h0[1][:], FIRST, S)
         project(1)
         h1 = kept("h1", [S], F32)
         copy_h(h1, 1, 0, S)
@@ -268,9 +272,9 @@ def tile_list_place_field_atlas_kernel(
         project(4)
         make_consts()
 
-        joined = kept("joined", [M, PACK], BF16)
-        woven0 = kept("woven0", [BANK, PACK], BF16)
-        joined_s = kept("joined_s", [M], U8)
+        joined = kept("joined", [3 * CHUNK, PACK], BF16)
+        woven0 = kept("woven0", [M - CHUNK, PACK], BF16)
+        joined_s = kept("joined_s", [3 * CHUNK], U8)
         woven = [kept("woven1%d" % k, [CHUNK, PACK], BF16) for k in range(CHUNKS)]
         spans = [(CHUNK * k, CHUNK * (k + 1)) for k in range(CHUNKS)]
         wd_woven, wd_q, z_q, res = {}, {}, {}, {}
@@ -287,7 +291,7 @@ def tile_list_place_field_atlas_kernel(
 
         def weave_wd(b, offset):
             wd_woven[b] = placed("wd_woven%d" % b, [2 * P, PACK], BF16, offset)
-            early = joined[:, BANK + 2 * P * b : BANK + 2 * P * (b + 1), :]
+            early = joined[:, CHUNK + 2 * P * b : CHUNK + 2 * P * (b + 1), :]
             if b == 0:
                 halves = wd_raw[b][:].rearrange("p t (j i n) -> p i j n t", i=2, j=2)
                 nc.scalar.copy(wd_woven[b][:].rearrange("p (j n) t -> p j n t", j=2), halves[:, 0])
@@ -303,7 +307,7 @@ def tile_list_place_field_atlas_kernel(
                 out=codes[:].bitcast(FP8X4), scales=wd_s[b, j][:], in_=wd_woven[b][:].rearrange("p n t -> p (n t)")
             )
 
-        def out_pass(k, nt, b, alone=None):
+        def out_pass(k, nt, b, alone=None, lone=False):
             j, part = divmod(nt, 2)
             half, place = (j, part) if b == 1 else (part, j)
             nc.tensor.matmul_mx(
@@ -311,19 +315,19 @@ def tile_list_place_field_atlas_kernel(
                 lhsT=wd_q[b, half][:, P * place : P * (place + 1)].bitcast(FP8X4),
                 lhsT_scale=wd_s[b, half][:, P * place : P * (place + 1)],
                 rhs=z_q[b, k].bitcast(FP8X4),
-                rhs_scale=(joined_s if b == 0 and k < 2 else z_s[b])[:, CHUNK * k : CHUNK * (k + 1)],
+                rhs_scale=(joined_s if b == 0 and k == 0 else z_s[b])[:, CHUNK * k : CHUNK * (k + 1)],
                 start=(b == 0 and (part == 0 or alone is not None)),
-                stop=(b == PASSES - 1 and (part == 1 or alone is not None)),
+                stop=lone or (b == PASSES - 1 and (part == 1 or alone is not None)),
             )
 
         def quantise_z0(codes, lo, hi):
             nc.vector.quantize_mx(
-                out=codes.bitcast(FP8X4), scales=z_s[0][:, lo:hi], in_=woven0[:, lo - BANK : hi - BANK, :].rearrange("p m t -> p (m t)")
+                out=codes.bitcast(FP8X4), scales=z_s[0][:, lo:hi], in_=woven0[:, lo - CHUNK : hi - CHUNK, :].rearrange("p m t -> p (m t)")
             )
 
         def open_sums(j, chunks):
             for k in chunks:
-                res[k, j] = bank("res", [2, CHUNK], 2 * k + j if k < 2 else (4, 0)[j])
+                res[k, j] = bank("res", [2, CHUNK], 2 * k + j)
                 out_pass(k, 2 * j, 0)
                 out_pass(k, 2 * j + 1, 0)
 
@@ -345,19 +349,22 @@ def tile_list_place_field_atlas_kernel(
                 copy_h(lead, s + 2, 0, LEAD)
                 scatter(s + 2, lead[:], 0, LEAD)
             elif s + 2 == LAST:
-                joined_q = placed("joined_q", [M], U32, curve_at(s - 1))
-                nc.vector.quantize_mx(
-                    out=joined_q[:].bitcast(FP8X4), scales=joined_s[:], in_=joined[:].rearrange("p m t -> p (m t)")
-                )
+                joined_q = placed("joined_q", [3 * CHUNK], U32, curve_at(s - 1))
+                for cols in (slice(0, 3 * P), slice(3 * P, 6 * P)):
+                    nc.vector.quantize_mx(
+                        out=joined_q[:, cols].bitcast(FP8X4), scales=joined_s[:, cols], in_=joined[:, cols, :].rearrange("p m t -> p (m t)")
+                    )
+                z_q[0, 0] = joined_q[:, :CHUNK]
                 for k in range(2):
-                    z_q[0, k] = joined_q[:, slice(*spans[k])]
-                    cols = slice(*spans[2 + k])
+                    cols = slice(*spans[1 + k])
                     wd_q[k, 1 - k], wd_s[k, 1 - k] = joined_q[:, cols], joined_s[:, cols]
             else:
                 quantise_wd(0, 0, placed("wd_q00", [2 * P], U32, slot(s - 1)))
-                for k in range(2):
-                    open_sums(0, [k])
-                    open_sums(1, [k])
+                open_sums(0, [0])
+                open_sums(1, [0])
+                unread = bank("unread", [CHUNK], 7)
+                for n in range(4):
+                    out_pass(0, 0, 0, unread[:], lone=True)
             curve = placed("curve%d" % s, [M], F32, curve_at(s))
             nc.scalar.activation(curve[:], squares[:], ACT.Exp, scale=-0.25)
             if s + 2 <= LAST:
@@ -368,8 +375,8 @@ def tile_list_place_field_atlas_kernel(
             if s + 5 <= LAST:
                 project(s + 5)
             if s < PACK:
-                nc.scalar.activation(joined[:, :BANK, s], curve[:, :BANK], ACT.Copy, scale=gain_of(s))
-                nc.scalar.activation(woven0[:, :, s], curve[:, BANK:], ACT.Copy, scale=gain_of(s))
+                nc.scalar.activation(joined[:, :CHUNK, s], curve[:, :CHUNK], ACT.Copy, scale=gain_of(s))
+                nc.scalar.activation(woven0[:, :, s], curve[:, CHUNK:], ACT.Copy, scale=gain_of(s))
             else:
                 for k in range(CHUNKS):
                     nc.scalar.activation(woven[k][:, :, s - PACK], curve[:, slice(*spans[k])], ACT.Copy, scale=gain_of(s))
@@ -431,19 +438,19 @@ def tile_list_place_field_atlas_kernel(
         quantise_wd(1, 1, placed("wd_q11", [2 * P], U32, tail))
         quantise_chunk(0, kept("z_q10", [CHUNK], U32))
         gain_chunk(1)
-        late_z0(2, tail + starts[1])
+        late_z0(1, tail + starts[1])
         quantise_chunk(1, kept("z_q11", [CHUNK], U32))
         gain_chunk(2)
-        late_z0(3, tail + starts[2] + 4 * unit)
+        late_z0(2, tail + starts[2] + 4 * unit)
         quantise_chunk(2, kept("z_q12", [CHUNK], U32))
         gain_chunk(3)
+        late_z0(3, tail + starts[3])
         quantise_chunk(3, kept("z_q13", [CHUNK], U32))
         out_v = out.rearrange("(j i p) m -> j p i m", j=2, i=2)
         for k in range(CHUNKS - 1):
-            if k >= 2:
-                open_sums(0, [k])
-                open_sums(1, [k])
             for j in range(2):
+                if k >= 1:
+                    open_sums(j, [k])
                 out_pass(k, 2 * j, 1)
                 out_pass(k, 2 * j + 1, 1)
                 if k == 0:
@@ -456,13 +463,12 @@ def tile_list_place_field_atlas_kernel(
                     nc.scalar.copy(staged[:], res[k, j][:])
                 nc.sync.dma_start(out_v[j][:, :, CHUNK * k : CHUNK * (k + 1)], staged[:])
         k = CHUNKS - 1
-        single = [bank("single", [CHUNK], (5, 1, 2, 3)[nt]) for nt in range(4)]
-        for nt in range(4):
-            out_pass(k, nt, 0, single[nt][:])
+        single = [bank("single", [CHUNK], (6, 7, 0, 1)[nt]) for nt in range(4)]
         for j in range(2):
             staged = kept("staged%d%d" % (k, j), [2, CHUNK], F32, tag="page%d" % (2 * k + j))
             for part in range(2):
-                out_pass(k, 2 * j + part, 1, single[2 * j + part][:])
+                for b in range(PASSES):
+                    out_pass(k, 2 * j + part, b, single[2 * j + part][:])
             nc.scalar.copy(staged[:, 0, :], single[2 * j][:])
             nc.vector.tensor_copy(staged[:, 1, :], single[2 * j + 1][:])
             nc.sync.dma_start(out_v[j][:, :, CHUNK * k : CHUNK * (k + 1)], staged[:])

@@ -307,29 +307,23 @@ def tile_list_place_field_atlas_kernel(
                 out=codes[:].bitcast(FP8X4), scales=wd_s[b, j][:], in_=wd_woven[b][:].rearrange("p n t -> p (n t)")
             )
 
-        def out_pass(k, nt, b, alone=None, lone=False):
+        def out_pass(k, nt, b, unread=None):
             j, part = divmod(nt, 2)
             half, place = (j, part) if b == 1 else (part, j)
             nc.tensor.matmul_mx(
-                out=res[k, j][:, part, :] if alone is None else alone,
+                out=res[k, nt][:] if unread is None else unread,
                 lhsT=wd_q[b, half][:, P * place : P * (place + 1)].bitcast(FP8X4),
                 lhsT_scale=wd_s[b, half][:, P * place : P * (place + 1)],
                 rhs=z_q[b, k].bitcast(FP8X4),
                 rhs_scale=(joined_s if b == 0 and k == 0 else z_s[b])[:, CHUNK * k : CHUNK * (k + 1)],
-                start=(b == 0 and (part == 0 or alone is not None)),
-                stop=lone or (b == PASSES - 1 and (part == 1 or alone is not None)),
+                start=(b == 0),
+                stop=(b == PASSES - 1 or unread is not None),
             )
 
         def quantise_z0(codes, lo, hi):
             nc.vector.quantize_mx(
                 out=codes.bitcast(FP8X4), scales=z_s[0][:, lo:hi], in_=woven0[:, lo - CHUNK : hi - CHUNK, :].rearrange("p m t -> p (m t)")
             )
-
-        def open_sums(j, chunks):
-            for k in chunks:
-                res[k, j] = bank("res", [2, CHUNK], 2 * k + j)
-                out_pass(k, 2 * j, 0)
-                out_pass(k, 2 * j + 1, 0)
 
         rest = {1: h1[:, LEAD:]}
         for s in range(LAST):
@@ -360,11 +354,16 @@ def tile_list_place_field_atlas_kernel(
                     wd_q[k, 1 - k], wd_s[k, 1 - k] = joined_q[:, cols], joined_s[:, cols]
             else:
                 quantise_wd(0, 0, placed("wd_q00", [2 * P], U32, slot(s - 1)))
-                open_sums(0, [0])
-                open_sums(1, [0])
-                unread = bank("unread", [CHUNK], 7)
-                for n in range(4):
-                    out_pass(0, 0, 0, unread[:], lone=True)
+                for nt in (0, 2):
+                    res[0, nt] = bank("res", [CHUNK], nt)
+                    out_pass(0, nt, 0)
+                for nt in (1, 3):
+                    unread = bank("unread", [CHUNK], nt)
+                    for n in range(2):
+                        out_pass(0, 0, 0, unread[:])
+                for nt in (1, 3):
+                    res[0, nt] = bank("res", [CHUNK], nt)
+                    out_pass(0, nt, 0)
             curve = placed("curve%d" % s, [M], F32, curve_at(s))
             nc.scalar.activation(curve[:], squares[:], ACT.Exp, scale=-0.25)
             if s + 2 <= LAST:
@@ -446,29 +445,20 @@ def tile_list_place_field_atlas_kernel(
         gain_chunk(3)
         late_z0(3, tail + starts[3])
         quantise_chunk(3, kept("z_q13", [CHUNK], U32))
-        out_v = out.rearrange("(j i p) m -> j p i m", j=2, i=2)
-        for k in range(CHUNKS - 1):
-            for j in range(2):
-                if k >= 1:
-                    open_sums(j, [k])
-                out_pass(k, 2 * j, 1)
-                out_pass(k, 2 * j + 1, 1)
+        for k in range(CHUNKS):
+            for nt in range(4):
+                if k > 0:
+                    res[k, nt] = bank("res", [CHUNK], 4 * (k % 2) + nt)
+                    out_pass(k, nt, 0)
+                out_pass(k, nt, 1)
                 if k == 0:
-                    staged = placed("staged0%d" % j, [2, CHUNK], F32, tail + starts[2] + 2 * unit * j)
+                    staged = placed("staged0%d" % nt, [CHUNK], F32, tail + starts[2] + unit * nt)[:]
                 else:
-                    staged = kept("staged%d%d" % (k, j), [2, CHUNK], F32, tag="page%d" % (2 * k + j))
-                if k >= 2 and j == 1:
-                    nc.vector.tensor_copy(staged[:], res[k, j][:])
+                    if nt == 0:
+                        four = kept("staged%d" % k, [4, CHUNK], F32, tag="page%d" % k)
+                    staged = four[:, nt, :]
+                if k >= 2 and nt % 2 == 1:
+                    nc.vector.tensor_copy(staged, res[k, nt][:])
                 else:
-                    nc.scalar.copy(staged[:], res[k, j][:])
-                nc.sync.dma_start(out_v[j][:, :, CHUNK * k : CHUNK * (k + 1)], staged[:])
-        k = CHUNKS - 1
-        single = [bank("single", [CHUNK], (6, 7, 0, 1)[nt]) for nt in range(4)]
-        for j in range(2):
-            staged = kept("staged%d%d" % (k, j), [2, CHUNK], F32, tag="page%d" % (2 * k + j))
-            for part in range(2):
-                for b in range(PASSES):
-                    out_pass(k, 2 * j + part, b, single[2 * j + part][:])
-            nc.scalar.copy(staged[:, 0, :], single[2 * j][:])
-            nc.vector.tensor_copy(staged[:, 1, :], single[2 * j + 1][:])
-            nc.sync.dma_start(out_v[j][:, :, CHUNK * k : CHUNK * (k + 1)], staged[:])
+                    nc.scalar.copy(staged, res[k, nt][:])
+                nc.sync.dma_start(out[P * nt : P * (nt + 1), CHUNK * k : CHUNK * (k + 1)], staged)

@@ -98,7 +98,8 @@ def tile_list_place_field_atlas_kernel(
 
         def load_w4(b):
             w4_raw[b] = kept("w4_raw%d" % b, [PASSES, W4_WORDS], I32)
-            nc.sync.dma_start(w4_raw[b][:], w4_src[:, :, W4_WORDS * b : W4_WORDS * (b + 1)])
+            for a in range(PASSES):
+                nc.sync.dma_start(w4_raw[b][:, a, :], w4_src[:, a, W4_WORDS * b : W4_WORDS * (b + 1)])
 
         w4s_src = w4_scales.rearrange("a q c -> q a c").bitcast(I32)
 
@@ -165,7 +166,6 @@ def tile_list_place_field_atlas_kernel(
         load_table(1)
         load_w4(0)
         order_w4(0)
-        nc.sync.dma_start(idx2[:], offs2)
 
         v_sc = kept("v_sc", [S], U8)
         for lo in (0, BANK):
@@ -190,6 +190,7 @@ def tile_list_place_field_atlas_kernel(
                 nc.sync.dma_start(wd_raw[b][:, t, :], wd_src[b, t])
 
         load_page(0)
+        nc.sync.dma_start(idx2[:], offs2)
         carry(v_plane[1], v_sc[:, BANK:])
         load_page(1)
         load_wgs(1, 0, LEAD)

@@ -274,7 +274,7 @@ def tile_list_place_field_atlas_kernel(
         make_consts()
 
         joined = kept("joined", [3 * CHUNK, PACK], BF16)
-        woven0 = kept("woven0", [M - CHUNK, PACK], BF16)
+        woven0 = kept("woven0", [M, PACK], BF16)
         joined_s = kept("joined_s", [3 * CHUNK], U8)
         woven = [kept("woven1%d" % k, [CHUNK, PACK], BF16) for k in range(CHUNKS)]
         spans = [(CHUNK * k, CHUNK * (k + 1)) for k in range(CHUNKS)]
@@ -291,16 +291,13 @@ def tile_list_place_field_atlas_kernel(
             return consts[:, t, PASSES + b : PASSES + b + 1]
 
         def weave_wd(b, offset):
-            wd_woven[b] = placed("wd_woven%d" % b, [2 * P, PACK], BF16, offset)
-            early = joined[:, CHUNK + 2 * P * b : CHUNK + 2 * P * (b + 1), :]
+            columns = wd_raw[b][:].rearrange("p t n -> p n t")
             if b == 0:
-                halves = wd_raw[b][:].rearrange("p t (j i n) -> p i j n t", i=2, j=2)
-                nc.scalar.copy(wd_woven[b][:].rearrange("p (j n) t -> p j n t", j=2), halves[:, 0])
-                nc.scalar.copy(early.rearrange("p (j n) t -> p j n t", j=2), halves[:, 1])
+                nc.scalar.copy(joined[:, :N, :], columns)
             else:
-                halves = wd_raw[b][:].rearrange("p t (j n) -> p j n t", j=2)
-                nc.scalar.copy(wd_woven[b][:], halves[:, 1])
-                nc.scalar.copy(early, halves[:, 0])
+                wd_woven[b] = placed("wd_woven%d" % b, [2 * P, PACK], BF16, offset)
+                nc.scalar.copy(wd_woven[b][:], columns[:, 2 * P :, :])
+                nc.scalar.copy(joined[:, N:, :], columns[:, : 2 * P, :])
 
         def quantise_wd(b, j, codes):
             wd_q[b, j], wd_s[b, j] = codes, kept("wd_s%d" % b, [2 * P], U8)
@@ -310,20 +307,19 @@ def tile_list_place_field_atlas_kernel(
 
         def out_pass(k, nt, b, unread=None):
             j, part = divmod(nt, 2)
-            half, place = (j, part) if b == 1 else (part, j)
             nc.tensor.matmul_mx(
                 out=res[k, nt][:] if unread is None else unread,
-                lhsT=wd_q[b, half][:, P * place : P * (place + 1)].bitcast(FP8X4),
-                lhsT_scale=wd_s[b, half][:, P * place : P * (place + 1)],
+                lhsT=wd_q[b, j][:, P * part : P * (part + 1)].bitcast(FP8X4),
+                lhsT_scale=wd_s[b, j][:, P * part : P * (part + 1)],
                 rhs=z_q[b, k].bitcast(FP8X4),
-                rhs_scale=(joined_s if b == 0 and k == 0 else z_s[b])[:, CHUNK * k : CHUNK * (k + 1)],
+                rhs_scale=z_s[b][:, CHUNK * k : CHUNK * (k + 1)],
                 start=(b == 0),
                 stop=(b == PASSES - 1 or unread is not None),
             )
 
         def quantise_z0(codes, lo, hi):
             nc.vector.quantize_mx(
-                out=codes.bitcast(FP8X4), scales=z_s[0][:, lo:hi], in_=woven0[:, lo - CHUNK : hi - CHUNK, :].rearrange("p m t -> p (m t)")
+                out=codes.bitcast(FP8X4), scales=z_s[0][:, lo:hi], in_=woven0[:, lo:hi, :].rearrange("p m t -> p (m t)")
             )
 
         rest = {1: h1[:, LEAD:]}
@@ -349,22 +345,17 @@ def tile_list_place_field_atlas_kernel(
                     nc.vector.quantize_mx(
                         out=joined_q[:, cols].bitcast(FP8X4), scales=joined_s[:, cols], in_=joined[:, cols, :].rearrange("p m t -> p (m t)")
                     )
-                z_q[0, 0] = joined_q[:, :CHUNK]
-                for k in range(2):
-                    cols = slice(*spans[1 + k])
-                    wd_q[k, 1 - k], wd_s[k, 1 - k] = joined_q[:, cols], joined_s[:, cols]
+                for n, half in enumerate(((0, 0), (0, 1), (1, 0))):
+                    wd_q[half], wd_s[half] = joined_q[:, slice(*spans[n])], joined_s[:, slice(*spans[n])]
             else:
-                quantise_wd(0, 0, placed("wd_q00", [2 * P], U32, slot(s - 1)))
-                for nt in (0, 2):
+                z_q[0, 0] = placed("z_q00", [CHUNK], U32, slot(s - 1))[:]
+                quantise_z0(z_q[0, 0], 0, CHUNK)
+                for nt in range(4):
                     res[0, nt] = bank("res", [CHUNK], nt)
                     out_pass(0, nt, 0)
-                for nt in (1, 3):
-                    unread = bank("unread", [CHUNK], nt)
-                    for n in range(2):
-                        out_pass(0, 0, 0, unread[:])
-                for nt in (1, 3):
-                    res[0, nt] = bank("res", [CHUNK], nt)
-                    out_pass(0, nt, 0)
+                unread = bank("unread", [CHUNK], 7)
+                for n in range(4):
+                    out_pass(0, 0, 0, unread[:])
             curve = placed("curve%d" % s, [M], F32, curve_at(s))
             nc.scalar.activation(curve[:], squares[:], ACT.Exp, scale=-0.25)
             if s + 2 <= LAST:
@@ -375,8 +366,7 @@ def tile_list_place_field_atlas_kernel(
             if s + 5 <= LAST:
                 project(s + 5)
             if s < PACK:
-                nc.scalar.activation(joined[:, :CHUNK, s], curve[:, :CHUNK], ACT.Copy, scale=gain_of(s))
-                nc.scalar.activation(woven0[:, :, s], curve[:, CHUNK:], ACT.Copy, scale=gain_of(s))
+                nc.scalar.activation(woven0[:, :, s], curve[:], ACT.Copy, scale=gain_of(s))
             else:
                 for k in range(CHUNKS):
                     nc.scalar.activation(woven[k][:, :, s - PACK], curve[:, slice(*spans[k])], ACT.Copy, scale=gain_of(s))

@@ -353,9 +353,6 @@ def tile_list_place_field_atlas_kernel(
                 for nt in range(4):
                     res[0, nt] = bank("res", [CHUNK], nt)
                     out_pass(0, nt, 0)
-                unread = bank("unread", [CHUNK], 7)
-                for n in range(4):
-                    out_pass(0, 0, 0, unread[:])
             curve = placed("curve%d" % s, [M], F32, curve_at(s))
             nc.scalar.activation(curve[:], squares[:], ACT.Exp, scale=-0.25)
             if s + 2 <= LAST:

from contextlib import ExitStack

import concourse.mybir as mybir
from concourse.masks import make_identity

K, T, S, H, T2, M, N = 1024, 2048, 1024, 1024, 2048, 1024, 512
FLOPS = 2 * K * H * S + 2 * H * N * M

F32 = mybir.dt.float32
BF16 = mybir.dt.bfloat16
I32 = mybir.dt.int32
U32 = mybir.dt.uint32
U16 = mybir.dt.uint16
U8 = mybir.dt.uint8
FP8X4 = mybir.dt.float8_e4m3fn_x4
FP4X4 = mybir.dt.float4_e2m1fn_x4
ACT = mybir.ActivationFunctionType
MULT = mybir.AluOpType.mult

P = 128
PACK = 4
PASSES = 2
SLICES = PASSES * PACK
LAST = SLICES - 1
QUADRANTS = 4
RUN = 4
BANK = 512
PER_COLUMN = 16
CHUNK = 256
CHUNKS = M // CHUNK
ROW = 4 * M
LEAD = 256
W4_WORDS = BANK // 2
SLOT = 2 * ROW
SLOTS = 3
FIRST_PIECES = ((0, 256), (256, 384))
FIRST = 384
OVERLAP = 64


def tile_list_place_field_atlas_kernel(
    tc, tab_words, tab_scales, offs, w4_words, w4_scales, wgs, page0, offs2, offs3, pref, gain, wd, out
):
    nc = tc.nc
    with ExitStack() as ctx:
        lists = ctx.enter_context(tc.tile_pool(name="lists", bufs=1))
        keep = ctx.enter_context(tc.tile_pool(name="keep", bufs=1))
        ring = ctx.enter_context(tc.tile_pool(name="ring", bufs=1))
        psum = ctx.enter_context(tc.psum_pool(name="psum", bufs=1))

        idx = lists.tile([P, S // PER_COLUMN], U16, name="idx")
        idx2 = lists.tile([P, S // PER_COLUMN], U16, name="idx2")
        idx3 = lists.tile([P, M // PER_COLUMN], U16, name="idx3")

        def entries(offsets, lo, hi):
            return offsets[:, lo // PER_COLUMN : hi // PER_COLUMN]

        def kept(name, shape, dtype, tag=""):
            return keep.tile([P] + shape, dtype, name=name, tag=tag or name, align_bytes=64)

        def placed(name, shape, dtype, offset):
            return ring.tile([P] + shape, dtype, name=name, offset=offset, align_bytes=64)

        def bank(name, shape, number):
            return psum.tile([P] + shape, F32, name=name, tag="bank%d" % number)

        def slot(s):
            return SLOT * (s % SLOTS)

        def curve_at(s):
            return SLOT * SLOTS + ROW * s

        tab_sc = kept("tab_sc", [T], U8)
        w4s_raw = [kept("w4s_raw%d" % b, [PASSES, BANK], U8) for b in range(PASSES)]
        v_plane = [kept("v_plane%d" % c, [PASSES, BANK], U8) for c in range(2)]
        w4_plane = {}
        nc.vector.memset(w4s_raw[0][:].bitcast(I32), 0)
        nc.vector.memset(tab_sc[32:64, :].bitcast(I32), 0)
        nc.vector.memset(tab_sc[64:128, :].bitcast(I32), 0)
        ident = keep.tile([P, P], F32, name="ident")
        make_identity(nc, ident[:])
        for plane in (v_plane[0], v_plane[1], w4s_raw[1]):
            nc.gpsimd.memset(plane[:].bitcast(I32), 0)
        rows = kept("rows", [PACK, P], F32)
        nc.gpsimd.memset(rows[:], 0.0)

        nc.sync.dma_start(idx[:], offs)
        nc.sync.dma_start(tab_sc[0:32, :].bitcast(I32), tab_scales.rearrange("a q t -> q a t").bitcast(I32))
        wg0_rows = placed("wg0_rows", [S // 4], F32, curve_at(SLICES) + BANK)
        nc.sync.dma_start(wg0_rows[:], wgs.rearrange("(x t y) (c s) -> t (y c) x s", t=PACK, y=RUN, c=4)[0])

        tab_w, w4_raw, w4_w = {}, {}, {}
        w4_src = w4_words.rearrange("a p c -> p a c").bitcast(I32)

        def load_table(a):
            tab_w[a] = kept("tab_w%d" % a, [T], I32)
            nc.sync.dma_start(tab_w[a][:], tab_words[a].rearrange("p t i -> p (t i)").bitcast(I32))

        def load_w4(b):
            w4_raw[b] = kept("w4_raw%d" % b, [PASSES, W4_WORDS], I32)
            for a in range(PASSES):
                nc.sync.dma_start(w4_raw[b][:, a, :], w4_src[:, a, W4_WORDS * b : W4_WORDS * (b + 1)])

        w4s_src = w4_scales.rearrange("a q c -> q a c").bitcast(I32)

        def load_w4_scales(b):
            for q in (0, 2, 1, 3):
                nc.sync.dma_start(
                    w4s_raw[b][32 * q : 32 * q + 4, :, :].bitcast(I32), w4s_src[4 * q : 4 * q + 4, :, P * b : P * (b + 1)]
                )

        def order_w4(b):
            w4_plane[b] = placed("w4_plane%d" % b, [PASSES, BANK], U8, curve_at(SLICES + b))
            nc.scalar.copy(
                w4_plane[b][:].bitcast(U32).rearrange("p a (t x) -> p a t x", t=PACK),
                w4s_raw[b][:].bitcast(U32).rearrange("p a (x t) -> p a t x", t=PACK),
            )
            w4_w[b] = placed("w4_w%d" % b, [PASSES, PACK, 2 * P], U8, curve_at(SLICES + b) + PASSES * BANK)
            for ts in (slice(0, 1), slice(1, PACK)) if b == 0 else (slice(0, PACK),):
                nc.scalar.copy(
                    w4_w[b][:].bitcast(U32).rearrange("p a t (x e) -> p a t x e", e=2)[:, :, ts],
                    w4_raw[b][:].bitcast(U32).rearrange("p a (x t e) -> p a t x e", t=PACK, e=2)[:, :, ts],
                )

        def carry(plane, scale_rows):
            for q in (0, 2, 1, 3):
                nc.sync.dma_start(plane[32 * q : 32 * q + 4, :, :].bitcast(I32), scale_rows[8 * q : 8 * q + 8, :].bitcast(I32))

        page_src = page0.rearrange("(b x t y) c -> b t x y c", b=PASSES, t=PACK, y=RUN)
        pages = [kept("page%d" % s, [T2], F32) for s in range(SLICES)]

        def load_page(s):
            b, t = divmod(s, PACK)
            nc.sync.dma_start(pages[s][:], page_src[b, t])

        wgs_src = wgs.rearrange("(x t y) s -> t x y s", t=PACK, y=RUN)
        wg = [kept("wg%d" % t, [S], F32) for t in range(PACK)]

        def load_wgs(t, lo, hi):
            for q in (0, 2, 1, 3):
                nc.sync.dma_start(wg[t][32 * q : 32 * (q + 1), lo:hi], wgs_src[t][:, :, lo:hi])

        def spread_wg0():
            across = bank("across", [2, P], 6)
            for i in range(2):
                nc.tensor.transpose(across[:, i, :], wg0_rows[:, P * i : P * (i + 1)], ident[:])
            fourfold = kept("fourfold", [4, 2, QUADRANTS, 32], F32)
            for i in range(2):
                nc.scalar.copy(
                    fourfold[:, :, i, :, :].rearrange("p c q (x y) -> p c q x y", y=RUN),
                    across[:, i, :]
                    .rearrange("p (y c x) -> p c x y", y=RUN, c=4)
                    .unsqueeze(2)
                    .to_broadcast([P, 4, QUADRANTS, 8, RUN]),
                )
            for half in range(2):
                back = bank("back", [4, P], (7, 4)[half])
                for n in range(4):
                    c, i = divmod(4 * half + n, 2)
                    nc.tensor.transpose(back[:, n, :], fourfold[:, c, i, :, :].rearrange("p q u -> p (q u)"), ident[:])
                nc.scalar.copy(wg[0][:, BANK * half : BANK * (half + 1)], back[:].rearrange("p n j -> p (n j)"))

        spread_wg0()
        load_table(0)
        load_w4_scales(0)
        load_table(1)
        load_w4(0)
        order_w4(0)

        v_sc = kept("v_sc", [S], U8)
        for lo in (0, BANK):
            nc.vector.tensor_copy(v_sc[:, lo : lo + BANK], tab_sc[:].indirect(entries(idx, lo, lo + BANK)))
        carry(v_plane[0], v_sc[:, :BANK])
        v_w = [kept("v_w%d" % a, [S], U32) for a in range(PASSES)]

        def gather_words(a, lo, hi):
            nc.vector.tensor_copy(v_w[a][:, lo:hi], tab_w[a][:].bitcast(U32).indirect(entries(idx, lo, hi)))

        gather_words(0, 0, S)
        gather_words(1, 0, LEAD)
        gather_words(1, LEAD, FIRST)
        gather_words(1, FIRST, S)

        wd_src = wd.rearrange("(b x t y) n -> b t x y n", b=PASSES, t=PACK, y=RUN)
        wd_raw = [placed("wd_raw0", [PACK, N], F32, slot(1)), kept("wd_raw1", [PACK, N], F32, tag="tab_w1")]
        vecs = keep.tile([2 * PASSES, BANK], F32, name="vecs")

        def load_wd(b):
            for t in range(PACK):
                nc.sync.dma_start(wd_raw[b][:, t, :], wd_src[b, t])

        load_page(0)
        nc.sync.dma_start(idx2[:], offs2)
        carry(v_plane[1], v_sc[:, BANK:])
        load_page(1)
        load_wgs(1, 0, LEAD)
        nc.sync.dma_start(idx3[:], offs3)
        load_wgs(1, LEAD, S)
        load_w4_scales(1)
        load_w4(1)
        load_wgs(2, 0, S)
        for i, vec in enumerate((pref, gain)):
            nc.sync.dma_start(vecs[PASSES * i : PASSES * (i + 1), :], vec.rearrange("(b r) -> b r", b=PASSES))
        load_page(2)
        load_wgs(3, 0, S)
        load_wd(0)
        load_page(3)
        load_page(4)
        load_page(5)
        load_wd(1)
        load_page(6)
        load_page(7)

        consts = keep.tile([P, PACK, 2 * PASSES], F32, name="consts")

        def make_consts():
            nc.scalar.copy(
                rows[0 : 2 * PASSES].rearrange("p t (x y) -> p t x y", y=RUN),
                vecs[:].rearrange("p (x t y) -> p t x y", t=PACK, y=RUN),
            )
            turned = bank("turned", [PACK, P], 6)
            for t in range(PACK):
                nc.tensor.transpose(turned[:, t, :], rows[:, t, :], ident[:])
            nc.scalar.copy(consts[:], turned[:, :, 0 : 2 * PASSES])

        acc = {}

        def passes(dst, s, lo, hi):
            b, t = divmod(s, PACK)
            for a in range(PASSES):
                nc.tensor.matmul_mx(
                    out=dst,
                    lhsT=w4_w[b][:, a, t, :].bitcast(FP4X4),
                    lhsT_scale=w4_plane[b][:, a, P * t : P * (t + 1)],
                    rhs=v_w[a][:, lo:hi].bitcast(FP8X4),
                    rhs_scale=v_plane[lo // BANK][:, a, lo % BANK : (hi - 1) % BANK + 1],
                    start=(a == 0),
                    stop=(a == PASSES - 1),
                )

        def project(s):
            for c in range(s == 0, 2):
                acc[s, c] = bank("acc", [BANK], (s + c) % 6)
                passes(acc[s, c][:], s, BANK * c, BANK * (c + 1))

        def copy_h(dst, s, lo, hi):
            for c in range(lo // BANK, (hi - 1) // BANK + 1):
                first, last = max(lo, BANK * c), min(hi, BANK * (c + 1))
                nc.scalar.copy(dst[:, first - lo : last - lo], acc[s, c][:, first - BANK * c : last - BANK * c])

        def scatter(s, values, lo, hi):
            nc.vector.tensor_tensor(pages[s][:].indirect(entries(idx2, lo, hi)), values, wg[s % PACK][:, lo:hi], MULT)

        h0 = [kept("h00", [FIRST], F32), kept("h01", [S - FIRST], F32)]
        for number, (lo, hi) in zip((0, 5), FIRST_PIECES):
            first = bank("first", [hi - lo], number)
            passes(first[:], 0, lo, hi)
            nc.scalar.copy(h0[0][:, lo:hi], first[:])
        scatter(0, h0[0][:], 0, FIRST)
        first = bank("first", [BANK - FIRST], 6)
        passes(first[:], 0, FIRST, BANK)
        nc.scalar.copy(h0[1][:, : BANK - FIRST], first[:])
        project(0)
        copy_h(h0[1][:, BANK - FIRST :], 0, BANK, S)
        scatter(0, h0[1][:], FIRST, S)
        project(1)
        h1 = kept("h1", [S], F32)
        copy_h(h1, 1, 0, S)
        scatter(1, h1[:, :LEAD], 0, LEAD)
        project(2)
        project(3)
        order_w4(1)
        project(4)
        make_consts()

        joined = kept("joined", [3 * CHUNK, PACK], BF16)
        woven0 = kept("woven0", [M, PACK], BF16)
        joined_s = kept("joined_s", [3 * CHUNK], U8)
        woven = [kept("woven1%d" % k, [CHUNK, PACK], BF16) for k in range(CHUNKS)]
        spans = [(CHUNK * k, CHUNK * (k + 1)) for k in range(CHUNKS)]
        wd_woven, wd_q, z_q, res = {}, {}, {}, {}
        wd_s = {}
        z_s = [kept("z_s%d" % b, [M], U8) for b in range(PASSES)]

        def pref_of(s):
            b, t = divmod(s, PACK)
            return consts[:, t, b : b + 1]

        def gain_of(s):
            b, t = divmod(s, PACK)
            return consts[:, t, PASSES + b : PASSES + b + 1]

        def weave_wd(b, offset):
            columns = wd_raw[b][:].rearrange("p t n -> p n t")
            if b == 0:
                nc.scalar.copy(joined[:, :N, :], columns)
            else:
                wd_woven[b] = placed("wd_woven%d" % b, [2 * P, PACK], BF16, offset)
                nc.scalar.copy(wd_woven[b][:], columns[:, 2 * P :, :])
                nc.scalar.copy(joined[:, N:, :], columns[:, : 2 * P, :])

        def quantise_wd(b, j, codes):
            wd_q[b, j], wd_s[b, j] = codes, kept("wd_s%d" % b, [2 * P], U8)
            nc.vector.quantize_mx(
                out=codes[:].bitcast(FP8X4), scales=wd_s[b, j][:], in_=wd_woven[b][:].rearrange("p n t -> p (n t)")
            )

        def out_pass(k, nt, b, unread=None):
            j, part = divmod(nt, 2)
            nc.tensor.matmul_mx(
                out=res[k, nt][:] if unread is None else unread,
                lhsT=wd_q[b, j][:, P * part : P * (part + 1)].bitcast(FP8X4),
                lhsT_scale=wd_s[b, j][:, P * part : P * (part + 1)],
                rhs=z_q[b, k].bitcast(FP8X4),
                rhs_scale=z_s[b][:, CHUNK * k : CHUNK * (k + 1)],
                start=(b == 0),
                stop=(b == PASSES - 1 or unread is not None),
            )

        def quantise_z0(codes, lo, hi):
            nc.vector.quantize_mx(
                out=codes.bitcast(FP8X4), scales=z_s[0][:, lo:hi], in_=woven0[:, lo:hi, :].rearrange("p m t -> p (m t)")
            )

        rest = {1: h1[:, LEAD:]}
        for s in range(LAST):
            step = M
            x = placed("x%d" % s, [M], F32, slot(s - 1))
            for lo in range(0, M, step):
                nc.vector.tensor_copy(x[:, lo : lo + step], pages[s][:].indirect(entries(idx3, lo, lo + step)))
            if s < LAST - 1:
                scatter(s + 1, rest[s + 1], LEAD, S)
            else:
                scatter(LAST, rest[LAST], 0, S)
            squares = placed("squares%d" % s, [M], F32, slot(s) + OVERLAP)
            for lo in range(0, M, step):
                nc.scalar.activation(squares[:, lo : lo + step], x[:, lo : lo + step], ACT.Square, bias=pref_of(s), scale=-1.0)
            if s + 2 < LAST:
                lead = placed("lead%d" % (s + 2), [LEAD], F32, slot(s - 1))
                copy_h(lead, s + 2, 0, LEAD)
                scatter(s + 2, lead[:], 0, LEAD)
            elif s + 2 == LAST:
                joined_q = placed("joined_q", [3 * CHUNK], U32, curve_at(s - 1))
                for cols in (slice(0, 3 * P), slice(3 * P, 6 * P)):
                    nc.vector.quantize_mx(
                        out=joined_q[:, cols].bitcast(FP8X4), scales=joined_s[:, cols], in_=joined[:, cols, :].rearrange("p m t -> p (m t)")
                    )
                for n, half in enumerate(((0, 0), (0, 1), (1, 0))):
                    wd_q[half], wd_s[half] = joined_q[:, slice(*spans[n])], joined_s[:, slice(*spans[n])]
            else:
                z_q[0, 0] = placed("z_q00", [CHUNK], U32, slot(s - 1))[:]
                quantise_z0(z_q[0, 0], 0, CHUNK)
                for nt in range(4):
                    res[0, nt] = bank("res", [CHUNK], nt)
                    out_pass(0, nt, 0)
            curve = placed("curve%d" % s, [M], F32, curve_at(s))
            nc.scalar.activation(curve[:], squares[:], ACT.Exp, scale=-0.25)
            if s + 2 <= LAST:
                lo = LEAD if s + 2 < LAST else 0
                held = placed("rest%d" % (s + 2), [S - lo], F32, slot(s) + ROW)
                copy_h(held, s + 2, lo, S)
                rest[s + 2] = held[:]
            if s + 5 <= LAST:
                project(s + 5)
            if s < PACK:
                nc.scalar.activation(woven0[:, :, s], curve[:], ACT.Copy, scale=gain_of(s))
            else:
                for k in range(CHUNKS):
                    nc.scalar.activation(woven[k][:, :, s - PACK], curve[:, slice(*spans[k])], ACT.Copy, scale=gain_of(s))
            if s in (0, 2):
                weave_wd(s // 2, curve_at(s))

        unit = 4 * CHUNK
        tail = curve_at(SLICES + 2)
        pieces = {"0a": (0, P), "0b": (P, CHUNK), "1": spans[1], "2": spans[2], "3": spans[3]}
        x_piece, squares, curves = {}, {}, {}

        def gather_piece(name):
            lo, hi = pieces[name]
            x_piece[name] = placed("x_piece" + name, [hi - lo], F32, curve_at(LAST - 1) + 4 * lo)
            nc.vector.tensor_copy(x_piece[name][:], pages[LAST][:].indirect(entries(idx3, lo, hi)))

        def square_piece(name, offset, units):
            lo, hi = pieces[name]
            squares[name] = placed("squares_" + name, [units * CHUNK], F32, offset)[:, : hi - lo]
            nc.scalar.activation(squares[name], x_piece[name][:], ACT.Square, bias=pref_of(LAST), scale=-1.0)

        def exp_piece(name):
            lo, hi = pieces[name]
            curves[name] = placed("curve_" + name, [CHUNK], F32, curve_at(1) + unit * (lo // P) if lo < CHUNK else curve_at(3) + 4 * lo)[:, : hi - lo]
            nc.scalar.activation(curves[name], squares[name], ACT.Exp, scale=-0.25)

        def gain_half(name):
            lo, hi = pieces[name]
            nc.scalar.activation(woven[0][:, lo:hi, PACK - 1], curves[name], ACT.Copy, scale=gain_of(LAST))

        def gain_chunk(k):
            nc.vector.tensor_scalar(woven[k][:, :, PACK - 1], curves[str(k)], gain_of(LAST), None, MULT)

        def late_z0(k, offset):
            z_q[0, k] = placed("z_q0%d" % k, [CHUNK], U32, offset)[:]
            quantise_z0(z_q[0, k], *spans[k])

        def quantise_chunk(k, codes):
            z_q[1, k] = codes[:]
            nc.vector.quantize_mx(
                out=z_q[1, k].bitcast(FP8X4), scales=z_s[1][:, slice(*spans[k])], in_=woven[k][:].rearrange("p m t -> p (m t)")
            )

        starts = (0, unit, 2 * unit, 7 * unit)
        for name in pieces:
            gather_piece(name)
        square_piece("0a", slot(LAST - 1), 1)
        square_piece("0b", tail, 8)
        exp_piece("0a")
        exp_piece("0b")
        gain_half("0a")
        square_piece("1", tail + starts[1], 1)
        gain_half("0b")
        exp_piece("1")
        square_piece("2", tail + starts[2], 5)
        square_piece("3", tail + starts[3], 1)
        exp_piece("2")
        exp_piece("3")
        quantise_wd(1, 1, placed("wd_q11", [2 * P], U32, tail))
        quantise_chunk(0, kept("z_q10", [CHUNK], U32))
        gain_chunk(1)
        late_z0(1, tail + starts[1])
        quantise_chunk(1, kept("z_q11", [CHUNK], U32))
        gain_chunk(2)
        late_z0(2, tail + starts[2] + 4 * unit)
        quantise_chunk(2, kept("z_q12", [CHUNK], U32))
        gain_chunk(3)
        late_z0(3, tail + starts[3])
        quantise_chunk(3, kept("z_q13", [CHUNK], U32))
        for k in range(CHUNKS):
            for nt in range(4):
                if k > 0:
                    res[k, nt] = bank("res", [CHUNK], 4 * (k % 2) + nt)
                    out_pass(k, nt, 0)
                out_pass(k, nt, 1)
                if k == 0:
                    staged = placed("staged0%d" % nt, [CHUNK], F32, tail + starts[2] + unit * nt)[:]
                else:
                    if nt == 0:
                        four = kept("staged%d" % k, [4, CHUNK], F32, tag="page%d" % k)
                    staged = four[:, nt, :]
                if k >= 2 and nt % 2 == 1:
                    nc.vector.tensor_copy(staged, res[k, nt][:])
                else:
                    nc.scalar.copy(staged, res[k, nt][:])
                nc.sync.dma_start(out[P * nt : P * (nt + 1), CHUNK * k : CHUNK * (k + 1)], staged)
